import numpy as np, ml_dtypes
CORES = [6,15,38,47]
N = 4
BF = ml_dtypes.bfloat16
def gentries(a):
    return np.ascontiguousarray(a.reshape(8, 16, -1).transpose(0, 2, 1)).reshape(8, -1)
def gtable(e):
    e = np.asarray(e); return np.ascontiguousarray(e.reshape(8, -1, 16).transpose(0, 2, 1)).reshape(128, -1).astype(np.int32)
L, T, K, R = 256, 16, 16, 4
W = L * T
def mix(rng, a):
    return np.take_along_axis(a, np.argsort(rng.random(a.shape), axis=2), 2)
def spots(rng, q, m, n):
    a = np.add.accumulate(rng.integers(1, n // m + 1, (q, 8, m, L)), axis=2)
    return mix(rng, (a + rng.integers(0, n, (q, 8, 1, L))) % n)
def reals(rng, n):
    v = 2 * rng.random((N, 8, 16, n)) - 1
    return np.where(v < 0, -1.0, 1.0) * (0.25 + 0.75 * np.abs(v)) * rng.choice(np.array([0.5, 0.75, 1.0]), (N, 8, 1, n))
def parts(rng):
    pa = rng.integers(-128, 128, (N, 8, 16, W)); fc = rng.integers(-128, 128, (N, 8, 16, R * L))
    return pa, reals(rng, W), spots(rng, N, K, W), fc, reals(rng, R * L), np.exp2(-5 + 3 * rng.random((N, 8, 16, 1)))
def flat(a):
    return np.asarray(a, np.float32).reshape(N, 128, -1).astype(BF)
def pack(pa, ea, nd, fc, er, dl):
    return {"pa": flat(pa), "ea": flat(ea), "nd": np.stack([gtable(a.reshape(8, K * L)) for a in nd]), "fc": flat(fc), "er": flat(er),
            "dl": np.clip(np.asarray(dl, np.float32), np.float32(0.03125), np.float32(0.25)).reshape(N, 128, 1)}
def setup_inputs(rng):
    return pack(*parts(rng))
def setup_inputs_spread(rng):
    pa, ea, nd, fc, er, dl = parts(rng)
    pa = np.floor((2 * rng.random(pa.shape) - 1) * np.exp2(rng.integers(3, 8, (N, 8, 1, W))))
    fc = np.floor((2 * rng.random(fc.shape) - 1) * np.exp2(rng.integers(3, 8, (N, 8, 1, R * L))))
    ea = ea * np.exp2(-rng.integers(0, 2, (N, 8, 1, W)))
    er = er * np.exp2(-rng.integers(0, 2, (N, 8, 1, R * L)))
    return pack(pa, ea, nd, fc, er, dl)
def setup_inputs_ends(rng):
    pa, ea, nd, fc, er, dl = parts(rng)
    def ends(n):
        whole = rng.random((N, 8, 1, n)) < 0.5
        return np.where(whole, rng.random((N, 8, 1, n)) < 0.5, rng.random((N, 8, 16, n)) < 0.5)
    pa = np.where(ends(W), 127, -128); fc = np.where(ends(R * L), 127, -128)
    pa[..., [1, W - 2, W - 1]] = 127; pa[..., [2, W - 3]] = -128
    for t in range(R): fc[..., t * L + L - 1] = 127 if t % 2 else -128
    ea = np.where(ends(W), 1.0, -1.0); er = np.where(ends(R * L), 1.0, -1.0); dl = np.where(rng.random(dl.shape) < 0.5, 0.25, 0.03125)
    ea[:, :, 0] = 1.0; er[:, :, 0] = -1.0; ea[:, :, 15] = -1.0; er[:, :, 15] = 1.0
    dl[:, :, 0] = 0.25; dl[:, :, 15] = 0.25; dl[:, :, 1] = 0.03125
    a = rng.integers(1, K, (N, 8, 1, L)); a[N - 1, :, 0, L - 1] = K // 2; j = np.arange(K)[:, None]
    far = np.where(j < a, j, W - K + j)
    near = T * (1 + spots(rng, N, K, L - 2)) + rng.choice(np.array([0, T - 2, T - 1]), (N, 8, K, L)); near[:, :, 0] = 0; near[:, :, 1] = W - 1
    nd = np.where((np.arange(8) % 2 == 1)[None, :, None, None], far, near)
    return pack(pa, ea, mix(rng, nd), fc, er, dl)
def setup_inputs_corners(rng):
    pa, ea, nd, fc, er, dl = parts(rng); one = spots(rng, 1, N * K, W)[0]; s = spots(rng, N, K, L); j = np.arange(K)[:, None]; i = np.arange(L)
    for q in range(N):
        nd[q, 0] = one[0, :K]
        nd[q, 1] = np.concatenate([one[1, :K - 1], one[1, K - 1 + q:K + q]])
        nd[q, 2] = one[2, q * K:(q + 1) * K]
        nd[q, 6] = np.where(j < (i % (K + 1))[None, :], one[6, :K], one[6, q * K:(q + 1) * K])
    nd[:, 3] = s[:, 3] * T + T - 1
    nd[:, 4] = (T * rng.integers(0, L, (N, 1, L)) + j) % W
    nd[:, 5] = ((s[:, 5] - s[:, 5, :1] + i) % L) * T + rng.choice(np.array([0, T - 2, T - 1]), (N, K, L))
    pa[::2, 7] = -128; pa[1::2, 7] = np.where(rng.random((N // 2, 1, W)) < 0.5, 127, -128)
    dl[:, ::2, ::2] = 0.03125; dl[:, 1::2, ::4] = 0.25
    return pack(pa, ea, mix(rng, nd), fc, er, dl)
def setup_inputs_crowd(rng):
    pa, ea, nd, fc, er, dl = parts(rng)
    pa[:, ::2] = rng.integers(-1, 2, (N, 4, 1, W)); fc[:, ::2] = rng.integers(-1, 2, (N, 4, 1, R * L))
    s = spots(rng, N, K, L)[..., :1]; day = np.where(np.arange(K)[:, None] % 2 == 0, T - 2, rng.integers(0, T, (N, 8, K, 1)))
    c = s * T + day; c[:, 0] = c[:1, 0]
    same = np.zeros((N, 8, K, L), np.int64) + c
    same[:, 4:, :, L - 1] = nd[:, 4:, :, L - 1]
    nd = mix(rng, same); nd[:, 1] = same[:, 1]
    return pack(pa, ea, nd, fc, er, dl)
def setup_inputs_late(rng):
    pa, ea, nd, fc, er, dl = parts(rng); c = spots(rng, N, K, L); i = np.arange(L)
    def off(n, few):
        if few: return (np.arange(16)[:, None] == rng.integers(0, 32, (N, 1, n))).astype(np.int64)
        return rng.integers(0, 8, (N, 16, n))
    for g, few in ((1, False), (3, True), (4, False), (7, True)):
        a = off(W, few); w = off(R * L, few); low = (np.arange(R * L) // L + g) % 2 == 1
        pa[:, g] = 127 - a if g % 2 else a - 128
        fc[:, g] = np.where(low, w - 128, 127 - w)
    s = spots(rng, N, K, L // 2)[:, 6]
    c[:, 6] = 2 * s + (i + (np.arange(K)[:, None] == K - 1)) % 2
    x = rng.choice(np.array([-1.0, 1.0]), (N, 16, 1)) * np.where((np.arange(R)[:, None] + i) % 2 == 0, 1.0, -1.0).reshape(-1)
    er[:, 6] = x; ea[:, 6, :, T - 1::T] = -x[:, :, :L]; dl[:, 6] = 0.25
    return pack(pa, ea, mix(rng, c * T + T - 2), fc, er, dl)
def check_ranges(d):
    bad = []
    for k, lo, hi in (("pa", -128, 127), ("fc", -128, 127), ("ea", -1, 1), ("er", -1, 1), ("dl", 0.03125, 0.25), ("nd", 0, W - 1)):
        v = np.asarray(d[k]).astype(np.float64)
        if not (np.min(v) >= lo and np.max(v) <= hi): bad.append("range of " + k)
        elif k in ("pa", "fc") and np.any(v != np.floor(v)): bad.append(k + " holds a number that isn't whole")
        elif k in ("ea", "er") and np.any(np.abs(v) < 0.0625): bad.append("sizes of " + k)
    s = np.sort(np.stack([gentries(a) for a in d["nd"]]).reshape(N, 8, K, L), axis=2)
    if np.any(s[:, :, 1:] == s[:, :, :-1]): bad.append("nd names a place twice in one lane")
    return bad
def reference(pa, ea, nd, fc, er, dl):
    P = pa.astype(np.int32).reshape(N, 8, 16, W); E = ea.astype(np.float64).reshape(N, 8, 16, W)
    f = fc.astype(np.int32).reshape(N, 8, 16, R, L); z = er.astype(np.float64).reshape(N, 8, 16, R, L); lim = dl.astype(np.float64).reshape(N, 8, 16, 1)
    A = np.stack([gentries(a) for a in nd]).astype(np.int64).reshape(N, 8, K, L)
    yb, ys = [], []
    for t in range(R):
        own = A - A % T + (A + 1) % T
        come = np.roll(own, 1, axis=0)
        void = np.any(come[:, :, :, None, :] == own[:, :, None, :, :], axis=3)
        c = np.concatenate([own, come], axis=2)
        g = np.take_along_axis(P, c.reshape(N, 8, 1, 2 * K * L), 3).reshape(N, 8, 16, 2 * K, L)
        d = np.add.reduce(np.abs(g - f[:, :, :, t][:, :, :, None, :]), axis=2)
        d[:, :, K:] = np.where(void, 2 ** 20, d[:, :, K:])
        o = np.argsort(d, axis=2, kind="stable")[:, :, :K][:, :, ::-1]
        A = np.take_along_axis(c, o, 2)
        e = np.take_along_axis(E, A.reshape(N, 8, 1, K * L), 3).reshape(N, 8, 16, K, L)
        b = np.zeros((N, 8, 16, L))
        for k in range(K): b = b + np.minimum(np.maximum(0.5 * (e[:, :, :, k] - b), -lim), lim)
        yb.append(b); ys.append(np.add.reduce(np.exp(-np.abs(e - b[:, :, :, None, :])), axis=3))
        if t < R - 1:
            P[..., t::T] = f[:, :, :, t]; E[..., t::T] = z[:, :, :, t] - b
    return {"yb": np.concatenate(yb, axis=3).reshape(N, 128, R * L).astype(np.float32), "ys": np.concatenate(ys, axis=3).reshape(N, 128, R * L).astype(np.float32)}

def check_inputs(d):
    bad = list(check_ranges(d))
    if not bad:
        for name, y in reference(**d).items():
            for q in range(N):
                v = np.abs(np.asarray(y[q], np.float64)); s = np.sqrt(np.mean(v * v))
                if v.max() > 9 * s or s < 2.0 ** -4: bad.append('%s of rank %d is uneven or too small' % (name, q))
    return bad

@@ -1,0 +1,544 @@
+from concourse.mybir import AluOpType as ALU, ActivationFunctionType as ACT
+
+CFG = {
+    "np": 2,
+    "path": [["SVSV", "SVSV"], ["SSSS", "SSSS"], ["SSSS", "SSSS"], ["SSSS", "SSSS"]],
+    "sub": ["D", "D", "D", "V"],
+    "sum": ["D", "D", "D", "P"],
+    "halves": [[1, 1], [1, 1], [1, 1], [1, 2]],
+    "chain": ["SS", "SS", "SS", "SS"],
+    "void": ["VV", "VV", "VV", "VV"],
+    "egat": [["SS", "SS"], ["SS", "SS"], ["SS", "SS"], ["SS", "SS"]],
+    "bonus": {}, "ptv": 10, "slack": 100.0, "off": 20000.0,
+}
+COST = {"cy": 0.83 * 1.25, "G": 1.56, "fix": 25.0, "pe": 0.52, "pefix": 5.0, "same": 100.0, "cross": 150.0,
+        "dma": 2000.0, "bw": 500.0, "gi": 1000.0, "yi": 100.0, "rem": 3500.0}
+
+F32, BF, I32, U16 = "float32", "bfloat16", "int32", "uint16"
+
+
+def scratch(NP):
+    LW, IW = 256 // NP, 16 // NP
+    return {
+        "nds": ("sbuf", [128, 16, 16], I32), "ia": ("sbuf", [128, 3, 16, 16], I32),
+        "eas": ("sbuf", [128, 4096], BF), "ers": ("sbuf", [128, 1024], BF),
+        "dls": ("sbuf", [128, 4], F32), "mm": ("sbuf", [128, 4], F32), "mb": ("sbuf", [128, 36], F32),
+        "fr": ("sbuf", [128, 4 * NP, 1024], BF), "cs": ("sbuf", [128, 256], F32),
+        "pt0": ("sbuf", [128, 5120], BF), "pt1": ("sbuf", [128, 5120], BF), "nt": ("sbuf", [128, 5120], F32),
+        "jx": ("sbuf", [128, 144], F32), "pi": ("sbuf", [128, 8], I32), "pf": ("sbuf", [128, 8], F32),
+        "zz": ("sbuf", [128, 6, 144], BF), "idb": ("sbuf", [128, 5, 128], BF), "h2": ("sbuf", [128, NP, 2, 2 * LW], BF), "idf": ("sbuf", [128, 128], F32),
+        "sf": ("sbuf", [128, 2, 4 * NP, 64], BF), "sc": ("sbuf", [128, 32 * IW], BF),
+        "hl": ("sbuf", [128, 5 * NP, 2, 2, LW], BF), "ul": ("sbuf", [128, 2560], U16), "o2": ("sbuf", [128, NP, 2 * LW], F32),
+        "eq": ("sbuf", [128, NP, 16, LW], BF),
+        "dd": ("sbuf", [128, 8192], BF), "md": ("sbuf", [128, 8192], BF),
+        "sv": ("sbuf", [128, 2 * NP, 120, 2 * IW], F32),
+        "kk": ("sbuf", [128, NP, 16, 2 * IW], F32),
+        "ne0": ("sbuf", [128, NP, 16 * LW], F32), "ne1": ("sbuf", [128, NP, 16 * LW], F32), "ne2": ("sbuf", [128, NP, 16 * LW], F32),
+        "tt": ("sbuf", [128, 2, 256], F32), "cc": ("sbuf", [128, 2, 256], F32), "aa": ("sbuf", [128, 2, 256], F32),
+        "bs": ("sbuf", [128, 2 * NP, 4 * LW], F32), "so": ("sbuf", [128, 256], F32),
+        "key": ("psum", [128, 2 * NP, 2, 8 * IW], F32), "up": ("psum", [128, 512], F32),
+        "fp0": ("psum", [128, 512], F32), "fp1": ("psum", [128, 512], F32), "bb": ("psum", [128, 512], F32),
+        "sp0": ("psum", [128, 2 * NP, 8, 2 * IW], F32), "sp1": ("psum", [128, 2 * NP, 8, 2 * IW], F32), "sp2": ("psum", [128, 2 * NP, 8, 2 * IW], F32),
+    }
+
+
+NET = [(0,0,0,0,0,1,8,2,4),(0,0,1,1,4,1,0,2,4),(0,1,0,0,0,1,9,2,4),(0,1,1,1,4,1,1,2,4),
+       (1,0,0,0,0,1,16,2,4),(1,0,1,2,4,1,0,2,4),(1,1,0,0,0,1,17,2,4),(1,1,1,2,4,1,1,2,4),
+       (2,0,0,0,0,1,24,2,4),(2,0,1,0,4,1,0,2,4),(2,1,0,0,0,1,25,2,4),(2,1,1,0,4,1,1,2,4),
+       (3,0,0,0,0,1,80,1,1),(3,0,0,0,4,3,33,5,2),(3,0,1,1,1,2,2,3,2),(3,0,1,1,2,3,1,2,2),(3,0,1,1,6,1,7,1,1),
+       (3,1,0,0,0,1,34,5,2),(3,1,0,0,2,1,35,1,3),(3,1,1,1,5,1,4,2,2),(3,1,1,1,7,1,0,1,1),
+       (4,0,0,0,1,4,44,1,2),(4,0,0,0,6,1,46,2,2),(4,0,1,2,2,1,4,1,3),(4,1,0,0,2,1,42,5,2),(4,1,0,0,4,3,43,12,2),
+       (4,1,1,2,1,4,2,5,2),(4,1,1,2,6,1,3,1,1),
+       (5,0,0,0,2,2,52,29,2),(5,0,0,0,5,2,60,2,2),(5,0,1,0,3,3,2,5,2),(5,1,0,0,6,1,50,13,2),(5,1,1,0,2,2,0,4,2),(5,1,1,1,3,2,1,4,2),
+       (6,0,0,0,2,2,70,12,2),(6,0,1,1,0,7,4,2,2),(6,1,0,0,0,4,61,4,2),(6,1,1,1,2,5,2,5,2),
+       (7,0,1,2,4,1,1,2,4),(7,1,0,0,4,1,67,2,3),(7,1,1,2,7,1,6,1,1),
+       (8,0,0,0,1,2,83,2,2),(8,0,1,0,5,2,0,1,2),(8,0,1,1,6,1,4,1,1),(8,1,0,0,1,1,84,1,1),(8,1,0,0,3,2,72,1,2),(8,1,1,1,6,1,3,2,2),
+       (9,0,0,0,0,1,86,1,1),(9,0,1,1,1,1,7,1,1),(9,1,0,0,0,1,87,1,1),(9,1,1,1,1,1,6,1,1)]
+MAGIC = 1.5 * 2.0 ** 30
+EVEN = 1.5 * 2.0 ** 24
+BIG = 2.0 ** 24
+SP = ["sp0", "sp1", "sp2"]
+
+
+def build(cfg):
+    NP = cfg["np"]; LW, IW = 256 // NP, 16 // NP; VB = 2 * IW; NC = 8 // NP; SW = 8 * IW; FW = 4 * LW
+    ops = []
+    tag = ["init", 0]
+
+    def add(q, kind, n, fn, r=(), w=(), banks=(), gat=False):
+        ops.append({"q": q, "kind": kind, "n": n, "fn": fn, "r": list(r), "w": list(w), "banks": list(banks), "gat": gat,
+                    "bonus": cfg["bonus"].get(tag[0], 0.0) - cfg["off"] * tag[1]})
+
+    def V(n, fn, r, w, banks=(), gat=False): add("V", "c", n, lambda g, T: [fn(g.vector, T)], r, w, banks, gat)
+    def S(n, fn, r, w, banks=(), gat=False): add("S", "c", n, lambda g, T: [fn(g.scalar, T)], r, w, banks, gat)
+    def GC(n, fn, r, w): add("G", "c", n, lambda g, T: [fn(g, T)], r, w)
+    def Y(nb, fn, r, w): add("Y", "d", nb, lambda g, T: [fn(g.sync, T)], r, w)
+    def SD(nb, fn, r, w): add("S", "d", nb, lambda g, T: [fn(g.scalar, T)], r, w)
+    def GD(nb, fn, r, w): add("G", "d", nb, lambda g, T: [fn(g, T)], r, w)
+
+    def PE(mms, r, w, banks, start=True, stop=True):
+        def fn(g, T):
+            out = []
+            for i, m in enumerate(mms):
+                o, a, b = m[1](T)
+                out.append(g.tensor.matmul(o, a, b, start and i == 0, stop and i == len(mms) - 1))
+            return out
+        add("P", "c", [m[0] for m in mms], fn, r, w, banks)
+
+    def sl(a, s, n): return slice(a, a + s * (n - 1) + 1, s)
+
+    Y(1 << 17, lambda e, T: e.dma_start(T.nds[:], T.nd[:]), [], ["nds"])
+    PAS = [("md", c // NC, c % NC, j) for c in range(4) for j in range(2)]
+    SD(1 << 20, lambda e, T: e.dma_start(T.md[:, 0:4096], T.pa[:]), [], PAS)
+    for j in range(4):
+        Y(1 << 18, lambda e, T, j=j: e.dma_start(T.fr[:, :, j * LW:(j + 1) * LW], T.fc[:]), [], [("fr", j)])
+    FR = [("fr", j) for j in range(4)]
+    if NP == 2:
+        Y(1 << 20, lambda e, T: e.dma_start(T.fr[:, :, 512:1024], T.fr[:, :, 0:512]), FR, ["fr2"])
+    Y(1 << 20, lambda e, T: e.dma_start(T.eas[:], T.ea[:]), FR, ["eas"])
+    Y(1 << 18, lambda e, T: e.dma_start(T.ers[:], T.er[:]), FR, ["ers"])
+    Y(1 << 10, lambda e, T: e.dma_start(T.dls[:, 0:1], T.dl[:]), FR, ["dls"])
+    GC(450, lambda g, T: g.iota(T.jx[:], [[1, 144]], 0, 0, allow_small_or_imprecise_dtypes=True), [], ["jx"])
+    GC(160, lambda g, T: g.iota(T.pi[:, 0:1], [[0, 1]], 0, 1), [], ["pi0"])
+    GC(160, lambda g, T: g.iota(T.pf[:, 0:1], [[0, 1]], 0, 1, allow_small_or_imprecise_dtypes=True), [], ["pf0"])
+    GC(160 + 64 * IW, lambda g, T: g.iota(T.sc[:], [[128, 32], [0, IW]], 0, 0, allow_small_or_imprecise_dtypes=True), [], ["sc"])
+    V(1, lambda v, T: v.tensor_scalar(T.pi[:, 4:5], T.pi[:, 0:1], 112, None, ALU.bitwise_and), ["pi0"], ["pi4"])
+    for i in range(2):
+        V(1, lambda v, T, i=i: v.tensor_scalar(T.pf[:, 4 + i:5 + i], T.pi[:, 4:5], float(14 + i), None, ALU.add), ["pi4"], [("pf", i)])
+    for s, val in enumerate((4096.0, 8192.0, -4096.0)):
+        for i in range(2):
+            V(144, lambda v, T, s=s, i=i, val=val: v.tensor_scalar(T.zz[:, 2 * s + i, :], T.jx[:], T.pf[:, 4 + i:5 + i], val, ALU.is_equal, ALU.mult),
+              ["jx", ("pf", i)], [("zz", s, i)])
+    for s, val in enumerate((1.0, 64.0, BIG, -1.0, -64.0)):
+        V(128, lambda v, T, s=s, val=val: v.tensor_scalar(T.idb[:, s, :], T.jx[:, 0:128], T.pf[:, 0:1], val, ALU.is_equal, ALU.mult), ["jx", "pf0"], [("idb", s)])
+    V(128, lambda v, T: v.tensor_scalar(T.idf[:], T.jx[:, 0:128], T.pf[:, 0:1], None, ALU.is_equal), ["jx", "pf0"], ["idf"])
+    V(1, lambda v, T: v.tensor_scalar(T.mm[:, 0:1], T.dls[:, 0:1], 2.0, None, ALU.mult), ["dls"], ["mm"])
+    V(16, lambda v, T: v.tensor_scalar(T.mb[:, 20:36], T.jx[:, 0:16], -0.5, 9.0, ALU.mult, ALU.add), ["jx"], ["mb0"])
+    V(16, lambda v, T: v.tensor_scalar(T.mb[:, 0:16], T.mb[:, 20:36], T.dls[:, 0:1], None, ALU.mult), ["mb0", "dls"], ["mb1"])
+    V(1, lambda v, T: v.tensor_copy(T.mb[:, 0:1], T.dls[:, 0:1]), ["mb1", "dls"], ["mb2"])
+    V(1, lambda v, T: v.tensor_scalar(T.mb[:, 16:17], T.dls[:, 0:1], 16.0, None, ALU.mult), ["mb2", "dls"], ["mb"])
+
+    def zw(T, s, r):
+        i = r & 1
+        return T.zz[:, 2 * s + i, 14 + i - r:142 + i - r]
+    def ZT(s): return [("zz", s, 0), ("zz", s, 1)]
+    BB = [("b", d, i) for d in range(2) for i in range(4)]
+
+    PE([(256, lambda T, r=r: (T.bb[:, 0:256], zw(T, 2, r), T.fr[:, :, r:FW:16])) for r in range(16)], ZT(2) + FR, BB, ["bb"])
+    for j in range(NP):
+        w_ = 64 // NP
+        V(256, lambda v, T, j=j, w_=w_: v.tensor_copy(T.sf[:, 0, :, j * w_:(j + 1) * w_], T.bb[:, 0:256]), BB, [("sf0", j)], ["bb"])
+        V(256, lambda v, T, j=j, w_=w_: v.tensor_tensor(T.sf[:, 1, :, j * w_:(j + 1) * w_], T.bb[:, 0:256], T.sf[:, 0, :, j * w_:(j + 1) * w_], ALU.subtract),
+          BB + [("sf0", j)], [("sf1", j)], ["bb"])
+    SF = [(a, j) for a in ("sf0", "sf1") for j in range(NP)]
+
+    V(256, lambda v, T: v.tensor_scalar(T.ia[:, 0], T.nds[:], 15, None, ALU.bitwise_and), ["nds"], ["ia0"])
+    V(256, lambda v, T: v.tensor_scalar(T.ia[:, 1], T.nds[:], 10, None, ALU.logical_shift_right), ["nds"], ["ia1"])
+    V(256, lambda v, T: v.tensor_scalar(T.ia[:, 2], T.nds[:], 4, 63, ALU.logical_shift_right, ALU.bitwise_and), ["nds"], ["ia2"])
+    for p in range(NP):
+        c = slice(p * IW, (p + 1) * IW); u0 = 2 * LW * p
+        V(LW, lambda v, T, c=c, u0=u0: v.tensor_scalar(T.up[:, u0:u0 + LW], T.ia[:, 0, :, c], 4.0, -32.0, ALU.mult, ALU.add), ["ia0"], [("up", p, 0)], ["up"])
+        V(LW, lambda v, T, c=c, u0=u0, p=p: v.tensor_tensor(T.hl[:, p, 0, 0, :], T.ia[:, 1, :, c], T.up[:, u0:u0 + LW], ALU.add), ["ia1", ("up", p, 0)], [("hl", 0, p, 0, 0)], ["up"])
+        V(LW, lambda v, T, c=c, p=p: v.tensor_scalar(T.hl[:, p, 0, 1, :], T.ia[:, 2, :, c], -32.0, None, ALU.add), ["ia2"], [("hl", 0, p, 0, 1)])
+
+    def blk(q): return slice(q * 256, (q + 1) * 256)
+    for q in range(1, 17):
+        if q <= cfg["ptv"]:
+            V(128, lambda v, T, q=q: v.tensor_copy(T.pt0[:, blk(q)], T.md[:, q % 16:4096:16]), PAS, [("pt0", q)])
+        else:
+            S(256, lambda a, T, q=q: a.activation(T.pt0[:, blk(q)], T.md[:, q % 16:4096:16], ACT.Copy), PAS, [("pt0", q)])
+    def pcopy(dst, q, src, qs, n):
+        Y(n << 16, lambda e, T: e.dma_start(T[dst][:, q * 256:(q + n) * 256], T[src][:, qs * 256:(qs + n) * 256]),
+          [(src, qs + i) for i in range(n)], [(dst, q + i) for i in range(n)])
+    def pnew(dst, d):
+        Y(1 << 16, lambda e, T: e.dma_start(T[dst][:, blk(16 + d)], T.fc[:, blk(d)]), [], [(dst, 16 + d)])
+    tag[0] = "late"
+    pcopy("pt1", 2, "pt0", 2, 14); pcopy("pt1", 17, "pt0", 1, 1); pcopy("pt1", 19, "pt0", 3, 1); pcopy("pt0", 18, "pt0", 2, 1)
+    pnew("pt1", 0); pnew("pt1", 2); pnew("pt0", 1)
+    for q in range(1, 20):
+        S(256, lambda a, T, q=q: a.activation(T.nt[:, blk(q)], T.eas[:, q % 16::16], ACT.Identity, scale=-1.0), ["eas"], [("nt", q, p) for p in range(NP)])
+
+    def umm(t, p, h, half):
+        c0 = (2 * p + half) * LW
+        PE([(LW, lambda T: (T.up[:, c0:c0 + LW], T.idb[:, 1, :], T.hl[:, t * NP + p, h, 0, :])),
+            (LW, lambda T: (T.up[:, c0:c0 + LW], T.idb[:, 0, :], T.hl[:, t * NP + p, h, 1, :]))],
+           [("hl", t, p, h, 0), ("hl", t, p, h, 1), ("idb", 0), ("idb", 1)], [("up", p, half)], ["up"])
+
+    def ucol(t, p, h): return ((t * NP + p) * 2 + h) * LW
+
+    def u16(t, p, h):
+        c = ucol(t, p, h)
+        V(LW, lambda v, T: v.tensor_scalar(T.ul[:, c:c + LW], T.up[:, 2 * p * LW:(2 * p + 1) * LW], 2080.0, None, ALU.add), [("up", p, 0)], [("ul", t, p, h)], ["up"])
+
+    def own_lists(t, p):
+        if t < 4:
+            add("G", "r", t * NP + p, None, [("hl", t, p, 0, 0), ("hl", t, p, 0, 1)], [("hl", t, p, 1, 0), ("hl", t, p, 1, 1)])
+        umm(t, p, 0, 0)
+        u16(t, p, 0)
+        if t < 4 and cfg["void"][t][p] == "S":
+            for j in range(2):
+                Y(1 << 16, lambda e, T, j=j: e.dma_start(T.h2[:, p, :, j * LW:(j + 1) * LW], T.hl[:, t * NP + p, 0]),
+                  [("hl", t, p, 0, 0), ("hl", t, p, 0, 1)], [("h2", p, j)])
+        elif t < 4:
+            umm(t, p, 0, 1)
+            S(2 * LW, lambda a, T: a.activation(T.o2[:, p, :], T.up[:, 2 * p * LW:(2 * p + 2) * LW], ACT.Copy), [("up", p, 0), ("up", p, 1)], [("o2", p)], ["up"])
+
+    def select(t, p):
+        w0 = (t + 1) * 256; tp_ = t * NP + p
+        pt = "pt%d" % (t % 2); fp = "fp%d" % p
+        PW = [(pt, q) for q in range(t + 1, t + 17)]
+        path = cfg["path"][t][p]
+        assert not ("S" in path and cfg["void"][t][p] == "S")
+        if "S" in path:
+            PE([(512, lambda T: (T[fp][:], T.idb[:, 0, :], T.fr[:, tp_, 0:512]))], FR + [("idb", 0)], [fp], [fp])
+        umm(t, p, 1, 0)
+        u16(t, p, 1)
+        sign = cfg["void"][t][p] == "S"
+        if sign:
+            nr = 512 // LW; u1 = (2 * p + 1) * LW
+            for r0 in range(0, 16, nr):
+                for r in range(r0, r0 + nr):
+                    def out(T, r=r, r0=r0): return T[fp][:, (r - r0) * LW:(r - r0 + 1) * LW]
+                    PE([(LW, lambda T, out=out, du=du: (out(T), T.idb[:, 1 - du, :], T.hl[:, tp_, 1, du, :])) for du in range(2)] +
+                       [(LW, lambda T, out=out, du=du, r=r: (out(T), T.idb[:, 4 - du, :], T.h2[:, p, du, IW * r:IW * r + LW])) for du in range(2)],
+                       [("hl", t, p, 1, 0), ("hl", t, p, 1, 1), ("h2", p, 0), ("h2", p, 1)] + [("idb", i) for i in (0, 1, 3, 4)], [(fp, r - r0)] + ([fp] if r0 == 0 else []), [fp])
+                S(512, lambda a, T, r0=r0: a.activation(T.eq[:, p, r0:r0 + nr, :], T[fp][:], ACT.Sign), [(fp, i) for i in range(nr)],
+                  [("eq", p, r) for r in range(r0, r0 + nr)] + ([fp] if r0 + nr == 16 else []), [fp])
+            PE([(LW, lambda T, r=r: (T.up[:, u1:u1 + LW], T.idb[:, 0, :], T.eq[:, p, r, :])) for r in range(16)],
+               [("eq", p, r) for r in range(16)] + [("idb", 0)], [("up", p, 1)], ["up"])
+            V(LW, lambda v, T: v.tensor_scalar(T.o2[:, p, 0:LW], T.up[:, u1:u1 + LW], EVEN, -EVEN, ALU.add, ALU.add), [("up", p, 1)], [("o2", p)], ["up"])
+            V(LW, lambda v, T: v.tensor_tensor(T.eq[:, p, 0, :], T.o2[:, p, 0:LW], T.up[:, u1:u1 + LW], ALU.not_equal), [("up", p, 1), ("o2", p)], [("eq", p, 0)], ["up"])
+        else:
+            for r in range(16):
+                V(LW, lambda v, T, r=r: v.tensor_tensor(T.eq[:, p, r, :], T.o2[:, p, IW * r:IW * r + LW], T.up[:, 2 * p * LW:(2 * p + 1) * LW], ALU.is_equal),
+                  [("o2", p), ("up", p, 0)], [("eq", p, r)], ["up"])
+        for c in range(NC):
+            h, kc = c // (NC // 2), (c % (NC // 2)) * 64
+            o0 = ucol(t, p, h) + kc
+            d0 = (p * NC + c) * 1024
+            def win(T, a=0, n=64, o0=o0): return T[pt][:, w0:w0 + 4096].indirect(T.ul[:, o0 + a:o0 + a + n])
+            def ko(T, h=h, kc=kc): return T.key[:, 2 * p + h, kc // SW, kc % SW:kc % SW + 64]
+            rd = PW + [("ul", t, p, h)]
+            dt_ = [("dd", p, c, 0), ("dd", p, c, 1)]; mt = [("md", p, c, 0), ("md", p, c, 1)]
+            def relu(d0=d0, dt_=dt_, mt=mt):
+                V(512, lambda v, T: v.tensor_scalar(T.md[:, d0:d0 + 1024], T.dd[:, d0:d0 + 1024], 0.0, None, ALU.max), dt_, mt)
+            parts = [(2, "dd"), (1, "md")]
+            if path[c] == "S":
+                S(1024, lambda a, T, win=win, d0=d0: a.activation(T.dd[:, d0:d0 + 1024], win(T), ACT.Copy), rd, dt_, gat=True)
+                for j in range(2):
+                    e0 = d0 + 512 * j
+                    V(512, lambda v, T, e0=e0: v.tensor_tensor(T.md[:, e0:e0 + 512], T.dd[:, e0:e0 + 512], T[fp][:], ALU.max), dt_ + [fp], [mt[j]], [fp])
+            elif path[c] == "D":
+                S(1024, lambda a, T, win=win, d0=d0: a.activation(T.dd[:, d0:d0 + 1024], win(T), ACT.Identity, scale=-1.0), rd, dt_, gat=True)
+                GD(1 << 19, lambda g, T, d0=d0: g.dma_start(T.dd[:, d0:d0 + 1024], T.fr[:, tp_, :], accum_op=ALU.add), FR + ["fr2"] + dt_, dt_)
+                relu()
+            else:
+                for j in range(NP):
+                    V(FW, lambda v, T, win=win, j=j, e0=d0 + j * FW: v.tensor_tensor(T.dd[:, e0:e0 + FW], win(T, j * FW // 16, FW // 16), T.fr[:, tp_, 0:FW], ALU.subtract),
+                      rd + FR, dt_[j:j + 3 - NP], gat=True)
+                if path[c] == "V":
+                    S(1024, lambda a, T, d0=d0: a.activation(T.md[:, d0:d0 + 1024], T.dd[:, d0:d0 + 1024], ACT.Abs), dt_, mt)
+                    parts = [(0, "md")]
+                else:
+                    relu()
+            mms = [(64, lambda T, ko=ko, c=c: (ko(T), T.idb[:, 0, :], T.sc[:, c * 64:c * 64 + 64]))]
+            rr = ["sc", ("idb", 0), parts[0][1] == "dd" and dt_[0] or mt[0]]
+            if path[c] == "S":
+                rr += SF
+                for i in range(2):
+                    mms.append((64, lambda T, ko=ko, i=i: (ko(T), T.idb[:, 0, :], T.sf[:, i, tp_, :])))
+            if h == 1:
+                rr += [("eq", p, r) for r in range(1 if sign else 16)] + [("idb", 2)]
+                for r in range(1 if sign else 16):
+                    mms.append((64, lambda T, ko=ko, r=r, kc=kc: (ko(T), T.idb[:, 2, :], T.eq[:, p, r, kc:kc + 64])))
+            PE(mms, rr, [("key", p, c), "turn"], ["key"], True, False)
+            for s, name in parts:
+                mms = [(64, lambda T, ko=ko, s=s, r=r, name=name, d0=d0: (ko(T), zw(T, s, r), T[name][:, d0 + r:d0 + 1024:16])) for r in range(16)]
+                PE(mms, ZT(s) + (mt if name == "md" else dt_), [("key", p, c), "turn"], ["key"], False, name == "md")
+        if t < 2 and p == NP - 1:
+            pnew(pt, t)
+        H = slice(2 * p, 2 * p + 2); h0, h1 = 2 * p, 2 * p + 1
+        def ts(h, x): return ("sv", p, h, x)
+        def tp(b, h, x): return ("sp", p, b, h, x)
+        for side in range(2):
+            for du in range(2):
+                kr = [("key", p, c) for c in range(NC) if ((c % (NC // 2)) * 64) // SW == side] + [("hl", t, p, h, du) for h in range(2)]
+                dst = (lambda T, du=du: T.sv[:, H, 0:8, du * IW:(du + 1) * IW]) if side == 0 else (lambda T, du=du: T.sp0[:, H, :, du * IW:(du + 1) * IW])
+                wt = [(ts(h, x) if side == 0 else tp(0, h, x)) + (du,) for h in range(2) for x in range(8)]
+                V(LW, lambda v, T, dst=dst, side=side, du=du: v.tensor_tensor(dst(T), T.hl[:, tp_, :, du, side * SW:(side + 1) * SW], T.key[:, H, side, :], ALU.add),
+                  kr, wt, ["key"] + (["sp0"] if side else []))
+        def both(xs): return [x + (du,) for x in xs for du in range(2)]
+        for (l, op, side, bank, i0, si, p0, so, n) in NET:
+            ins = [i0 + si * j for j in range(n)]; outs = [p0 + so * j for j in range(n)]
+            rt = both([ts(h, 8 * l + i) for h in range(2) for i in ins] + [tp(l % 3, h, i) for h in range(2) for i in ins])
+            wt = both([(tp(bank, h, x) if side else ts(h, x)) for h in range(2) for x in outs])
+            V(2 * VB * n, lambda v, T, l=l, op=op, side=side, bank=bank, i0=i0, si=si, p0=p0, so=so, n=n: v.tensor_tensor(
+                (T[SP[bank]] if side else T.sv)[:, H, sl(p0, so, n), :], T.sv[:, H, sl(8 * l + i0, si, n), :], T[SP[l % 3]][:, H, sl(i0, si, n), :],
+                ALU.max if op else ALU.min), rt, wt)
+        V(LW, lambda v, T: v.tensor_tensor(T.sv[:, h0, 88:96, :], T.sv[:, h0, 80:88, :], T.sp1[:, h1, :, :], ALU.min),
+          both([ts(0, 80 + i) for i in range(8)] + [tp(1, 1, i) for i in range(8)]), both([ts(0, 88 + i) for i in range(8)]))
+        V(LW, lambda v, T: v.tensor_tensor(T.sp2[:, h0, ::-1, :], T.sv[:, h1, 80:88, :], T.sp1[:, h0, :, :], ALU.min),
+          both([ts(1, 80 + i) for i in range(8)] + [tp(1, 0, i) for i in range(8)]), both([tp(2, 0, i) for i in range(8)]))
+        for m in range(3):
+            sb, pb, nb = 88 + 8 * m, (2 + m) % 3, m % 3
+            for side in range(2):
+                for op in range(2):
+                    rt = both([ts(0, sb + 4 * side + j) for j in range(4)] + [tp(pb, 0, 4 * side + j) for j in range(4)])
+                    wt = both([(tp(nb, 0, op + 2 * j) if side else ts(0, sb + 8 + op + 2 * j)) for j in range(4)])
+                    V(4 * VB, lambda v, T, sb=sb, pb=pb, nb=nb, side=side, op=op: v.tensor_tensor(
+                        T[SP[nb]][:, h0, op:8:2, :] if side else T.sv[:, h0, sb + 8 + op:sb + 16:2, :],
+                        T.sv[:, h0, sb + 4 * side:sb + 4 * side + 4, :], T[SP[pb]][:, h0, 4 * side:4 * side + 4, :],
+                        ALU.min if op else ALU.max), rt, wt)
+        for op in range(2):
+            V(LW, lambda v, T, op=op: v.tensor_tensor(T.kk[:, p, op:16:2, :], T.sv[:, h0, 112:120, :], T.sp2[:, h0, :, :], ALU.min if op else ALU.max),
+              both([ts(0, 112 + j) for j in range(8)] + [tp(2, 0, j) for j in range(8)]), [("kk", p, op)])
+        rw = both([tp(0, 1, j) for j in range(8)]); kt = [("kk", p, 0), ("kk", p, 1)]
+        V(LW, lambda v, T: v.tensor_scalar(T.sp0[:, h1, :, :], T.kk[:, p, :, 0:IW], MAGIC, -MAGIC, ALU.add, ALU.add), kt, rw)
+        for du in range(2):
+            V(LW, lambda v, T, du=du: v.tensor_tensor(T.hl[:, tp_ + NP, 0, du, :], T.kk[:, p, :, du * IW:(du + 1) * IW], T.sp0[:, h1, :, :], ALU.subtract),
+              kt + rw, [("hl", t + 1, p, 0, du)])
+
+    def nk(t, p, k): return [("ne", t % 3, p, k, j) for j in range(4 // NP)]
+    def bq(t, p): return [("b", t % 2, i) for i in range(p * 4 // NP, (p + 1) * 4 // NP)]
+
+    def bias(t, p):
+        w0 = (t + 1) * 256
+        ne = "ne%d" % (t % 3)
+        NW = [("nt", q, i) for q in range(t + 1, t + 17) for i in range(NP)] + [("ul", t + 1, p, 0)]
+        nh = cfg["halves"][t][p]; wd = LW // nh; per = 4 // NP // nh
+        eg = cfg["egat"][t][p]; ng = len(eg); ck_ = 16 // ng; en = ck_ * LW
+        for c in range(ng):
+            o0 = ucol(t + 1, p, 0) + c * en // 16
+            wt = [x for k in range(ck_ * c, ck_ * (c + 1)) for x in nk(t, p, k)]
+            def win(T, o0=o0): return T.nt[:, w0:w0 + 4096].indirect(T.ul[:, o0:o0 + en // 16])
+            if eg[c] == "S":
+                S(en, lambda a, T, c=c, win=win: a.activation(T[ne][:, p, c * en:(c + 1) * en], win(T), ACT.Copy), NW, wt, gat=True)
+            else:
+                V(en, lambda v, T, c=c, win=win: v.tensor_copy(T[ne][:, p, c * en:(c + 1) * en], win(T)), NW, wt, gat=True)
+        yield
+        b0 = (t % 2) * 256 + p * LW
+        if cfg["chain"][t][p] == "Q":
+            fp = "fp%d" % p; a = p * LW; at = [("aa", 0, x[2]) for x in bq(t, p)]; bo = ("bs", t % 2, p, 0)
+            for k in range(16):
+                src = (lambda T: T[fp][:, 0:LW]) if k else (lambda T: T[ne][:, p, 0:LW])
+                if k:
+                    PE([(4 * LW, lambda T, k=k: (T[fp][:, 0:LW], T.idf[:], T[ne][:, p, k * LW:(k + 1) * LW]))], nk(t, p, k) + ["idf"], [fp], [fp], True, False)
+                    PE([(4 * LW, lambda T: (T[fp][:, 0:LW], T.idf[:], T.cs[:, a:a + LW]))], [("cs", p), "idf"], [fp], [fp], False, True)
+                S(LW, lambda s, T, src=src, k=k: s.activation(T.aa[:, 0, a:a + LW], src(T), ACT.Relu, bias=T.mb[:, k:k + 1], scale=-0.5),
+                  ([fp] if k else nk(t, p, 0)) + ["mb"], at, [fp] if k else [])
+                S(LW, lambda s, T: s.activation(T[fp][:, LW:2 * LW], T.aa[:, 0, a:a + LW], ACT.Relu, bias=T.mm[:, 0:1], scale=-1.0), at + ["mm"], [(fp, 1)] + ([] if k else [fp]), [fp])
+                if k:
+                    V(LW, lambda v, T, k=k: v.tensor_tensor(T.cs[:, a:a + LW] if k < 15 else T.bs[:, (t % 2) * NP + p, 0:LW], T.cs[:, a:a + LW], T[fp][:, LW:2 * LW], ALU.subtract),
+                      [(fp, 1), ("cs", p)], [("cs", p)] if k < 15 else [bo, fp], [fp])
+                else:
+                    V(LW, lambda v, T: v.tensor_scalar(T.cs[:, a:a + LW], T[fp][:, LW:2 * LW], -1.0, T.mb[:, 16:17], ALU.mult, ALU.add), [(fp, 1), "mb"], [("cs", p)], [fp])
+            e0 = (16 + t) * 256 + p * LW; r0 = t * 256 + p * LW
+            V(2 * LW, lambda v, T: v.tensor_tensor(T.nt[:, e0:e0 + LW], T.bs[:, (t % 2) * NP + p, 0:LW], T.ers[:, r0:r0 + LW], ALU.subtract), [bo, "ers"], [("nt", 16 + t, p)])
+            return
+        for k in range(16):
+            for j in range(nh):
+                a = p * LW + j * wd; x0 = k * LW + j * wd; bc = b0 + j * wd
+                et = nk(t, p, k)[j * per:(j + 1) * per]; bt = bq(t, p)[j * per:(j + 1) * per]
+                tt_, ct, at = [[(nm, k % 2, x[2]) for x in bt] for nm in ("tt", "cc", "aa")]
+                src = (lambda T, k=k, a=a: T.tt[:, k % 2, a:a + wd]) if k else (lambda T, x0=x0: T[ne][:, p, x0:x0 + wd])
+                if k:
+                    V(wd, lambda v, T, src=src, x0=x0, bc=bc: v.tensor_tensor(src(T), T[ne][:, p, x0:x0 + wd], T.bb[:, bc:bc + wd], ALU.add), et + bt, tt_, ["bb"])
+                S(wd, lambda s, T, src=src, k=k, a=a: s.activation(T.aa[:, k % 2, a:a + wd], src(T), ACT.Relu, bias=T.mb[:, k:k + 1], scale=-0.5),
+                  (tt_ if k else et) + ["mb"], at)
+                S(wd, lambda s, T, k=k, a=a: s.activation(T.cc[:, k % 2, a:a + wd], T.aa[:, k % 2, a:a + wd], ACT.Relu, bias=T.mm[:, 0:1], scale=-1.0),
+                  at + ["mm"], ct)
+                if k:
+                    V(wd, lambda v, T, k=k, a=a, bc=bc: v.tensor_tensor(T.bb[:, bc:bc + wd], T.bb[:, bc:bc + wd], T.cc[:, k % 2, a:a + wd], ALU.subtract), ct + bt, bt, ["bb"])
+                else:
+                    V(wd, lambda v, T, a=a, bc=bc: v.tensor_scalar(T.bb[:, bc:bc + wd], T.cc[:, 0, a:a + wd], -1.0, T.mb[:, 16:17], ALU.mult, ALU.add),
+                      ct + ["mb"], bt, ["bb"])
+        if t < 3:
+            e0 = (16 + t) * 256 + p * LW; r0 = t * 256 + p * LW
+            V(LW, lambda v, T: v.tensor_tensor(T.nt[:, e0:e0 + LW], T.bb[:, b0:b0 + LW], T.ers[:, r0:r0 + LW], ALU.subtract),
+              bq(t, p) + ["ers"], [("nt", 16 + t, p)], ["bb"])
+        S(LW, lambda s, T: s.activation(T.bs[:, (t % 2) * NP + p, 0:LW], T.bb[:, b0:b0 + LW], ACT.Copy), bq(t, p), [("bs", t % 2, p, 0)], ["bb"])
+
+    def spread(t):
+        ne = "ne%d" % (t % 3); D = slice((t % 2) * NP, (t % 2 + 1) * NP)
+        BS = [("bs", t % 2, p, 0) for p in range(NP)]
+        tag[1] = NP - 1
+        Y(1 << 17, lambda e, T: e.dma_start(T.yb[:, blk(t)], T.bs[:, D, 0:LW]), BS, [("yb", t)])
+        def ck(p, k0, k1): return [x for k in range(k0, k1) for x in nk(t, p, k)]
+        def allp(k0, k1): return [x for p in range(NP) for x in ck(p, k0, k1)]
+        if cfg["sub"][t] == "D":
+            for i in range(1, 4):
+                Y(1 << 17, lambda e, T, i=i: e.dma_start(T.bs[:, D, i * LW:(i + 1) * LW], T.bs[:, D, 0:LW]), BS, [("bs", t % 2, "r", i)])
+            for c in range(4):
+                GD(1 << 20, lambda g, T, c=c: g.dma_start(T[ne][:, :, c * FW:(c + 1) * FW], T.bs[:, D, :], accum_op=ALU.add),
+                   BS + [("bs", t % 2, "r", i) for i in range(1, 4)] + allp(4 * c, 4 * c + 4), allp(4 * c, 4 * c + 4))
+        for p in range(NP):
+            tag[1] = p
+            b0 = (t % 2) * 256 + p * LW; fp = "fp%d" % p
+            nc = 4 if cfg["sub"][t] == "V" else 4 // NP
+            kc = 16 // nc; n = kc * LW
+            for c in range(nc):
+                if cfg["sub"][t] == "V":
+                    for k in range(kc * c, kc * (c + 1)):
+                        V(LW, lambda v, T, p=p, k=k, b0=b0: v.tensor_tensor(T[ne][:, p, k * LW:(k + 1) * LW], T[ne][:, p, k * LW:(k + 1) * LW], T.bb[:, b0:b0 + LW], ALU.add),
+                          nk(t, p, k) + bq(t, p), nk(t, p, k), ["bb"])
+                def xs(T, p=p, c=c, n=n): return T[ne][:, p, c * n:(c + 1) * n]
+                x = ck(p, kc * c, kc * (c + 1))
+                S(n, lambda s, T, xs=xs: s.activation(xs(T), xs(T), ACT.Abs), x, x)
+                S(n + (1600 if t + p + c == 0 else 0), lambda s, T, xs=xs: s.activation(xs(T), xs(T), ACT.Exp, scale=-1.0), x, x)
+                if cfg["sum"][t] == "P":
+                    PE([(4 * LW, lambda T, k=k, p=p, fp=fp: (T[fp][:, 0:LW], T.idf[:], T[ne][:, p, k * LW:(k + 1) * LW])) for k in range(kc * c, kc * (c + 1))],
+                       x + ["idf", fp], [fp], [fp], c == 0, c == nc - 1)
+            if cfg["sum"][t] == "P":
+                V(LW, lambda v, T, p=p, fp=fp: v.tensor_copy(T.so[:, p * LW:(p + 1) * LW], T[fp][:, 0:LW]), [fp], [("so", p)], [fp])
+                Y(1 << 16, lambda e, T, p=p: e.dma_start(T.ys[:, t * 256 + p * LW:t * 256 + (p + 1) * LW], T.so[:, p * LW:(p + 1) * LW]), [("so", p)], [("ys", t, p)])
+        if cfg["sum"][t] == "D":
+            for m in (8, 4, 2, 1):
+                GD(m << 18, lambda g, T, n=m * LW: g.dma_start(T[ne][:, :, 0:n], T[ne][:, :, n:2 * n], accum_op=ALU.add), allp(0, 2 * m), allp(0, m))
+            Y(1 << 17, lambda e, T: e.dma_start(T.ys[:, blk(t)], T[ne][:, :, 0:LW]), allp(0, 1), [("ys", t)])
+
+    tag[0] = "init"
+    for p in range(NP):
+        tag[1] = p
+        own_lists(0, p)
+    for t in range(4):
+        for p in range(NP):
+            tag[0], tag[1] = "s%d" % t, p
+            select(t, p)
+            own_lists(t + 1, p)
+        steps = [bias(t, p) for p in range(NP)]
+        for _ in range(2):
+            for p in range(NP):
+                tag[0], tag[1] = "b%d" % t, p
+                next(steps[p], None)
+        tag[0] = "e%d" % t
+        spread(t)
+    return ops
+
+
+def link(ops):
+    lastw, readers = {}, {}
+    for i, o in enumerate(ops):
+        d = set()
+        for x in o["r"]:
+            if x in lastw: d.add(lastw[x])
+        for x in o["w"]:
+            if x in lastw: d.add(lastw[x])
+            d.update(readers.get(x, ()))
+        d.discard(i)
+        for x in o["r"]: readers.setdefault(x, []).append(i)
+        for x in o["w"]:
+            lastw[x] = i; readers[x] = []
+        o["dep"] = d
+
+
+def times(o, C):
+    k, q, n = o["kind"], o["q"], o["n"]
+    if k == "r": return C["gi"], C["rem"]
+    if k == "d":
+        h = C["gi"] if q == "G" else C["yi"]
+        return h, h + C["dma"] + n / C["bw"]
+    if q == "P":
+        t = sum(max(64, x) * C["pe"] + C["pefix"] for x in n)
+    elif q == "G":
+        t = n * C["cy"]
+    else:
+        t = (n * C["G"] + 40 if o["gat"] else max(n, 64)) * C["cy"] + C["fix"]
+    return t, t
+
+
+def lat(a, b, C):
+    return C["same"] if (a["q"] == b["q"] and a["kind"] == "c") else C["cross"]
+
+
+def plan(ops, C, slack, rounds=0):
+    n = len(ops); succ = [[] for _ in ops]
+    for i, o in enumerate(ops):
+        for d in o["dep"]: succ[d].append(i)
+    tm = [times(o, C) for o in ops]
+    pr = [0.0] * n
+    for i in range(n - 1, -1, -1):
+        pr[i] = tm[i][1] + max([pr[j] + lat(ops[i], ops[j], C) for j in succ[i]], default=0.0)
+    pred = [list(o["dep"]) for o in ops]
+
+    def sweep(pr, back):
+        a, z = (succ, pred) if back else (pred, succ)
+        left = [len(x) for x in a]; ready = [i for i in range(n) if not left[i]]
+        free = {q: 0.0 for q in "VSPGY"}; fin = [0.0] * n; st = [0.0] * n; bank = {}; order = []; extra = {}
+        rt = [tm[i][1] - tm[i][0] if back else 0.0 for i in range(n)]
+        while ready:
+            best = []
+            for i in ready:
+                o = ops[i]; s = max(rt[i], free[o["q"]])
+                for b in o["banks"]:
+                    for q, j in bank.get(b, {}).items():
+                        if q != o["q"]: s = max(s, fin[j] + C["cross"])
+                best.append((s, i))
+            m = min(best)
+            q0 = ops[m[1]]["q"]
+            s, i = max((x for x in best if ops[x[1]]["q"] == q0 and x[0] <= m[0] + slack), key=lambda x: pr[x[1]])
+            o = ops[i]
+            for b in o["banks"]:
+                extra.setdefault(i, set()).update(j for q, j in bank.get(b, {}).items() if q != o["q"])
+                bank.setdefault(b, {})[o["q"]] = i
+            free[o["q"]] = s + tm[i][0]; fin[i] = s + tm[i][0 if back else 1]; st[i] = s
+            order.append(i); ready.remove(i)
+            for j in z[i]:
+                rt[j] = max(rt[j], fin[i] + lat(o, ops[j], C) + (tm[j][1] - tm[j][0] if back else 0.0)); left[j] -= 1
+                if not left[j]: ready.append(j)
+        assert len(order) == n
+        return max(fin), order, st, fin, extra
+
+    best = cur = sweep([pr[i] + ops[i]["bonus"] for i in range(n)], False)
+    for _ in range(rounds):
+        cur = sweep(sweep(cur[3], True)[3], False)
+        if cur[0] < best[0]: best = cur
+    for i, o in enumerate(ops):
+        o["start"] = best[2][i]; o["dep"] = o["dep"] | best[4].get(i, set())
+    return best[1], best[0]
+
+
+CFG.update({'path': [['VDVS', 'VDDD'], ['DDDR', 'DDDD'], ['DVDD', 'DDDD'], ['SSDD', 'DDDD']], 'sub': ['D', 'D', 'V', 'V'], 'sum': ['D', 'D', 'D', 'P'], 'halves': [[1, 1], [1, 1], [1, 1], [2, 2]], 'chain': ['SS', 'SS', 'SS', 'SS'], 'egat': [['SSSS', 'SS'], ['SS', 'SSVV'], ['VS', 'SSSS'], ['SVSS', 'VS']], 'bonus': {'late': -39000, 'b1': 4000, 'e0': -5000, 'b3': 17000, 's0': 59000, 's3': -10000, 's2': 0, 'b2': 10000, 'e3': -67000, 'b0': 20000, 'e1': -8000, 's1': 7000, 'e2': -2000}, 'ptv': 6, 'slack': 0, 'off': 2000})
+SCRATCH = scratch(CFG["np"])
+OPS = build(CFG)
+link(OPS)
+ORDER, SPAN = plan(OPS, COST, CFG["slack"])
+SEMAPHORES = ["cV", "cS", "cP", "cG", "snt"] + ["arr%d" % t for t in range(4 * CFG["np"])] + ["d%d" % i for i, o in enumerate(OPS) if o["kind"] == "d"]
+
+
+def rank_program(g, core, T, topo):
+    rank = T.rank_of(core)
+    if rank is None:
+        return
+    nxt = T.cores[(rank + 1) % len(T.cores)]
+    prv = T.cores[(rank - 1) % len(T.cores)]
+    rid, pid, _ = topo.addr(nxt)
+    mask = topo.mask(core, nxt)
+    n_out = len(topo.engines(core, nxt)); n_in = len(topo.engines(prv, core))
+    Q = {"V": g.vector, "S": g.scalar, "P": g.tensor, "G": g, "Y": g.sync}
+    count = {q: 0 for q in Q}; know = {q: {} for q in Q}; mark = {}; clock = {}; total = {}
+    for i in ORDER:
+        o = OPS[i]; q = o["q"]; kn = know[q]
+        for d in sorted(o["dep"], key=lambda d: -OPS[d]["start"]):
+            s, v = mark[d]
+            if kn.get(s, 0) < v:
+                Q[q].wait_ge(T.sem[s], v)
+                kn[s] = v
+                for a, b in clock[d].items():
+                    if kn.get(a, 0) < b: kn[a] = b
+        clock[i] = dict(kn)
+        if o["kind"] == "r":
+            t = o["n"]
+            g.remote_dma(T.hl[:, t, 1], T.hl[:, t, 0], T.sem["arr%d" % t], T.sem.snt, pid, rid, mask)
+            mark[i] = ("arr%d" % t, n_in); total["snt"] = total.get("snt", 0) + n_out
+            clock[i] = {}
+        elif o["kind"] == "d":
+            o["fn"](g, T)[0].then_inc(T.sem["d%d" % i], 16)
+            mark[i] = ("d%d" % i, 16)
+        else:
+            for ins in o["fn"](g, T):
+                ins.then_inc(T.sem["c" + q], 1); count[q] += 1
+            mark[i] = ("c" + q, count[q])
+        total[mark[i][0]] = mark[i][1]
+    for s, v in total.items():
+        if all(kn.get(s, 0) < v for kn in know.values()):
+            g.wait_ge(T.sem[s], v)

@@ -1,417 +1,409 @@
+from concourse.bass import DstId, RemoteDMATransfer
 from concourse.mybir import AluOpType as ALU, ActivationFunctionType as ACT
-
-CFG = {
-    "np": 2,
-    "path": [["SVSV", "SVSV"], ["SSSS", "SSSS"], ["SSSS", "SSSS"], ["SSSS", "SSSS"]],
-    "sub": ["D", "D", "D", "V"],
-    "sum": ["D", "D", "D", "P"],
-    "halves": [[1, 1], [1, 1], [1, 1], [1, 2]],
-    "chain": ["SS", "SS", "SS", "SS"],
-    "void": ["VV", "VV", "VV", "VV"],
-    "egat": [["SS", "SS"], ["SS", "SS"], ["SS", "SS"], ["SS", "SS"]],
-    "bonus": {}, "ptv": 10, "slack": 100.0, "off": 20000.0,
-}
-COST = {"cy": 0.83 * 1.25, "G": 1.56, "fix": 25.0, "pe": 0.52, "pefix": 5.0, "same": 100.0, "cross": 150.0,
-        "dma": 2000.0, "bw": 500.0, "gi": 1000.0, "yi": 100.0, "rem": 3500.0}
 
 F32, BF, I32, U16 = "float32", "bfloat16", "int32", "uint16"
 
+SCRATCH = {
+    "nds": ("sbuf", [128, 16, 16], I32), "ia": ("sbuf", [128, 3, 16, 16], I32),
+    "eas": ("sbuf", [128, 4096], BF), "ers": ("sbuf", [128, 1024], BF),
+    "dls": ("sbuf", [128, 4], F32), "mm": ("sbuf", [128, 8], F32),
+    "fr": ("sbuf", [128, 8, 2048], BF),
+    "pt0": ("sbuf", [128, 5120], BF), "pt1": ("sbuf", [128, 5120], BF), "nt": ("sbuf", [128, 5120], F32),
+    "jx": ("sbuf", [128, 2, 144], F32), "pi": ("sbuf", [128, 8], I32), "pf": ("sbuf", [128, 8], F32),
+    "zz": ("sbuf", [128, 3, 2, 144], BF), "idb": ("sbuf", [128, 4, 128], BF), "idf": ("sbuf", [128, 2, 128], F32),
+    "sc": ("sbuf", [128, 256], BF), "sf": ("sbuf", [128, 8, 64], F32),
+    "hl": ("sbuf", [128, 10, 2, 2, 128], BF), "ul": ("sbuf", [128, 2560], U16), "o2": ("sbuf", [128, 2, 2, 192], F32),
+    "eq": ("sbuf", [128, 2, 8, 256], BF),
+    "dd": ("sbuf", [128, 8192], BF), "md": ("sbuf", [128, 8192], BF),
+    "sv": ("sbuf", [128, 4, 72, 16], F32),
+    "kk": ("sbuf", [128, 2, 16, 16], F32),
+    "ne0": ("sbuf", [128, 2, 2048], F32), "ne1": ("sbuf", [128, 2, 2048], F32), "ne2": ("sbuf", [128, 2, 2048], F32),
+    "tt": ("sbuf", [128, 256], F32), "cs": ("sbuf", [128, 256], F32),
+    "bs": ("sbuf", [128, 2, 2, 1024], F32), "so": ("sbuf", [128, 256], F32), "s2": ("sbuf", [128, 256], F32),
+    "key0": ("psum", [128, 4, 128], F32), "key1": ("psum", [128, 4, 128], F32), "aa": ("psum", [128, 512], F32),
+    "bb": ("psum", [128, 512], F32), "xb": ("psum", [128, 512], F32),
+    "sp": ("psum", [128, 4, 24, 16], F32),
+}
 
-def scratch(NP):
-    LW, IW = 256 // NP, 16 // NP
-    return {
-        "nds": ("sbuf", [128, 16, 16], I32), "ia": ("sbuf", [128, 3, 16, 16], I32),
-        "eas": ("sbuf", [128, 4096], BF), "ers": ("sbuf", [128, 1024], BF),
-        "dls": ("sbuf", [128, 4], F32), "mm": ("sbuf", [128, 4], F32), "mb": ("sbuf", [128, 36], F32),
-        "fr": ("sbuf", [128, 4 * NP, 1024], BF), "cs": ("sbuf", [128, 256], F32),
-        "pt0": ("sbuf", [128, 5120], BF), "pt1": ("sbuf", [128, 5120], BF), "nt": ("sbuf", [128, 5120], F32),
-        "jx": ("sbuf", [128, 144], F32), "pi": ("sbuf", [128, 8], I32), "pf": ("sbuf", [128, 8], F32),
-        "zz": ("sbuf", [128, 6, 144], BF), "idb": ("sbuf", [128, 5, 128], BF), "h2": ("sbuf", [128, NP, 2, 2 * LW], BF), "idf": ("sbuf", [128, 128], F32),
-        "sf": ("sbuf", [128, 2, 4 * NP, 64], BF), "sc": ("sbuf", [128, 32 * IW], BF),
-        "hl": ("sbuf", [128, 5 * NP, 2, 2, LW], BF), "ul": ("sbuf", [128, 2560], U16), "o2": ("sbuf", [128, NP, 2 * LW], F32),
-        "eq": ("sbuf", [128, NP, 16, LW], BF),
-        "dd": ("sbuf", [128, 8192], BF), "md": ("sbuf", [128, 8192], BF),
-        "sv": ("sbuf", [128, 2 * NP, 120, 2 * IW], F32),
-        "kk": ("sbuf", [128, NP, 16, 2 * IW], F32),
-        "ne0": ("sbuf", [128, NP, 16 * LW], F32), "ne1": ("sbuf", [128, NP, 16 * LW], F32), "ne2": ("sbuf", [128, NP, 16 * LW], F32),
-        "tt": ("sbuf", [128, 2, 256], F32), "cc": ("sbuf", [128, 2, 256], F32), "aa": ("sbuf", [128, 2, 256], F32),
-        "bs": ("sbuf", [128, 2 * NP, 4 * LW], F32), "so": ("sbuf", [128, 256], F32),
-        "key": ("psum", [128, 2 * NP, 2, 8 * IW], F32), "up": ("psum", [128, 512], F32),
-        "fp0": ("psum", [128, 512], F32), "fp1": ("psum", [128, 512], F32), "bb": ("psum", [128, 512], F32),
-        "sp0": ("psum", [128, 2 * NP, 8, 2 * IW], F32), "sp1": ("psum", [128, 2 * NP, 8, 2 * IW], F32), "sp2": ("psum", [128, 2 * NP, 8, 2 * IW], F32),
-    }
-
-
-NET = [(0,0,0,0,0,1,8,2,4),(0,0,1,1,4,1,0,2,4),(0,1,0,0,0,1,9,2,4),(0,1,1,1,4,1,1,2,4),
-       (1,0,0,0,0,1,16,2,4),(1,0,1,2,4,1,0,2,4),(1,1,0,0,0,1,17,2,4),(1,1,1,2,4,1,1,2,4),
-       (2,0,0,0,0,1,24,2,4),(2,0,1,0,4,1,0,2,4),(2,1,0,0,0,1,25,2,4),(2,1,1,0,4,1,1,2,4),
-       (3,0,0,0,0,1,80,1,1),(3,0,0,0,4,3,33,5,2),(3,0,1,1,1,2,2,3,2),(3,0,1,1,2,3,1,2,2),(3,0,1,1,6,1,7,1,1),
-       (3,1,0,0,0,1,34,5,2),(3,1,0,0,2,1,35,1,3),(3,1,1,1,5,1,4,2,2),(3,1,1,1,7,1,0,1,1),
-       (4,0,0,0,1,4,44,1,2),(4,0,0,0,6,1,46,2,2),(4,0,1,2,2,1,4,1,3),(4,1,0,0,2,1,42,5,2),(4,1,0,0,4,3,43,12,2),
-       (4,1,1,2,1,4,2,5,2),(4,1,1,2,6,1,3,1,1),
-       (5,0,0,0,2,2,52,29,2),(5,0,0,0,5,2,60,2,2),(5,0,1,0,3,3,2,5,2),(5,1,0,0,6,1,50,13,2),(5,1,1,0,2,2,0,4,2),(5,1,1,1,3,2,1,4,2),
-       (6,0,0,0,2,2,70,12,2),(6,0,1,1,0,7,4,2,2),(6,1,0,0,0,4,61,4,2),(6,1,1,1,2,5,2,5,2),
-       (7,0,1,2,4,1,1,2,4),(7,1,0,0,4,1,67,2,3),(7,1,1,2,7,1,6,1,1),
-       (8,0,0,0,1,2,83,2,2),(8,0,1,0,5,2,0,1,2),(8,0,1,1,6,1,4,1,1),(8,1,0,0,1,1,84,1,1),(8,1,0,0,3,2,72,1,2),(8,1,1,1,6,1,3,2,2),
-       (9,0,0,0,0,1,86,1,1),(9,0,1,1,1,1,7,1,1),(9,1,0,0,0,1,87,1,1),(9,1,1,1,1,1,6,1,1)]
+NET = [(0, 0, 1, 0, 1, 4, 0, 8, 2), (1, 0, 1, 0, 1, 4, 1, 9, 2), (0, 4, 1, 4, 1, 4, 1, 8, 2), (1, 4, 1, 4, 1, 4, 0, 9, 2),
+       (1, 8, 1, 8, 1, 4, 0, 27, 1), (0, 12, 1, 12, 1, 4, 0, 16, 1), (1, 12, 1, 12, 1, 4, 1, 18, 1), (0, 8, 1, 8, 1, 4, 1, 4, 1),
+       (0, 27, 2, 5, 2, 2, 0, 20, 2), (1, 27, 2, 5, 2, 2, 1, 14, 2), (0, 17, 2, 18, 2, 2, 1, 9, 2), (1, 17, 2, 18, 2, 2, 0, 24, 2),
+       (1, 16, 4, 4, 5, 4, 0, 31, 9), (0, 18, 4, 6, 5, 4, 0, 44, 9), (0, 16, 4, 4, 5, 4, 1, 22, -5), (1, 18, 4, 6, 5, 4, 1, 23, -5),
+       (0, 31, 9, 12, -5, 2, 0, 45, 2), (0, 62, 9, 23, -5, 2, 1, 5, 4), (1, 31, 9, 12, -5, 2, 1, 19, 2), (1, 62, 9, 23, -5, 2, 0, 55, 2),
+       (0, 45, 2, 17, 2, 3, 0, 46, 4), (1, 53, 2, 5, 4, 3, 0, 48, 4), (1, 45, 2, 17, 2, 3, 1, 18, -4), (0, 53, 2, 5, 4, 3, 1, 20, -4),
+       (1, 44, 2, 22, -2, 4, 0, 1, 1), (1, 52, 2, 14, -2, 4, 0, 40, 1), (0, 52, 2, 14, -2, 4, 1, 9, 2), (0, 44, 2, 22, -2, 4, 1, 7, -1),
+       (0, 1, 1, 9, 2, 4, 0, 36, 1), (1, 1, 1, 9, 2, 4, 1, 3, -1),
+       (0, 36, 1, 5, -1, 6, 0, 0, 7), (1, 36, 1, 5, -1, 6, 1, 8, 2),
+       (0, 0, 7, 6, 2, 7, 0, 50, -1), (1, 0, 7, 6, 2, 7, 1, 9, 2)]
 MAGIC = 1.5 * 2.0 ** 30
-EVEN = 1.5 * 2.0 ** 24
 BIG = 2.0 ** 24
-SP = ["sp0", "sp1", "sp2"]
+
+
+def pieces(spec):
+    out, a = [], 0
+    for i in range(0, len(spec), 2):
+        n = int(spec[i + 1]); out.append((spec[i], a, n)); a += n
+    return out
 
 
 def build(cfg):
-    NP = cfg["np"]; LW, IW = 256 // NP, 16 // NP; VB = 2 * IW; NC = 8 // NP; SW = 8 * IW; FW = 4 * LW
     ops = []
     tag = ["init", 0]
 
-    def add(q, kind, n, fn, r=(), w=(), banks=(), gat=False):
+    def add(q, kind, n, fn, r=(), w=(), banks=(), gat=False, grp=None):
         ops.append({"q": q, "kind": kind, "n": n, "fn": fn, "r": list(r), "w": list(w), "banks": list(banks), "gat": gat,
-                    "bonus": cfg["bonus"].get(tag[0], 0.0) - cfg["off"] * tag[1]})
+                    "tag": tag[0], "part": tag[1], "grp": grp, "last": [False]})
 
     def V(n, fn, r, w, banks=(), gat=False): add("V", "c", n, lambda g, T: [fn(g.vector, T)], r, w, banks, gat)
     def S(n, fn, r, w, banks=(), gat=False): add("S", "c", n, lambda g, T: [fn(g.scalar, T)], r, w, banks, gat)
     def GC(n, fn, r, w): add("G", "c", n, lambda g, T: [fn(g, T)], r, w)
-    def Y(nb, fn, r, w): add("Y", "d", nb, lambda g, T: [fn(g.sync, T)], r, w)
-    def SD(nb, fn, r, w): add("S", "d", nb, lambda g, T: [fn(g.scalar, T)], r, w)
-    def GD(nb, fn, r, w): add("G", "d", nb, lambda g, T: [fn(g, T)], r, w)
+    def Y(nb, fn, r, w, runs=1): add("Y", "d", (nb, runs), lambda g, T: [fn(g.sync, T)], r, w)
+    def SD(nb, fn, r, w): add("S", "d", (nb, 1), lambda g, T: [fn(g.scalar, T)], r, w)
+    def GD(nb, fn, r, w, runs=1): add("G", "d", (nb, runs), lambda g, T: [fn(g, T)], r, w)
 
-    def PE(mms, r, w, banks, start=True, stop=True):
+    def PE(mms, r, w, banks, start=True, stop=True, grp=None):
+        last = [False]
         def fn(g, T):
             out = []
             for i, m in enumerate(mms):
                 o, a, b = m[1](T)
-                out.append(g.tensor.matmul(o, a, b, start and i == 0, stop and i == len(mms) - 1))
+                out.append(g.tensor.matmul(o, a, b, start and i == 0, (last[0] if grp else stop) and i == len(mms) - 1))
             return out
-        add("P", "c", [m[0] for m in mms], fn, r, w, banks)
+        add("P", "c", [m[0] for m in mms], fn, r, w, banks, grp=grp)
+        ops[-1]["last"] = last
 
-    def sl(a, s, n): return slice(a, a + s * (n - 1) + 1, s)
+    def sl(a, s, n): return slice(a, a + s * (n - 1) + 1, s) if s > 0 else slice(a, a + s * n if a + s * n >= 0 else None, s)
+    def blk(q, n=1): return slice(q * 256, (q + n) * 256)
+    def hb(q, n=1): return slice(q * 128, (q + n) * 128)
 
     Y(1 << 17, lambda e, T: e.dma_start(T.nds[:], T.nd[:]), [], ["nds"])
-    PAS = [("md", c // NC, c % NC, j) for c in range(4) for j in range(2)]
+    PAS = [("md", j) for j in range(8)]
     SD(1 << 20, lambda e, T: e.dma_start(T.md[:, 0:4096], T.pa[:]), [], PAS)
     for j in range(4):
-        Y(1 << 18, lambda e, T, j=j: e.dma_start(T.fr[:, :, j * LW:(j + 1) * LW], T.fc[:]), [], [("fr", j)])
-    FR = [("fr", j) for j in range(4)]
-    if NP == 2:
-        Y(1 << 20, lambda e, T: e.dma_start(T.fr[:, :, 512:1024], T.fr[:, :, 0:512]), FR, ["fr2"])
-    Y(1 << 20, lambda e, T: e.dma_start(T.eas[:], T.ea[:]), FR, ["eas"])
-    Y(1 << 18, lambda e, T: e.dma_start(T.ers[:], T.er[:]), FR, ["ers"])
-    Y(1 << 10, lambda e, T: e.dma_start(T.dls[:, 0:1], T.dl[:]), FR, ["dls"])
-    GC(450, lambda g, T: g.iota(T.jx[:], [[1, 144]], 0, 0, allow_small_or_imprecise_dtypes=True), [], ["jx"])
+        Y(1 << 16, lambda e, T, j=j: e.dma_start(T.fr[:, 0:2, hb(j)], T.fc[:, blk(0)]), [], [("fr", 0, j)], 2)
+    Y(1 << 18, lambda e, T: e.dma_start(T.fr[:, 0:2, 512:1024], T.fr[:, 0:2, 0:512]), [("fr", 0, j) for j in range(4)], [("fr", 0, 4)], 2)
+    def FR(t, n): return [("fr", 0, j) for j in range(3 + n // 512)] if t == 0 else [("fr", min(t, 2), m) for m in (128, 256, 512, 1024, 2048) if m < 2 * n]
+    Y(1 << 20, lambda e, T: e.dma_start(T.eas[:], T.ea[:]), PAS, ["eas"])
+    tag[0] = "late"
+    for j, a, z in ((1, 2, 4), (2, 4, 8)):
+        wide = max(n for x in cfg["path"][a:z] for _, _, n in pieces(x)) * 512
+        Y((z - a) << 15, lambda e, T, a=a, z=z: e.dma_start(T.fr[:, a:z, 0:128], T.fc[:, hb(a, z - a)]), ["eas"], [("fr", j, 128)], z - a)
+        for n in (128, 256, 512, 1024):
+            if n < wide:
+                Y(n * (z - a) * 256, lambda e, T, n=n, a=a, z=z: e.dma_start(T.fr[:, a:z, n:2 * n], T.fr[:, a:z, 0:n]),
+                  [("fr", j, m) for m in (128, 256, 512, 1024) if m <= n], [("fr", j, 2 * n)], z - a)
+    Y(1 << 18, lambda e, T: e.dma_start(T.ers[:], T.er[:]), ["eas"], ["ers"])
+    Y(1 << 10, lambda e, T: e.dma_start(T.dls[:, 0:1], T.dl[:]), ["eas"], ["dls"])
+    MM = [("mm", s) for s in range(5)]
+    for s, val in enumerate((1.0, -1.0, 1.5, 2.0, -2.0)):
+        S(1, lambda a, T, s=s, val=val: a.activation(T.mm[:, s:s + 1], T.dls[:, 0:1], ACT.Identity, scale=val), ["dls"], [MM[s]])
+    tag[0] = "init"
     GC(160, lambda g, T: g.iota(T.pi[:, 0:1], [[0, 1]], 0, 1), [], ["pi0"])
+    GC(160 + 576, lambda g, T: g.iota(T.jx[:], [[-1, 2], [1, 144]], 0, 0, allow_small_or_imprecise_dtypes=True), [], ["jx"])
     GC(160, lambda g, T: g.iota(T.pf[:, 0:1], [[0, 1]], 0, 1, allow_small_or_imprecise_dtypes=True), [], ["pf0"])
-    GC(160 + 64 * IW, lambda g, T: g.iota(T.sc[:], [[128, 32], [0, IW]], 0, 0, allow_small_or_imprecise_dtypes=True), [], ["sc"])
+    GC(160 + 512, lambda g, T: g.iota(T.sc[:], [[128, 32], [0, 8]], 0, 0, allow_small_or_imprecise_dtypes=True), [], ["sc"])
     V(1, lambda v, T: v.tensor_scalar(T.pi[:, 4:5], T.pi[:, 0:1], 112, None, ALU.bitwise_and), ["pi0"], ["pi4"])
-    for i in range(2):
-        V(1, lambda v, T, i=i: v.tensor_scalar(T.pf[:, 4 + i:5 + i], T.pi[:, 4:5], float(14 + i), None, ALU.add), ["pi4"], [("pf", i)])
-    for s, val in enumerate((4096.0, 8192.0, -4096.0)):
-        for i in range(2):
-            V(144, lambda v, T, s=s, i=i, val=val: v.tensor_scalar(T.zz[:, 2 * s + i, :], T.jx[:], T.pf[:, 4 + i:5 + i], val, ALU.is_equal, ALU.mult),
-              ["jx", ("pf", i)], [("zz", s, i)])
-    for s, val in enumerate((1.0, 64.0, BIG, -1.0, -64.0)):
-        V(128, lambda v, T, s=s, val=val: v.tensor_scalar(T.idb[:, s, :], T.jx[:, 0:128], T.pf[:, 0:1], val, ALU.is_equal, ALU.mult), ["jx", "pf0"], [("idb", s)])
-    V(128, lambda v, T: v.tensor_scalar(T.idf[:], T.jx[:, 0:128], T.pf[:, 0:1], None, ALU.is_equal), ["jx", "pf0"], ["idf"])
-    V(1, lambda v, T: v.tensor_scalar(T.mm[:, 0:1], T.dls[:, 0:1], 2.0, None, ALU.mult), ["dls"], ["mm"])
-    V(16, lambda v, T: v.tensor_scalar(T.mb[:, 20:36], T.jx[:, 0:16], -0.5, 9.0, ALU.mult, ALU.add), ["jx"], ["mb0"])
-    V(16, lambda v, T: v.tensor_scalar(T.mb[:, 0:16], T.mb[:, 20:36], T.dls[:, 0:1], None, ALU.mult), ["mb0", "dls"], ["mb1"])
-    V(1, lambda v, T: v.tensor_copy(T.mb[:, 0:1], T.dls[:, 0:1]), ["mb1", "dls"], ["mb2"])
-    V(1, lambda v, T: v.tensor_scalar(T.mb[:, 16:17], T.dls[:, 0:1], 16.0, None, ALU.mult), ["mb2", "dls"], ["mb"])
+    V(1, lambda v, T: v.tensor_scalar(T.pf[:, 4:5], T.pi[:, 4:5], 14.0, None, ALU.add), ["pi4"], ["pf4"])
+    V(288, lambda v, T: v.tensor_scalar(T.zz[:, 0], T.jx[:], T.pf[:, 4:5], 4096.0, ALU.is_equal, ALU.mult), ["jx", "pf4"], [("zz", 0)])
+    for s, val in ((1, 2.0), (2, -1.0)):
+        S(288, lambda a, T, s=s, val=val: a.activation(T.zz[:, s], T.zz[:, 0], ACT.Identity, scale=val), [("zz", 0)], [("zz", s)])
+    V(128, lambda v, T: v.tensor_scalar(T.idb[:, 0, :], T.jx[:, 0, 0:128], T.pf[:, 0:1], None, ALU.is_equal), ["jx", "pf0"], [("idb", 0)])
+    for s, val in ((1, 64.0), (2, BIG)):
+        S(128, lambda a, T, s=s, val=val: a.activation(T.idb[:, s, :], T.idb[:, 0, :], ACT.Identity, scale=val), [("idb", 0)], [("idb", s)])
+    tag[0] = "late"
+    S(128, lambda a, T: a.activation(T.idb[:, 3, :], T.idb[:, 0, :], ACT.Identity, scale=-1.0), [("idb", 0)], [("idb", 3)])
+    for s, val in enumerate((0.5, 1.0)):
+        S(128, lambda a, T, s=s, val=val: a.activation(T.idf[:, s, :], T.idb[:, 0, :], ACT.Identity, scale=val), [("idb", 0)], [("idf", s)])
+    tag[0] = "init"
 
     def zw(T, s, r):
         i = r & 1
-        return T.zz[:, 2 * s + i, 14 + i - r:142 + i - r]
-    def ZT(s): return [("zz", s, 0), ("zz", s, 1)]
-    BB = [("b", d, i) for d in range(2) for i in range(4)]
-
-    PE([(256, lambda T, r=r: (T.bb[:, 0:256], zw(T, 2, r), T.fr[:, :, r:FW:16])) for r in range(16)], ZT(2) + FR, BB, ["bb"])
-    for j in range(NP):
-        w_ = 64 // NP
-        V(256, lambda v, T, j=j, w_=w_: v.tensor_copy(T.sf[:, 0, :, j * w_:(j + 1) * w_], T.bb[:, 0:256]), BB, [("sf0", j)], ["bb"])
-        V(256, lambda v, T, j=j, w_=w_: v.tensor_tensor(T.sf[:, 1, :, j * w_:(j + 1) * w_], T.bb[:, 0:256], T.sf[:, 0, :, j * w_:(j + 1) * w_], ALU.subtract),
-          BB + [("sf0", j)], [("sf1", j)], ["bb"])
-    SF = [(a, j) for a in ("sf0", "sf1") for j in range(NP)]
+        return T.zz[:, s, i, 14 + i - r:142 + i - r]
 
     V(256, lambda v, T: v.tensor_scalar(T.ia[:, 0], T.nds[:], 15, None, ALU.bitwise_and), ["nds"], ["ia0"])
     V(256, lambda v, T: v.tensor_scalar(T.ia[:, 1], T.nds[:], 10, None, ALU.logical_shift_right), ["nds"], ["ia1"])
     V(256, lambda v, T: v.tensor_scalar(T.ia[:, 2], T.nds[:], 4, 63, ALU.logical_shift_right, ALU.bitwise_and), ["nds"], ["ia2"])
-    for p in range(NP):
-        c = slice(p * IW, (p + 1) * IW); u0 = 2 * LW * p
-        V(LW, lambda v, T, c=c, u0=u0: v.tensor_scalar(T.up[:, u0:u0 + LW], T.ia[:, 0, :, c], 4.0, -32.0, ALU.mult, ALU.add), ["ia0"], [("up", p, 0)], ["up"])
-        V(LW, lambda v, T, c=c, u0=u0, p=p: v.tensor_tensor(T.hl[:, p, 0, 0, :], T.ia[:, 1, :, c], T.up[:, u0:u0 + LW], ALU.add), ["ia1", ("up", p, 0)], [("hl", 0, p, 0, 0)], ["up"])
-        V(LW, lambda v, T, c=c, p=p: v.tensor_scalar(T.hl[:, p, 0, 1, :], T.ia[:, 2, :, c], -32.0, None, ALU.add), ["ia2"], [("hl", 0, p, 0, 1)])
+    for p in range(2):
+        c = slice(8 * p, 8 * p + 8)
+        V(128, lambda v, T, c=c, p=p: v.tensor_scalar(T.xb[:, hb(p)], T.ia[:, 0, :, c], 4.0, None, ALU.mult), ["ia0"], [("xb", p)], ["xb"])
+        V(128, lambda v, T, c=c, p=p: v.tensor_tensor(T.hl[:, p, 0, 0, :], T.ia[:, 1, :, c], T.xb[:, hb(p)], ALU.add), ["ia1", ("xb", p)], [("hl", 0, p, 0, 0), "xb"], ["xb"])
+        V(128, lambda v, T, c=c, p=p: v.tensor_scalar(T.hl[:, p, 0, 1, :], T.ia[:, 2, :, c], 0.0, None, ALU.add), ["ia2"], [("hl", 0, p, 0, 1)])
 
-    def blk(q): return slice(q * 256, (q + 1) * 256)
     for q in range(1, 17):
         if q <= cfg["ptv"]:
             V(128, lambda v, T, q=q: v.tensor_copy(T.pt0[:, blk(q)], T.md[:, q % 16:4096:16]), PAS, [("pt0", q)])
         else:
             S(256, lambda a, T, q=q: a.activation(T.pt0[:, blk(q)], T.md[:, q % 16:4096:16], ACT.Copy), PAS, [("pt0", q)])
-    def pcopy(dst, q, src, qs, n):
-        Y(n << 16, lambda e, T: e.dma_start(T[dst][:, q * 256:(q + n) * 256], T[src][:, qs * 256:(qs + n) * 256]),
-          [(src, qs + i) for i in range(n)], [(dst, q + i) for i in range(n)])
-    def pnew(dst, d):
-        Y(1 << 16, lambda e, T: e.dma_start(T[dst][:, blk(16 + d)], T.fc[:, blk(d)]), [], [(dst, 16 + d)])
     tag[0] = "late"
+    def pcopy(dst, q, src, qs, n):
+        Y(n << 16, lambda e, T: e.dma_start(T[dst][:, blk(q, n)], T[src][:, blk(qs, n)]), [(src, qs + i) for i in range(n)], [(dst, q + i) for i in range(n)])
+    def pnew(dst, d):
+        Y(1 << 16, lambda e, T: e.dma_start(T[dst][:, blk(16 + d)], T.fc[:, blk(d)]), ["eas"], [(dst, 16 + d)])
     pcopy("pt1", 2, "pt0", 2, 14); pcopy("pt1", 17, "pt0", 1, 1); pcopy("pt1", 19, "pt0", 3, 1); pcopy("pt0", 18, "pt0", 2, 1)
     pnew("pt1", 0); pnew("pt1", 2); pnew("pt0", 1)
-    for q in range(1, 20):
-        S(256, lambda a, T, q=q: a.activation(T.nt[:, blk(q)], T.eas[:, q % 16::16], ACT.Identity, scale=-1.0), ["eas"], [("nt", q, p) for p in range(NP)])
+    def NT(q): return [("nt", q, i) for i in range(2)]
+    for q in range(1, 17):
+        S(256, lambda a, T, q=q: a.activation(T.nt[:, blk(q)], T.eas[:, q % 16::16], ACT.Identity, scale=-1.0), ["eas"], NT(q))
+    Y(3 << 17, lambda e, T: e.dma_start(T.nt[:, blk(17, 3)], T.nt[:, blk(1, 3)]), NT(1) + NT(2) + NT(3), NT(17) + NT(18) + NT(19))
 
-    def umm(t, p, h, half):
-        c0 = (2 * p + half) * LW
-        PE([(LW, lambda T: (T.up[:, c0:c0 + LW], T.idb[:, 1, :], T.hl[:, t * NP + p, h, 0, :])),
-            (LW, lambda T: (T.up[:, c0:c0 + LW], T.idb[:, 0, :], T.hl[:, t * NP + p, h, 1, :]))],
-           [("hl", t, p, h, 0), ("hl", t, p, h, 1), ("idb", 0), ("idb", 1)], [("up", p, half)], ["up"])
+    if "F" in "".join(cfg["path"]):
+        PE([(384, lambda T, r=r: (T.bb[:, 0:384], zw(T, 2, r), T.fr[:, 2:8, r:1024:16])) for r in range(16)], [("zz", 2)] + FR(1, 1024) + FR(2, 1024), ["bb"], ["bb"])
+        S(384, lambda a, T: a.activation(T.sf[:, 2:8, :], T.bb[:, 0:384], ACT.Copy), ["bb"], ["sf"], ["bb"])
 
-    def ucol(t, p, h): return ((t * NP + p) * 2 + h) * LW
+    def ucol(t, p, h): return ((2 * t + p) * 2 + h) * 128
 
-    def u16(t, p, h):
+    def number(t, p, h, twice=True):
+        def umm(j):
+            PE([(128, lambda T, du=du: (T.aa[:, hb(2 * p + j)], T.idb[:, 1 - du, :], T.hl[:, 2 * t + p, h, du, :])) for du in range(2)],
+               [("hl", t, p, h, 0), ("hl", t, p, h, 1), ("idb", 0), ("idb", 1)], [("aa", p, j)], ["aa"])
+        old = tag[0]; tag[0] = "u%d" % t
+        umm(0)
+        if twice: umm(1)
         c = ucol(t, p, h)
-        V(LW, lambda v, T: v.tensor_scalar(T.ul[:, c:c + LW], T.up[:, 2 * p * LW:(2 * p + 1) * LW], 2080.0, None, ALU.add), [("up", p, 0)], [("ul", t, p, h)], ["up"])
+        V(128, lambda v, T: v.tensor_copy(T.ul[:, c:c + 128], T.aa[:, hb(2 * p)]), [("aa", p, 0)], [("ul", t, p, h)], ["aa"])
+        tag[0] = old
 
     def own_lists(t, p):
         if t < 4:
-            add("G", "r", t * NP + p, None, [("hl", t, p, 0, 0), ("hl", t, p, 0, 1)], [("hl", t, p, 1, 0), ("hl", t, p, 1, 1)])
-        umm(t, p, 0, 0)
-        u16(t, p, 0)
-        if t < 4 and cfg["void"][t][p] == "S":
+            add("G", "r", 2 * t + p, None, [("hl", t, p, 0, 0), ("hl", t, p, 0, 1)], [("hl", t, p, 1, 0), ("hl", t, p, 1, 1)])
+        number(t, p, 0, t < 4)
+        if t < 4:
             for j in range(2):
-                Y(1 << 16, lambda e, T, j=j: e.dma_start(T.h2[:, p, :, j * LW:(j + 1) * LW], T.hl[:, t * NP + p, 0]),
-                  [("hl", t, p, 0, 0), ("hl", t, p, 0, 1)], [("h2", p, j)])
-        elif t < 4:
-            umm(t, p, 0, 1)
-            S(2 * LW, lambda a, T: a.activation(T.o2[:, p, :], T.up[:, 2 * p * LW:(2 * p + 2) * LW], ACT.Copy), [("up", p, 0), ("up", p, 1)], [("o2", p)], ["up"])
+                a0 = 256 * p + 64 * j
+                S(184, lambda a, T, j=j, a0=a0: a.activation(T.o2[:, p, j, 0:184], T.aa[:, a0:a0 + 184], ACT.Copy), [("aa", p, 0), ("aa", p, 1)], [("o2", p, j)], ["aa"])
 
     def select(t, p):
-        w0 = (t + 1) * 256; tp_ = t * NP + p
-        pt = "pt%d" % (t % 2); fp = "fp%d" % p
+        w0 = (t + 1) * 256; tp_ = 2 * t + p; pt = "pt%d" % (t % 2); key = "key%d" % p
         PW = [(pt, q) for q in range(t + 1, t + 17)]
-        path = cfg["path"][t][p]
-        assert not ("S" in path and cfg["void"][t][p] == "S")
-        if "S" in path:
-            PE([(512, lambda T: (T[fp][:], T.idb[:, 0, :], T.fr[:, tp_, 0:512]))], FR + [("idb", 0)], [fp], [fp])
-        umm(t, p, 1, 0)
-        u16(t, p, 1)
-        sign = cfg["void"][t][p] == "S"
-        if sign:
-            nr = 512 // LW; u1 = (2 * p + 1) * LW
-            for r0 in range(0, 16, nr):
-                for r in range(r0, r0 + nr):
-                    def out(T, r=r, r0=r0): return T[fp][:, (r - r0) * LW:(r - r0 + 1) * LW]
-                    PE([(LW, lambda T, out=out, du=du: (out(T), T.idb[:, 1 - du, :], T.hl[:, tp_, 1, du, :])) for du in range(2)] +
-                       [(LW, lambda T, out=out, du=du, r=r: (out(T), T.idb[:, 4 - du, :], T.h2[:, p, du, IW * r:IW * r + LW])) for du in range(2)],
-                       [("hl", t, p, 1, 0), ("hl", t, p, 1, 1), ("h2", p, 0), ("h2", p, 1)] + [("idb", i) for i in (0, 1, 3, 4)], [(fp, r - r0)] + ([fp] if r0 == 0 else []), [fp])
-                S(512, lambda a, T, r0=r0: a.activation(T.eq[:, p, r0:r0 + nr, :], T[fp][:], ACT.Sign), [(fp, i) for i in range(nr)],
-                  [("eq", p, r) for r in range(r0, r0 + nr)] + ([fp] if r0 + nr == 16 else []), [fp])
-            PE([(LW, lambda T, r=r: (T.up[:, u1:u1 + LW], T.idb[:, 0, :], T.eq[:, p, r, :])) for r in range(16)],
-               [("eq", p, r) for r in range(16)] + [("idb", 0)], [("up", p, 1)], ["up"])
-            V(LW, lambda v, T: v.tensor_scalar(T.o2[:, p, 0:LW], T.up[:, u1:u1 + LW], EVEN, -EVEN, ALU.add, ALU.add), [("up", p, 1)], [("o2", p)], ["up"])
-            V(LW, lambda v, T: v.tensor_tensor(T.eq[:, p, 0, :], T.o2[:, p, 0:LW], T.up[:, u1:u1 + LW], ALU.not_equal), [("up", p, 1), ("o2", p)], [("eq", p, 0)], ["up"])
-        else:
-            for r in range(16):
-                V(LW, lambda v, T, r=r: v.tensor_tensor(T.eq[:, p, r, :], T.o2[:, p, IW * r:IW * r + LW], T.up[:, 2 * p * LW:(2 * p + 1) * LW], ALU.is_equal),
-                  [("o2", p), ("up", p, 0)], [("eq", p, r)], ["up"])
-        for c in range(NC):
-            h, kc = c // (NC // 2), (c % (NC // 2)) * 64
-            o0 = ucol(t, p, h) + kc
-            d0 = (p * NC + c) * 1024
-            def win(T, a=0, n=64, o0=o0): return T[pt][:, w0:w0 + 4096].indirect(T.ul[:, o0 + a:o0 + a + n])
-            def ko(T, h=h, kc=kc): return T.key[:, 2 * p + h, kc // SW, kc % SW:kc % SW + 64]
+        grp = (key, t)
+        KEY = [(key, j) for j in range(8)] + [(key, "v", r) for r in range(8)]
+        PE([(256, lambda T: (T[key][:, 0:2, :], T.idb[:, 0, :], T.sc[:]))], ["sc", ("idb", 0)], KEY + [(key, "open")], [key], True, grp=grp)
+
+        def chunk(who, u0, nu):
+            e0, n = p * 4096 + u0 * 512, nu * 512; h = u0 // 4; o0 = ucol(t, p, 0) + u0 * 32; k0 = u0 % 4 * 32
+            def win(T): return T[pt][:, w0:w0 + 4096].indirect(T.ul[:, o0:o0 + n // 16])
+            def dd(T): return T.dd[:, e0:e0 + n]
+            def md(T): return T.md[:, e0:e0 + n]
             rd = PW + [("ul", t, p, h)]
-            dt_ = [("dd", p, c, 0), ("dd", p, c, 1)]; mt = [("md", p, c, 0), ("md", p, c, 1)]
-            def relu(d0=d0, dt_=dt_, mt=mt):
-                V(512, lambda v, T: v.tensor_scalar(T.md[:, d0:d0 + 1024], T.dd[:, d0:d0 + 1024], 0.0, None, ALU.max), dt_, mt)
-            parts = [(2, "dd"), (1, "md")]
-            if path[c] == "S":
-                S(1024, lambda a, T, win=win, d0=d0: a.activation(T.dd[:, d0:d0 + 1024], win(T), ACT.Copy), rd, dt_, gat=True)
-                for j in range(2):
-                    e0 = d0 + 512 * j
-                    V(512, lambda v, T, e0=e0: v.tensor_tensor(T.md[:, e0:e0 + 512], T.dd[:, e0:e0 + 512], T[fp][:], ALU.max), dt_ + [fp], [mt[j]], [fp])
-            elif path[c] == "D":
-                S(1024, lambda a, T, win=win, d0=d0: a.activation(T.dd[:, d0:d0 + 1024], win(T), ACT.Identity, scale=-1.0), rd, dt_, gat=True)
-                GD(1 << 19, lambda g, T, d0=d0: g.dma_start(T.dd[:, d0:d0 + 1024], T.fr[:, tp_, :], accum_op=ALU.add), FR + ["fr2"] + dt_, dt_)
-                relu()
+            dt_ = [("dd", 8 * p + u0 + j) for j in range(nu)]; mt = [("md", 8 * p + u0 + j) for j in range(nu)]
+            if who == "F":
+                S(n, lambda a, T: a.activation(dd(T), win(T), ACT.Copy), rd, dt_, gat=True)
+                add("G", "f", (n * 512, 2), lambda g, T: (md(T), 2, [(md(T), [dd(T), T.fr[:, tp_, 0:n]])]), FR(t, n) + dt_, mt)
+                ops[-1]["slot"] = 8 * p + u0
+                PE([(n // 4, lambda T: (T[key][:, h, k0:k0 + n // 16], T.idf[:, 1, :], T.sf[:, tp_, 0:n // 16]))], ["sf", ("idf", 1), (key, "open")],
+                   [(key, u0 + j) for j in range(nu)], [key], False, grp=grp)
+            elif who in "DA":
+                S(n, lambda a, T: a.activation(dd(T), win(T), ACT.Identity, scale=-1.0), rd, dt_, gat=True)
+                GD(n * 512, lambda g, T: g.dma_start(dd(T), T.fr[:, tp_, 0:n], accum_op=ALU.add), FR(t, n) + dt_, dt_)
             else:
-                for j in range(NP):
-                    V(FW, lambda v, T, win=win, j=j, e0=d0 + j * FW: v.tensor_tensor(T.dd[:, e0:e0 + FW], win(T, j * FW // 16, FW // 16), T.fr[:, tp_, 0:FW], ALU.subtract),
-                      rd + FR, dt_[j:j + 3 - NP], gat=True)
-                if path[c] == "V":
-                    S(1024, lambda a, T, d0=d0: a.activation(T.md[:, d0:d0 + 1024], T.dd[:, d0:d0 + 1024], ACT.Abs), dt_, mt)
-                    parts = [(0, "md")]
-                else:
-                    relu()
-            mms = [(64, lambda T, ko=ko, c=c: (ko(T), T.idb[:, 0, :], T.sc[:, c * 64:c * 64 + 64]))]
-            rr = ["sc", ("idb", 0), parts[0][1] == "dd" and dt_[0] or mt[0]]
-            if path[c] == "S":
-                rr += SF
-                for i in range(2):
-                    mms.append((64, lambda T, ko=ko, i=i: (ko(T), T.idb[:, 0, :], T.sf[:, i, tp_, :])))
-            if h == 1:
-                rr += [("eq", p, r) for r in range(1 if sign else 16)] + [("idb", 2)]
-                for r in range(1 if sign else 16):
-                    mms.append((64, lambda T, ko=ko, r=r, kc=kc: (ko(T), T.idb[:, 2, :], T.eq[:, p, r, kc:kc + 64])))
-            PE(mms, rr, [("key", p, c), "turn"], ["key"], True, False)
+                V(n, lambda v, T: v.tensor_tensor(dd(T), win(T), T.fr[:, tp_, 0:n], ALU.subtract), rd + FR(t, n), dt_, gat=True)
+            if who == "F":
+                parts = [(2, "dd"), (1, "md")]
+            elif who in "DR":
+                V(n // 2, lambda v, T: v.tensor_scalar(md(T), dd(T), 0.0, None, ALU.max), dt_, mt)
+                parts = [(2, "dd"), (1, "md")]
+            else:
+                S(n, lambda a, T: a.activation(md(T), dd(T), ACT.Abs), dt_, mt)
+                parts = [(0, "md")]
             for s, name in parts:
-                mms = [(64, lambda T, ko=ko, s=s, r=r, name=name, d0=d0: (ko(T), zw(T, s, r), T[name][:, d0 + r:d0 + 1024:16])) for r in range(16)]
-                PE(mms, ZT(s) + (mt if name == "md" else dt_), [("key", p, c), "turn"], ["key"], False, name == "md")
-        if t < 2 and p == NP - 1:
+                mms = [(n // 16, lambda T, s=s, r=r, name=name: (T[key][:, h, k0:k0 + n // 16], zw(T, s, r), T[name][:, e0 + r:e0 + n:16])) for r in range(16)]
+                for x in range(0, 16, cfg["run"]):
+                    PE(mms[x:x + cfg["run"]], [("zz", s), (key, "open")] + (mt if name == "md" else dt_), [(key, u0 + j) for j in range(nu)], [key], False, grp=grp)
+
+        tag[0] = "p%d" % t
+        todo = pieces(cfg["path"][tp_])
+        for who, u0, nu in todo:
+            if u0 < 4: chunk(who, u0, nu)
+        number(t, p, 1)
+        for who, u0, nu in todo:
+            if u0 >= 4: chunk(who, u0, nu)
+        if t < 2 and p == 1:
             pnew(pt, t)
+        tag[0] = "v%d" % t
+        for r in range(8):
+            V(256, lambda v, T, r=r: v.tensor_tensor(T.eq[:, p, r, :], T.o2[:, p, :, 8 * r:8 * r + 128], T.aa[:, blk(p)], ALU.is_equal),
+              [("o2", p, 0), ("o2", p, 1), ("aa", p, 0), ("aa", p, 1)], [("eq", p, r)], ["aa"])
+            PE([(128, lambda T, r=r, j=j: (T[key][:, 1, :], T.idb[:, 2, :], T.eq[:, p, r, hb(j)])) for j in range(2)],
+               [("eq", p, r), ("idb", 2), (key, "open")], [(key, "v", r)], [key], False, grp=grp)
+        tag[0] = "s%d" % t
         H = slice(2 * p, 2 * p + 2); h0, h1 = 2 * p, 2 * p + 1
         def ts(h, x): return ("sv", p, h, x)
-        def tp(b, h, x): return ("sp", p, b, h, x)
+        def tp(h, x): return ("sp", p, h, x)
         for side in range(2):
             for du in range(2):
-                kr = [("key", p, c) for c in range(NC) if ((c % (NC // 2)) * 64) // SW == side] + [("hl", t, p, h, du) for h in range(2)]
-                dst = (lambda T, du=du: T.sv[:, H, 0:8, du * IW:(du + 1) * IW]) if side == 0 else (lambda T, du=du: T.sp0[:, H, :, du * IW:(du + 1) * IW])
-                wt = [(ts(h, x) if side == 0 else tp(0, h, x)) + (du,) for h in range(2) for x in range(8)]
-                V(LW, lambda v, T, dst=dst, side=side, du=du: v.tensor_tensor(dst(T), T.hl[:, tp_, :, du, side * SW:(side + 1) * SW], T.key[:, H, side, :], ALU.add),
-                  kr, wt, ["key"] + (["sp0"] if side else []))
+                kr = KEY + [("hl", t, p, h, du) for h in range(2)]
+                c = slice(du * 8, du * 8 + 8); x = slice(side * 64, side * 64 + 64)
+                wt = [(tp if side else ts)(h, x_) + (du,) for h in range(2) for x_ in range(8)]
+                V(128, lambda v, T, c=c, x=x, side=side, du=du: v.tensor_tensor((T.sp if side else T.sv)[:, H, 0:8, c], T.hl[:, tp_, :, du, x],
+                                                                                T[key][:, 0:2, x], ALU.add), kr, wt, [key])
         def both(xs): return [x + (du,) for x in xs for du in range(2)]
-        for (l, op, side, bank, i0, si, p0, so, n) in NET:
-            ins = [i0 + si * j for j in range(n)]; outs = [p0 + so * j for j in range(n)]
-            rt = both([ts(h, 8 * l + i) for h in range(2) for i in ins] + [tp(l % 3, h, i) for h in range(2) for i in ins])
-            wt = both([(tp(bank, h, x) if side else ts(h, x)) for h in range(2) for x in outs])
-            V(2 * VB * n, lambda v, T, l=l, op=op, side=side, bank=bank, i0=i0, si=si, p0=p0, so=so, n=n: v.tensor_tensor(
-                (T[SP[bank]] if side else T.sv)[:, H, sl(p0, so, n), :], T.sv[:, H, sl(8 * l + i0, si, n), :], T[SP[l % 3]][:, H, sl(i0, si, n), :],
-                ALU.max if op else ALU.min), rt, wt)
-        V(LW, lambda v, T: v.tensor_tensor(T.sv[:, h0, 88:96, :], T.sv[:, h0, 80:88, :], T.sp1[:, h1, :, :], ALU.min),
-          both([ts(0, 80 + i) for i in range(8)] + [tp(1, 1, i) for i in range(8)]), both([ts(0, 88 + i) for i in range(8)]))
-        V(LW, lambda v, T: v.tensor_tensor(T.sp2[:, h0, ::-1, :], T.sv[:, h1, 80:88, :], T.sp1[:, h0, :, :], ALU.min),
-          both([ts(1, 80 + i) for i in range(8)] + [tp(1, 0, i) for i in range(8)]), both([tp(2, 0, i) for i in range(8)]))
+        def step(op, s0, ss, p0, ps, n, mem, o0, os_, hs=(0, 1), hp=(0, 1), ho=(0, 1)):
+            def at(h): return H if len(h) == 2 else 2 * p + h[0]
+            rt = both([ts(h, s0 + ss * j) for h in hs for j in range(n)] + [tp(h, p0 + ps * j) for h in hp for j in range(n)])
+            wt = both([(tp if mem else ts)(h, o0 + os_ * j) for h in ho for j in range(n)])
+            V(16 * n * len(hs), lambda v, T: v.tensor_tensor((T.sp if mem else T.sv)[:, at(ho), sl(o0, os_, n), :], T.sv[:, at(hs), sl(s0, ss, n), :],
+                                                             T.sp[:, at(hp), sl(p0, ps, n), :], ALU.max if op else ALU.min), rt, wt)
+        for x in NET:
+            step(*x)
+        step(0, 43, 1, 7, 2, 4, 1, 22, -4, [0], [1], [0]); step(0, 47, 1, 15, 2, 4, 0, 15, -2, [0], [1], [0])
+        step(0, 43, 1, 7, 2, 4, 0, 8, 2, [1], [0], [0]); step(0, 47, 1, 15, 2, 4, 1, 8, 4, [1], [0], [0])
+        SB, PB, PS = (8, 16, 24, 8), (8, 0, 8, 16), (2, 1, 1)
         for m in range(3):
-            sb, pb, nb = 88 + 8 * m, (2 + m) % 3, m % 3
             for side in range(2):
                 for op in range(2):
-                    rt = both([ts(0, sb + 4 * side + j) for j in range(4)] + [tp(pb, 0, 4 * side + j) for j in range(4)])
-                    wt = both([(tp(nb, 0, op + 2 * j) if side else ts(0, sb + 8 + op + 2 * j)) for j in range(4)])
-                    V(4 * VB, lambda v, T, sb=sb, pb=pb, nb=nb, side=side, op=op: v.tensor_tensor(
-                        T[SP[nb]][:, h0, op:8:2, :] if side else T.sv[:, h0, sb + 8 + op:sb + 16:2, :],
-                        T.sv[:, h0, sb + 4 * side:sb + 4 * side + 4, :], T[SP[pb]][:, h0, 4 * side:4 * side + 4, :],
-                        ALU.min if op else ALU.max), rt, wt)
+                    step(1 - op, SB[m] + 4 * side, 1, PB[m] + 4 * side * PS[m], PS[m], 4, side, (PB if side else SB)[m + 1] + op, 2, [0], [0], [0])
         for op in range(2):
-            V(LW, lambda v, T, op=op: v.tensor_tensor(T.kk[:, p, op:16:2, :], T.sv[:, h0, 112:120, :], T.sp2[:, h0, :, :], ALU.min if op else ALU.max),
-              both([ts(0, 112 + j) for j in range(8)] + [tp(2, 0, j) for j in range(8)]), [("kk", p, op)])
-        rw = both([tp(0, 1, j) for j in range(8)]); kt = [("kk", p, 0), ("kk", p, 1)]
-        V(LW, lambda v, T: v.tensor_scalar(T.sp0[:, h1, :, :], T.kk[:, p, :, 0:IW], MAGIC, -MAGIC, ALU.add, ALU.add), kt, rw)
+            V(128, lambda v, T, op=op: v.tensor_tensor(T.kk[:, p, op:16:2, :], T.sv[:, h0, 8:16, :], T.sp[:, h0, 16:24, :], ALU.min if op else ALU.max),
+              both([ts(0, 8 + j) for j in range(8)] + [tp(0, 16 + j) for j in range(8)]), [("kk", p, op)])
+        rw = both([tp(1, 8 + j) for j in range(8)]); kt = [("kk", p, 0), ("kk", p, 1)]
+        V(128, lambda v, T: v.tensor_scalar(T.sp[:, h1, 8:16, :], T.kk[:, p, :, 0:8], MAGIC, -MAGIC, ALU.add, ALU.add), kt, rw)
         for du in range(2):
-            V(LW, lambda v, T, du=du: v.tensor_tensor(T.hl[:, tp_ + NP, 0, du, :], T.kk[:, p, :, du * IW:(du + 1) * IW], T.sp0[:, h1, :, :], ALU.subtract),
+            V(128, lambda v, T, du=du: v.tensor_tensor(T.hl[:, tp_ + 2, 0, du, :], T.kk[:, p, :, du * 8:(du + 1) * 8], T.sp[:, h1, 8:16, :], ALU.subtract),
               kt + rw, [("hl", t + 1, p, 0, du)])
 
-    def nk(t, p, k): return [("ne", t % 3, p, k, j) for j in range(4 // NP)]
-    def bq(t, p): return [("b", t % 2, i) for i in range(p * 4 // NP, (p + 1) * 4 // NP)]
+    def nk(t, ps, k0, n=1): return [("ne", t % 3, p, k) for p in ps for k in range(k0, k0 + n)]
+    REG = {"bb": (lambda T, n: T.bb[:, 0:n], ["bb"]), "xb": (lambda T, n: T.xb[:, 0:n], ["xb"]),
+           "key0": (lambda T, n: T.key0[:, 0, 0:n], [("key0", 0)]), "key1": (lambda T, n: T.key1[:, 0, 0:n], [("key1", 0)])}
+    def lanes(t):
+        return {1: [(["bb", "xb"], [0, 1])], 2: [(["bb"], [0]), (["xb"], [1])], 3: [(["bb", "key0"], [0]), (["xb", "key1"], [1])]}[cfg["parts"][t]]
+    IDF = [("idf", s) for s in range(2)]
+    last = []
 
-    def bias(t, p):
-        w0 = (t + 1) * 256
-        ne = "ne%d" % (t % 3)
-        NW = [("nt", q, i) for q in range(t + 1, t + 17) for i in range(NP)] + [("ul", t + 1, p, 0)]
-        nh = cfg["halves"][t][p]; wd = LW // nh; per = 4 // NP // nh
-        eg = cfg["egat"][t][p]; ng = len(eg); ck_ = 16 // ng; en = ck_ * LW
-        for c in range(ng):
-            o0 = ucol(t + 1, p, 0) + c * en // 16
-            wt = [x for k in range(ck_ * c, ck_ * (c + 1)) for x in nk(t, p, k)]
-            def win(T, o0=o0): return T.nt[:, w0:w0 + 4096].indirect(T.ul[:, o0:o0 + en // 16])
-            if eg[c] == "S":
-                S(en, lambda a, T, c=c, win=win: a.activation(T[ne][:, p, c * en:(c + 1) * en], win(T), ACT.Copy), NW, wt, gat=True)
+    def errors(t, p):
+        w0 = (t + 1) * 256; ne = "ne%d" % (t % 3)
+        NW = [x for q in range(t + 1, t + 17) for x in NT(q)] + [("ul", t + 1, p, 0)]
+        for who, k0, n in pieces(cfg["egat"][2 * t + p]):
+            o0 = ucol(t + 1, p, 0) + k0 * 8
+            def win(T, o0=o0, n=n): return T.nt[:, w0:w0 + 4096].indirect(T.ul[:, o0:o0 + n * 8])
+            if who == "S":
+                S(n * 128, lambda a, T, k0=k0, n=n, win=win: a.activation(T[ne][:, p, hb(k0, n)], win(T), ACT.Copy), NW, nk(t, [p], k0, n), gat=True)
             else:
-                V(en, lambda v, T, c=c, win=win: v.tensor_copy(T[ne][:, p, c * en:(c + 1) * en], win(T)), NW, wt, gat=True)
-        yield
-        b0 = (t % 2) * 256 + p * LW
-        if cfg["chain"][t][p] == "Q":
-            fp = "fp%d" % p; a = p * LW; at = [("aa", 0, x[2]) for x in bq(t, p)]; bo = ("bs", t % 2, p, 0)
-            for k in range(16):
-                src = (lambda T: T[fp][:, 0:LW]) if k else (lambda T: T[ne][:, p, 0:LW])
-                if k:
-                    PE([(4 * LW, lambda T, k=k: (T[fp][:, 0:LW], T.idf[:], T[ne][:, p, k * LW:(k + 1) * LW]))], nk(t, p, k) + ["idf"], [fp], [fp], True, False)
-                    PE([(4 * LW, lambda T: (T[fp][:, 0:LW], T.idf[:], T.cs[:, a:a + LW]))], [("cs", p), "idf"], [fp], [fp], False, True)
-                S(LW, lambda s, T, src=src, k=k: s.activation(T.aa[:, 0, a:a + LW], src(T), ACT.Relu, bias=T.mb[:, k:k + 1], scale=-0.5),
-                  ([fp] if k else nk(t, p, 0)) + ["mb"], at, [fp] if k else [])
-                S(LW, lambda s, T: s.activation(T[fp][:, LW:2 * LW], T.aa[:, 0, a:a + LW], ACT.Relu, bias=T.mm[:, 0:1], scale=-1.0), at + ["mm"], [(fp, 1)] + ([] if k else [fp]), [fp])
-                if k:
-                    V(LW, lambda v, T, k=k: v.tensor_tensor(T.cs[:, a:a + LW] if k < 15 else T.bs[:, (t % 2) * NP + p, 0:LW], T.cs[:, a:a + LW], T[fp][:, LW:2 * LW], ALU.subtract),
-                      [(fp, 1), ("cs", p)], [("cs", p)] if k < 15 else [bo, fp], [fp])
-                else:
-                    V(LW, lambda v, T: v.tensor_scalar(T.cs[:, a:a + LW], T[fp][:, LW:2 * LW], -1.0, T.mb[:, 16:17], ALU.mult, ALU.add), [(fp, 1), "mb"], [("cs", p)], [fp])
-            e0 = (16 + t) * 256 + p * LW; r0 = t * 256 + p * LW
-            V(2 * LW, lambda v, T: v.tensor_tensor(T.nt[:, e0:e0 + LW], T.bs[:, (t % 2) * NP + p, 0:LW], T.ers[:, r0:r0 + LW], ALU.subtract), [bo, "ers"], [("nt", 16 + t, p)])
-            return
+                V(n * 128, lambda v, T, k0=k0, n=n, win=win: v.tensor_copy(T[ne][:, p, hb(k0, n)], win(T)), NW, nk(t, [p], k0, n), gat=True)
+
+    def bias(t, banks, ps):
+        ne = "ne%d" % (t % 3); a, wd = ps[0] * 128, len(ps) * 128; P_ = slice(ps[0], ps[-1] + 1)
+        mode, off = [], [0]
+        for k, c in enumerate(cfg["pre"][t]):
+            if off[k] and c == "P": c = "Q"
+            elif k == 15 and not off[k]: c = "P"
+            mode.append(c); off.append(0 if c == "P" else 1 - off[k])
+        def cs(T): return T.cs[:, a:a + wd]
+        def tt(T): return T.tt[:, a:a + wd]
+        def done(T): return T.bs[:, t % 2, P_, 0:128]
+        tk = [("tt", p) for p in ps]; bk = [("bs", t % 2, 0, p) for p in ps]
+        bank = banks[0]; old = None
         for k in range(16):
-            for j in range(nh):
-                a = p * LW + j * wd; x0 = k * LW + j * wd; bc = b0 + j * wd
-                et = nk(t, p, k)[j * per:(j + 1) * per]; bt = bq(t, p)[j * per:(j + 1) * per]
-                tt_, ct, at = [[(nm, k % 2, x[2]) for x in bt] for nm in ("tt", "cc", "aa")]
-                src = (lambda T, k=k, a=a: T.tt[:, k % 2, a:a + wd]) if k else (lambda T, x0=x0: T[ne][:, p, x0:x0 + wd])
-                if k:
-                    V(wd, lambda v, T, src=src, x0=x0, bc=bc: v.tensor_tensor(src(T), T[ne][:, p, x0:x0 + wd], T.bb[:, bc:bc + wd], ALU.add), et + bt, tt_, ["bb"])
-                S(wd, lambda s, T, src=src, k=k, a=a: s.activation(T.aa[:, k % 2, a:a + wd], src(T), ACT.Relu, bias=T.mb[:, k:k + 1], scale=-0.5),
-                  (tt_ if k else et) + ["mb"], at)
-                S(wd, lambda s, T, k=k, a=a: s.activation(T.cc[:, k % 2, a:a + wd], T.aa[:, k % 2, a:a + wd], ACT.Relu, bias=T.mm[:, 0:1], scale=-1.0),
-                  at + ["mm"], ct)
-                if k:
-                    V(wd, lambda v, T, k=k, a=a, bc=bc: v.tensor_tensor(T.bb[:, bc:bc + wd], T.bb[:, bc:bc + wd], T.cc[:, k % 2, a:a + wd], ALU.subtract), ct + bt, bt, ["bb"])
+            if mode[k] != "O": bank = banks[k % len(banks)]
+            bt = REG[bank][1]; o = off[k]; et = nk(t, ps, k)
+            def e(T, k=k): return T[ne][:, P_, hb(k)]
+            def x(T, bank=bank): return REG[bank][0](T, wd)
+            new = (done, bk, []) if k == 15 else (x, bt, [bank]) if mode[k + 1] == "O" else (cs, [("cs", p) for p in ps], [])
+            def relus(src, half, last):
+                S(wd, lambda s, T, o=o: s.activation(tt(T), src[0](T), ACT.Relu, bias=T.mm[:, 2 * o:2 * o + 1], scale=(1.0 - 2 * o) * half), src[1] + MM, tk, src[2])
+                S(wd, lambda s, T: s.activation(last[0](T), tt(T), ACT.Relu, bias=T.mm[:, 3:4], scale=-1.0), tk + MM, last[1], last[2])
+            if k == 0 and mode[0] == "P":
+                V(wd, lambda v, T, e=e: v.tensor_scalar(tt(T), e(T), T.mm[:, 3:4], T.mm[:, 4:5], ALU.min, ALU.max), et + MM, tk)
+                V(wd, lambda v, T, new=new: v.tensor_scalar(new[0](T), tt(T), -0.5, None, ALU.mult), tk, new[1], new[2])
+            elif k == 0:
+                relus((e, et, []), 0.5, new)
+            else:
+                if mode[k] == "O":
+                    V(wd, lambda v, T, e=e, x=x: v.tensor_tensor(tt(T), e(T), x(T), ALU.add), et + bt, tk, [bank])
+                    relus((tt, tk, []), 0.5, (tt, tk, []))
+                    step = (tt, tk)
                 else:
-                    V(wd, lambda v, T, a=a, bc=bc: v.tensor_scalar(T.bb[:, bc:bc + wd], T.cc[:, 0, a:a + wd], -1.0, T.mb[:, 16:17], ALU.mult, ALU.add),
-                      ct + ["mb"], bt, ["bb"])
+                    grp = ("b", t, k, a); step = (x, bt)
+                    PE([(4 * wd, lambda T, e=e, x=x: (x(T), T.idf[:, 0, :], e(T)))], et + IDF, bt, [bank], True, grp=grp)
+                    PE([(4 * wd, lambda T, x=x: (x(T), T.idf[:, 0, :], cs(T)))], old[1] + IDF, bt, [bank], False, grp=grp)
+                    if mode[k] == "P":
+                        V(wd, lambda v, T, x=x: v.tensor_scalar(x(T), x(T), T.mm[:, 0:1], T.mm[:, 1:2], ALU.min, ALU.max), bt + MM, bt, [bank])
+                    else:
+                        relus((x, bt, [bank]), 1.0, (x, bt, [bank]))
+                V(wd, lambda v, T, old=old, new=new, step=step, op=ALU.add if off[k + 1] else ALU.subtract: v.tensor_tensor(new[0](T), old[0](T), step[0](T), op),
+                  old[1] + step[1], new[1], [bank])
+            old = new
         if t < 3:
-            e0 = (16 + t) * 256 + p * LW; r0 = t * 256 + p * LW
-            V(LW, lambda v, T: v.tensor_tensor(T.nt[:, e0:e0 + LW], T.bb[:, b0:b0 + LW], T.ers[:, r0:r0 + LW], ALU.subtract),
-              bq(t, p) + ["ers"], [("nt", 16 + t, p)], ["bb"])
-        S(LW, lambda s, T: s.activation(T.bs[:, (t % 2) * NP + p, 0:LW], T.bb[:, b0:b0 + LW], ACT.Copy), bq(t, p), [("bs", t % 2, p, 0)], ["bb"])
+            e0 = (16 + t) * 256 + a; r0 = t * 256 + a
+            PE([(wd, lambda T: (x(T), T.idb[:, 3, :], T.ers[:, r0:r0 + wd])), (4 * wd, lambda T: (x(T), T.idf[:, 1, :], done(T)))],
+               bk + IDF + ["ers", ("idb", 3)], bt, [bank])
+            S(wd, lambda s, T: s.activation(T.nt[:, e0:e0 + wd], x(T), ACT.Copy), bt, [NT(16 + t)[p] for p in ps], [bank])
 
     def spread(t):
-        ne = "ne%d" % (t % 3); D = slice((t % 2) * NP, (t % 2 + 1) * NP)
-        BS = [("bs", t % 2, p, 0) for p in range(NP)]
-        tag[1] = NP - 1
-        Y(1 << 17, lambda e, T: e.dma_start(T.yb[:, blk(t)], T.bs[:, D, 0:LW]), BS, [("yb", t)])
-        def ck(p, k0, k1): return [x for k in range(k0, k1) for x in nk(t, p, k)]
-        def allp(k0, k1): return [x for p in range(NP) for x in ck(p, k0, k1)]
+        ne = "ne%d" % (t % 3); D = t % 2; B = [0, 1]
+        BS = [("bs", t % 2, 0, p) for p in B]
+        tag[1] = 1
+        Y(1 << 17, lambda e, T: e.dma_start(T.yb[:, blk(t)], T.bs[:, D, :, 0:128]), BS, [("yb", t)], 2)
+        def fold(ps, k0, n, first):
+            def xs(T): return T[ne][:, ps[0]:ps[-1] + 1, hb(k0, n)]
+            x = nk(t, ps, k0, n); m = n * 128 * len(ps)
+            S(m, lambda s, T: s.activation(xs(T), xs(T), ACT.Abs), x, x)
+            S(m + (1600 if first else 0), lambda s, T: s.activation(xs(T), xs(T), ACT.Exp, scale=-1.0), x, x)
         if cfg["sub"][t] == "D":
-            for i in range(1, 4):
-                Y(1 << 17, lambda e, T, i=i: e.dma_start(T.bs[:, D, i * LW:(i + 1) * LW], T.bs[:, D, 0:LW]), BS, [("bs", t % 2, "r", i)])
-            for c in range(4):
-                GD(1 << 20, lambda g, T, c=c: g.dma_start(T[ne][:, :, c * FW:(c + 1) * FW], T.bs[:, D, :], accum_op=ALU.add),
-                   BS + [("bs", t % 2, "r", i) for i in range(1, 4)] + allp(4 * c, 4 * c + 4), allp(4 * c, 4 * c + 4))
-        for p in range(NP):
-            tag[1] = p
-            b0 = (t % 2) * 256 + p * LW; fp = "fp%d" % p
-            nc = 4 if cfg["sub"][t] == "V" else 4 // NP
-            kc = 16 // nc; n = kc * LW
-            for c in range(nc):
-                if cfg["sub"][t] == "V":
-                    for k in range(kc * c, kc * (c + 1)):
-                        V(LW, lambda v, T, p=p, k=k, b0=b0: v.tensor_tensor(T[ne][:, p, k * LW:(k + 1) * LW], T[ne][:, p, k * LW:(k + 1) * LW], T.bb[:, b0:b0 + LW], ALU.add),
-                          nk(t, p, k) + bq(t, p), nk(t, p, k), ["bb"])
-                def xs(T, p=p, c=c, n=n): return T[ne][:, p, c * n:(c + 1) * n]
-                x = ck(p, kc * c, kc * (c + 1))
-                S(n, lambda s, T, xs=xs: s.activation(xs(T), xs(T), ACT.Abs), x, x)
-                S(n + (1600 if t + p + c == 0 else 0), lambda s, T, xs=xs: s.activation(xs(T), xs(T), ACT.Exp, scale=-1.0), x, x)
-                if cfg["sum"][t] == "P":
-                    PE([(4 * LW, lambda T, k=k, p=p, fp=fp: (T[fp][:, 0:LW], T.idf[:], T[ne][:, p, k * LW:(k + 1) * LW])) for k in range(kc * c, kc * (c + 1))],
-                       x + ["idf", fp], [fp], [fp], c == 0, c == nc - 1)
-            if cfg["sum"][t] == "P":
-                V(LW, lambda v, T, p=p, fp=fp: v.tensor_copy(T.so[:, p * LW:(p + 1) * LW], T[fp][:, 0:LW]), [fp], [("so", p)], [fp])
-                Y(1 << 16, lambda e, T, p=p: e.dma_start(T.ys[:, t * 256 + p * LW:t * 256 + (p + 1) * LW], T.so[:, p * LW:(p + 1) * LW]), [("so", p)], [("ys", t, p)])
-        if cfg["sum"][t] == "D":
+            nr = cfg["rep"]
+            for i in (1, 2, 4)[:nr // 3 + 1]:
+                BS = BS + [("bs", D, i)]
+                Y(i << 17, lambda e, T, i=i: e.dma_start(T.bs[:, D, :, hb(i, i)], T.bs[:, D, :, hb(0, i)]), BS[:-1], BS[-1:], 2)
+            for c in range(0, 16, nr):
+                GD(nr << 18, lambda g, T, c=c: g.dma_start(T[ne][:, :, hb(c, nr)], T.bs[:, D, :, hb(0, nr)], accum_op=ALU.add), BS + nk(t, B, c, nr), nk(t, B, c, nr), 2)
+            for _, k0, n in pieces(cfg["exp"][t]):
+                fold(B, k0, n, t + k0 == 0)
+        else:
+            for p in B:
+                tag[1] = p
+                bank = ("bb", "xb")[p]
+                for i in range(4):
+                    PE([(512, lambda T, i=i, p=p, bank=bank: (T[bank][:, hb(i)], T.idf[:, 1, :], T.bs[:, D, p, 0:128]))], [BS[p]] + IDF, [bank], [bank])
+                for c in range(0, 16, 4):
+                    V(512, lambda v, T, c=c, p=p, bank=bank: v.tensor_tensor(T[ne][:, p, hb(c, 4)], T[ne][:, p, hb(c, 4)], T[bank][:], ALU.add),
+                      nk(t, [p], c, 4) + [bank], nk(t, [p], c, 4), [bank])
+                for _, k0, n in pieces(cfg["exp"][t]):
+                    fold([p], k0, n, t + k0 + p == 0)
+        if cfg["sum"][t] == "P":
+            for p in B:
+                tag[1] = p
+                key = "key%d" % p
+                for _, k0, n in pieces(cfg["exp"][t]):
+                    PE([(512, lambda T, k=k, p=p, key=key: (T[key][:, 2, :], T.idf[:, 1, :], T[ne][:, p, hb(k)])) for k in range(k0, k0 + n)],
+                       nk(t, [p], k0, n) + IDF, [(key, 0)], [key], k0 == 0, k0 + n == 16)
+                V(128, lambda v, T, p=p, key=key: v.tensor_copy(T.so[:, hb(p)], T[key][:, 2, :]), [(key, 0)], [("so", p)], [key])
+                Y(1 << 16, lambda e, T, p=p: e.dma_start(T.ys[:, hb(2 * t + p)], T.so[:, hb(p)]), [("so", p)], [("ys", t, p)])
+        elif cfg["sum"][t] == "A":
+            def later():
+                tag[:] = ["e%d" % t, 1]; A = [("aa", 0, 0), ("aa", 0, 1)]
+                for _, k0, n in pieces(cfg["exp"][t]):
+                    PE([(1024, lambda T, k=k: (T.aa[:, 0:256], T.idf[:, 1, :], T[ne][:, :, hb(k)])) for k in range(k0, k0 + n)],
+                       nk(t, B, k0, n) + IDF + [("ul", 4, 1, 0)], A, ["aa"], k0 == 0, k0 + n == 16)
+                S(256, lambda s, T: s.activation(T.s2[:], T.aa[:, 0:256], ACT.Copy), A, ["s2"], ["aa"])
+                Y(1 << 17, lambda e, T: e.dma_start(T.ys[:, blk(t)], T.s2[:]), ["s2"], [("ys", t)])
+            last.append(later)
+        elif cfg["sum"][t] == "F":
+            add("G", "f", (1 << 21, 32), lambda g, T: (T.so[:], 1, [(T.so[:, hb(p)], [T[ne][:, p, hb(k)] for k in range(16)]) for p in B]),
+                nk(t, B, 0, 16), [("so", 0), ("so", 1)])
+            ops[-1]["slot"] = 16
+            Y(1 << 17, lambda e, T: e.dma_start(T.ys[:, blk(t)], T.so[:]), [("so", 0), ("so", 1)], [("ys", t)])
+        else:
             for m in (8, 4, 2, 1):
-                GD(m << 18, lambda g, T, n=m * LW: g.dma_start(T[ne][:, :, 0:n], T[ne][:, :, n:2 * n], accum_op=ALU.add), allp(0, 2 * m), allp(0, m))
-            Y(1 << 17, lambda e, T: e.dma_start(T.ys[:, blk(t)], T[ne][:, :, 0:LW]), allp(0, 1), [("ys", t)])
+                GD(m << 18, lambda g, T, m=m: g.dma_start(T[ne][:, :, hb(0, m)], T[ne][:, :, hb(m, m)], accum_op=ALU.add), nk(t, B, 0, 2 * m), nk(t, B, 0, m), 2)
+            Y(1 << 17, lambda e, T: e.dma_start(T.ys[:, blk(t)], T[ne][:, :, hb(0)]), nk(t, B, 0), [("ys", t)], 2)
 
-    tag[0] = "init"
-    for p in range(NP):
-        tag[1] = p
+    for p in range(2):
+        tag[:] = ["init", p]
         own_lists(0, p)
     for t in range(4):
-        for p in range(NP):
-            tag[0], tag[1] = "s%d" % t, p
+        for p in range(2):
+            tag[:] = ["s%d" % t, p]
             select(t, p)
             own_lists(t + 1, p)
-        steps = [bias(t, p) for p in range(NP)]
-        for _ in range(2):
-            for p in range(NP):
-                tag[0], tag[1] = "b%d" % t, p
-                next(steps[p], None)
+        for p in range(2):
+            tag[:] = ["g%d" % t, p]
+            errors(t, p)
+        for banks, ps in lanes(t):
+            tag[:] = ["b%d" % t, ps[-1]]
+            bias(t, banks, ps)
         tag[0] = "e%d" % t
         spread(t)
+    for fn in last:
+        fn()
     return ops
 
 
@@ -421,6 +413,7 @@ def link(ops):
         d = set()
         for x in o["r"]:
             if x in lastw: d.add(lastw[x])
+        o["raw"] = set(d)
         for x in o["w"]:
             if x in lastw: d.add(lastw[x])
             d.update(readers.get(x, ()))
@@ -429,20 +422,26 @@ def link(ops):
         for x in o["w"]:
             lastw[x] = i; readers[x] = []
         o["dep"] = d
+        o["free"] = {j for j in d if o["grp"] and o["grp"] == ops[j]["grp"]}
+
+
+def moved(o, C):
+    return o["n"][0] / C["bw"] + 8 * o["n"][1] * C["row"]
 
 
 def times(o, C):
     k, q, n = o["kind"], o["q"], o["n"]
+    if k == "f": return C["gi"], C["fold"] + moved(o, C)
     if k == "r": return C["gi"], C["rem"]
     if k == "d":
         h = C["gi"] if q == "G" else C["yi"]
-        return h, h + C["dma"] + n / C["bw"]
+        return h, h + C["dma"] + moved(o, C)
     if q == "P":
         t = sum(max(64, x) * C["pe"] + C["pefix"] for x in n)
     elif q == "G":
         t = n * C["cy"]
     else:
-        t = (n * C["G"] + 40 if o["gat"] else max(n, 64)) * C["cy"] + C["fix"]
+        t = (n * C["G"] if o["gat"] else max(n, 64)) * C["cy"] + C["fix" + q]
     return t, t
 
 
@@ -450,65 +449,98 @@ def lat(a, b, C):
     return C["same"] if (a["q"] == b["q"] and a["kind"] == "c") else C["cross"]
 
 
-def plan(ops, C, slack, rounds=0):
+def plan(ops, C, cfg):
+    C = dict(C, **cfg["wary"])
     n = len(ops); succ = [[] for _ in ops]
     for i, o in enumerate(ops):
         for d in o["dep"]: succ[d].append(i)
     tm = [times(o, C) for o in ops]
     pr = [0.0] * n
     for i in range(n - 1, -1, -1):
-        pr[i] = tm[i][1] + max([pr[j] + lat(ops[i], ops[j], C) for j in succ[i]], default=0.0)
-    pred = [list(o["dep"]) for o in ops]
-
-    def sweep(pr, back):
-        a, z = (succ, pred) if back else (pred, succ)
-        left = [len(x) for x in a]; ready = [i for i in range(n) if not left[i]]
-        free = {q: 0.0 for q in "VSPGY"}; fin = [0.0] * n; st = [0.0] * n; bank = {}; order = []; extra = {}
-        rt = [tm[i][1] - tm[i][0] if back else 0.0 for i in range(n)]
-        while ready:
-            best = []
-            for i in ready:
-                o = ops[i]; s = max(rt[i], free[o["q"]])
-                for b in o["banks"]:
+        o = ops[i]; w = o["w"][0][0] if o["w"] else ""; due = []
+        if o["tag"][0] in "sbe" and (w in ("hl", "nt", "ys", "yb") or not succ[i]):
+            due = [-cfg["half"] * (2 * int(o["tag"][1]) + o["part"]) - cfg["due"][o["tag"]]]
+        pr[i] = (tm[i][0] * cfg["stretch"].get(o["tag"][0] + o["q"], 1.0) + tm[i][1] - tm[i][0]
+                 + max([pr[j] + lat(o, ops[j], C) for j in succ[i]] + due, default=-1e9))
+    B = cfg["bonus"]
+    pr = [pr[i] + B.get(o["tag"], 0.0) + B.get(o["tag"][0] + o["q"], 0.0) - cfg["off"] * o["part"] for i, o in enumerate(ops)]
+    left = [len(o["dep"]) for o in ops]; ready = {q: [] for q in "VSPGY"}
+    for i in range(n):
+        if not left[i]: ready[ops[i]["q"]].append(i)
+    free = dict.fromkeys(ready, 0.0); fin = [0.0] * n; rt = [0.0] * n; bank = {}; order = []; wire = 0.0; pick = dict.fromkeys(ready)
+    stale = set(ready); cross = C["cross"]
+    while len(order) < n:
+        for q0 in stale:
+            best = None; fence = 1e18; tol = cfg["tol"][q0]; f0 = free[q0]
+            for i in sorted(ready[q0], key=lambda x: -pr[x]):
+                s = rt[i] if rt[i] > f0 else f0
+                for b in ops[i]["banks"]:
                     for q, j in bank.get(b, {}).items():
-                        if q != o["q"]: s = max(s, fin[j] + C["cross"])
-                best.append((s, i))
-            m = min(best)
-            q0 = ops[m[1]]["q"]
-            s, i = max((x for x in best if ops[x[1]]["q"] == q0 and x[0] <= m[0] + slack), key=lambda x: pr[x[1]])
-            o = ops[i]
-            for b in o["banks"]:
-                extra.setdefault(i, set()).update(j for q, j in bank.get(b, {}).items() if q != o["q"])
-                bank.setdefault(b, {})[o["q"]] = i
-            free[o["q"]] = s + tm[i][0]; fin[i] = s + tm[i][0 if back else 1]; st[i] = s
-            order.append(i); ready.remove(i)
-            for j in z[i]:
-                rt[j] = max(rt[j], fin[i] + lat(o, ops[j], C) + (tm[j][1] - tm[j][0] if back else 0.0)); left[j] -= 1
-                if not left[j]: ready.append(j)
-        assert len(order) == n
-        return max(fin), order, st, fin, extra
-
-    best = cur = sweep([pr[i] + ops[i]["bonus"] for i in range(n)], False)
-    for _ in range(rounds):
-        cur = sweep(sweep(cur[3], True)[3], False)
-        if cur[0] < best[0]: best = cur
+                        if q != q0 and fin[j] + cross > s: s = fin[j] + cross
+                if (best is None or s < best[0]) and s + tm[i][0] - tol <= fence: best = (s, i)
+                if s < fence: fence = s
+            pick[q0] = best
+        s, i = min(x for x in pick.values() if x)
+        o = ops[i]; q0 = o["q"]; o["all"] = set(o["dep"]); o["start"] = s; stale = {q0}
+        for b in o["banks"]:
+            o["all"].update(j for q, j in bank.get(b, {}).items() if q != q0)
+            bank.setdefault(b, {})[q0] = i; stale.update("VSP")
+        free[q0] = s + tm[i][0]; fin[i] = s + tm[i][1]
+        if o["kind"] in "df":
+            wire = fin[i] = max(fin[i], wire + moved(o, C))
+        order.append(i); ready[q0].remove(i)
+        for j in succ[i]:
+            rt[j] = max(rt[j], fin[i] + (0.0 if i in ops[j]["free"] else lat(o, ops[j], C))); left[j] -= 1
+            if not left[j]: ready[ops[j]["q"]].append(j); stale.add(ops[j]["q"])
+    last = {ops[i]["grp"]: i for i in order if ops[i]["grp"]}
     for i, o in enumerate(ops):
-        o["start"] = best[2][i]; o["dep"] = o["dep"] | best[4].get(i, set())
-    return best[1], best[0]
+        o["last"][0] = last.get(o["grp"]) == i
+    return order, max(fin)
 
 
-CFG.update({'path': [['VDVS', 'VDDD'], ['DDDR', 'DDDD'], ['DVDD', 'DDDD'], ['SSDD', 'DDDD']], 'sub': ['D', 'D', 'V', 'V'], 'sum': ['D', 'D', 'D', 'P'], 'halves': [[1, 1], [1, 1], [1, 1], [2, 2]], 'chain': ['SS', 'SS', 'SS', 'SS'], 'egat': [['SSSS', 'SS'], ['SS', 'SSVV'], ['VS', 'SSSS'], ['SVSS', 'VS']], 'bonus': {'late': -39000, 'b1': 4000, 'e0': -5000, 'b3': 17000, 's0': 59000, 's3': -10000, 's2': 0, 'b2': 10000, 'e3': -67000, 'b0': 20000, 'e1': -8000, 's1': 7000, 'e2': -2000}, 'ptv': 6, 'slack': 0, 'off': 2000})
-SCRATCH = scratch(CFG["np"])
+COST = {"cy": 0.83, "G": 1.56, "fixV": 50.0, "fixS": 65.0, "pe": 0.42, "pefix": 5.0, "same": 140.0, "cross": 140.0,
+        "dma": 2000.0, "bw": 550.0, "row": 25.0, "gi": 1000.0, "yi": 100.0, "rem": 3800.0, "fold": 7500.0}
+CFG = {
+    "path": ["R2D2R2D2", "D2D2D2D2"] + ["D2D2D2D2"] * 6,
+    "egat": ["S8S8"] * 6 + ["S4S4S8", "S2V2S4V4S4"],
+    "pre": ["PPQQPPQQPPQQPPQP"] * 3 + ["P" * 16],
+    "parts": [1, 1, 1, 3], "sub": "DDDV", "sum": "DDDP", "exp": ["S8S8", "S8S8", "S8S8", "S4S4S4S4"],
+    "rounds": 0, "stretch": {}, "rep": 8, "ptv": 10, "slack": 0.0, "off": 10000.0, "bonus": {"late": -20000.0, "bV": 50000.0, "bS": 50000.0},
+}
+CFG = {'path': ['R2D2R1R1A2', 'D2D1D1D2D2', 'D2D2D2D2', 'D2A2A2A2', 'D2D2D2D1D1', 'V2D2D2D2', 'D2D2D2D2', 'D2D2D2D2'], 'egat': ['S8S4S4', 'S2S3S1S5S5', 'S8S5S3', 'V2S4S5S5', 'S8S3S4S1', 'S2S4S5S5', 'S8S8', 'S2S4S4S6'], 'pre': ['PQPPQQPPPPPPPPPP', 'PPPPPPPPPPPPPPPP', 'PPPPPPPPPPPQQQPP', 'PPPPPPPPPPPPPQQQ'], 'parts': [1, 1, 1, 3], 'sub': 'DDDV', 'sum': 'FFFP', 'exp': ['S2S2S4S2S1S1S1S1S2', 'S2S2S2S2S4S2S2', 'S2S1S1S2S2S2S2S2S2', 'S4S4S4S4'], 'rounds': 0, 'mix': 1, 'stretch': {'sV': 1.42, 'eY': 1.12, 'sG': 0.88, 'vV': 1.09, 'bV': 1.31, 'gV': 0.71, 'sP': 0.81, 'iS': 0.88, 'lS': 1.0, 'sS': 1.25, 'iV': 1.14, 'pG': 0.99, 'vP': 0.92, 'eG': 1.12, 'eV': 0.64, 'eS': 0.88, 'pV': 1.1, 'bP': 1.04, 'pS': 1.05, 'lY': 0.9, 'pP': 0.8, 'gS': 1.19, 'eP': 1.25, 'bS': 1.05}, 'rep': 4, 'ptv': 6, 'slack': 0, 'off': 1000, 'bonus': {'bV': 110000.0, 'bP': 100000.0, 'bS': 97000.0, 'sG': 100000.0, 'pG': 49000.0, 'late': -11300, 'sP': 98300.0, 'uV': 200000.0, 'uP': 200000.0, 'pS': 50000.0, 'sS': 41000.0, 'gS': 3000, 'g0': 11300, 'v2': -4300, 'lY': 10700, 'g1': 20000, 's2': -3000, 'b2': -10000, 'pP': -1000, 's0': -300, 'vP': 10000, 'b0': 7000, 'eV': 10000, 'p3': 300, 'sV': -1000, 'eS': -3000, 'e1': 12000, 'p0': -19400, 'b1': -9700, 'e3': 3700, 's3': 10000, 'g3': 10000, 'eG': -10000, 'lS': -6000, 'p1': 4000, 'gV': -10000, 'iV': 600, 'b3': 1000, 'e0': -300, 'eY': -4000, 'g2': -1000, 'v3': -300, 'iS': -1300, 'vV': -20000, 'e2': 3000}, 'half': 13600, 'due': {'s0': -5500, 's1': -4500, 's2': -1500, 's3': -11500, 'b0': 9500, 'b1': 10000, 'b2': 10000, 'b3': 14500, 'e0': 71000, 'e1': 48500, 'e2': 65000, 'e3': 54500}}
+CFG = {'path': ['R2A2V1V1D2', 'A2D2D2D2', 'D2A2D2D2', 'D2D2D2D2', 'D2D2D2D2', 'D2D2D2D2', 'D2D2D2D2', 'D2D2D2D2'], 'egat': ['S8S8', 'S2S4S5S5', 'S2S3S3S2S6', 'S2S4S5S3V2', 'S4S4S8', 'S2S2V2S5S5', 'S2S1S1S1S3S8', 'S2S3S1S5S2S3'], 'pre': ['PQPPPQQPPPPPPPPP', 'PPPPPPPPPPPPPPPP', 'PPPPPPPPPPPPPPPP', 'PPPPPPPPPPPPPPPP'], 'parts': [1, 1, 2, 3], 'sub': 'DDDV', 'sum': 'DDDP', 'exp': ['S2S2S2S2S2S2S1S1S2', 'S2S2S2S2S2S2S2S2', 'S2S1S1S2S2S2S2S2S2', 'S4S4S4S4'], 'stretch': {'sV': 1.66, 'eP': 1.25, 'sS': 0.8, 'gS': 1.28, 'eV': 1.36, 'lS': 0.85, 'lY': 1.43, 'sP': 1.14, 'iS': 0.84, 'bS': 1.31, 'bP': 1.09, 'eY': 0.69, 'pV': 0.9, 'vV': 0.9, 'eS': 1.35, 'iV': 1.3, 'eG': 0.94, 'pP': 0.72, 'vP': 1.12, 'pG': 1.28, 'pS': 1.19, 'bV': 0.85, 'gV': 1.21}, 'rep': 4, 'ptv': 13, 'off': -1000, 'run': 8, 'tol': {'V': 300, 'S': 600, 'P': 1200, 'G': 500, 'Y': 1000}, 'bonus': {'bV': 110000.0, 'bP': 91700.0, 'bS': 109700.0, 'sG': 117000.0, 'pG': 50700.0, 'late': -32400, 'sP': 102000.0, 'uV': 200000.0, 'uP': 200000.0, 'pS': 40000.0, 'sS': 37000.0, 'gS': -13000, 'iV': -3700, 'e3': 3000, 'pV': 3300, 'g2': -7000, 'b2': -6000, 'e2': -2000, 's1': -300, 'b3': 10300, 'lY': 19700, 'p3': -2000, 'p0': -1000, 'v0': -8700, 'vV': 1000, 'eY': -2000, 'eV': -10300, 's3': 5000, 'g0': -18700, 'v1': 2700, 'g1': -3000, 'e0': -5700, 'iS': -9300, 'eP': 3000, 'init': -3000, 'eG': -1000, 'v2': -3000, 'eS': -1000, 'lS': -9300, 'b1': 11300, 'g3': -11700, 's0': 700, 'vP': 3000, 'gV': -6000, 'e1': 1000, 'v3': -1000}, 'half': 14500, 'due': {'s0': -13500, 's1': -500, 's2': 4000, 's3': 4000, 'b0': 16000, 'b1': 31000, 'b2': 19500, 'b3': 500, 'e0': 65500, 'e1': 66500, 'e2': 45500, 'e3': 30000}}
+CFG = {'path': ['R2A2V1V1D2', 'A2D2D2D2', 'D2A1A1D2D2', 'D2D2D2D2', 'D2D2D2D2', 'D2D2A2D2', 'D2D2D2D2', 'D2D2D2D2'], 'egat': ['S8S8', 'S2S4S5S5', 'S2S3S3S2S6', 'S2S4S5S2S1V2', 'S4S4S8', 'V2S2V2S5S4S1', 'S2S1S1V1S3S8', 'V2S3S1S5S1S4'], 'pre': ['PQQPPQPPPPPPPPPP', 'PPPPPPPPPPPPPPPP', 'PPPPPPPPPPPPPPPP', 'PPPPPPPPPPPPPPPP'], 'parts': [1, 1, 2, 3], 'sub': 'DDDV', 'sum': 'DDDP', 'exp': ['S2S2S2S2S2S2S1S1S2', 'S2S2S2S2S4S2S2', 'S2S1S1S2S2S2S2S2S2', 'S4S4S1S3S4'], 'stretch': {'sV': 1.66, 'eP': 1.8, 'sS': 0.64, 'gS': 1.02, 'eV': 1.34, 'lS': 1.03, 'lY': 1.02, 'sP': 0.9, 'iS': 0.6, 'bS': 1.31, 'bP': 1.09, 'eY': 0.59, 'pV': 1.05, 'vV': 0.71, 'eS': 1.28, 'iV': 1.5, 'eG': 0.85, 'pP': 0.65, 'vP': 1.04, 'pG': 0.84, 'pS': 1.22, 'bV': 0.85, 'gV': 1.65, 'sG': 1.04}, 'rep': 4, 'ptv': 13, 'off': -1500, 'run': 8, 'tol': {'V': 300, 'S': 800, 'P': 300, 'G': 100, 'Y': 1000}, 'bonus': {'bV': 97000.0, 'bP': 101400.0, 'bS': 112700.0, 'sG': 118000.0, 'pG': 50400.0, 'late': -33100, 'sP': 112300.0, 'uV': 200000.0, 'uP': 200000.0, 'pS': 43000.0, 'sS': 36000.0, 'gS': -13000, 'iV': 6300, 'e3': 12000, 'pV': 3300, 'g2': 11300, 'b2': -16000, 'e2': 0, 's1': 400, 'b3': 2300, 'lY': 20000, 'p3': -2300, 'p0': -1700, 'v0': 1300, 'vV': 400, 'eY': -11000, 'eV': 2400, 's3': 8000, 'g0': 1600, 'v1': 2700, 'g1': -3000, 'e0': -4000, 'iS': -300, 'eP': 5600, 'init': -9300, 'eG': -9000, 'v2': -4000, 'eS': -11300, 'lS': -10600, 'b1': 14300, 'g3': -12000, 's0': -1900, 'vP': 3000, 'gV': 8000, 'e1': -2300, 'v3': -700, 'b0': -4000, 'pP': -1000, 's2': -300}, 'half': 13500, 'due': {'s0': -20500, 's1': 0, 's2': 3500, 's3': 13000, 'b0': 34500, 'b1': 36500, 'b2': 21500, 'b3': -6000, 'e0': 63000, 'e1': 77000, 'e2': 44000, 'e3': 27500}}
+CFG["wary"] = {"rem": 6500.0, "dma": 2400.0}
+CFG = {'path': ['D2A2V2D2', 'D2A2D2D1D1', 'D2D1A1D2D2', 'D2D2D2D2', 'D2D2D2D2', 'D1D1D2A2D2', 'A2D2D2D2', 'D2D2D2D2'], 'egat': ['S3S5S8', 'S6S5S5', 'S2S3S3S2S1S5', 'S2S4S5S2S1V2', 'S8S8', 'V2S2V2S1S4S4S1', 'S2S1S1V1S3S8', 'V2S3S1S5S1S4'], 'pre': ['PQQPPQPPPPPPPPPP', 'PPPPPPPPPPPPPPPP', 'PPPPPPPPPPPPPPPP', 'PPPPPPPPPPPPPPPP'], 'parts': [1, 2, 2, 3], 'sub': 'DDDV', 'sum': 'DDDP', 'exp': ['S2S2S2S2S2S2S1S1S2', 'S2S2S2S1S1S4S2S1S1', 'S2S2S2S2S2S2S2S2', 'S4S4S1S3S2S2'], 'stretch': {'sV': 1.66, 'eP': 1.44, 'sS': 0.8, 'gS': 0.86, 'eV': 1.34, 'lS': 1.84, 'lY': 1.03, 'sP': 0.86, 'iS': 0.63, 'bS': 0.77, 'bP': 0.98, 'eY': 0.59, 'pV': 1.08, 'vV': 0.69, 'eS': 1.03, 'iV': 1.07, 'eG': 0.75, 'pP': 0.42, 'vP': 0.78, 'pG': 0.91, 'pS': 1.18, 'bV': 0.85, 'gV': 1.32, 'sG': 0.71}, 'rep': 2, 'ptv': 13, 'off': -2000, 'run': 8, 'tol': {'V': 300, 'S': 2000, 'P': 300, 'G': 100, 'Y': 1000}, 'bonus': {'bV': 97700.0, 'bP': 92400.0, 'bS': 112700.0, 'sG': 108000.0, 'pG': 46100.0, 'late': -26400, 'sP': 114300.0, 'uV': 200000.0, 'uP': 200000.0, 'pS': 41600.0, 'sS': 36000.0, 'gS': -6300, 'iV': -3400, 'e3': 2000, 'pV': 3600, 'g2': 19000, 'b2': -16000, 'e2': -10000, 's1': 100, 'b3': 3300, 'lY': 13000, 'p3': 6700, 'p0': -2000, 'v0': -28700, 'vV': 700, 'eY': -5300, 'eV': 15400, 's3': 9000, 'g0': -400, 'v1': 1400, 'g1': -3000, 'e0': -4600, 'iS': -42200, 'eP': -6400, 'init': -9300, 'eG': -5000, 'v2': -7000, 'eS': -2000, 'lS': -7600, 'b1': 4300, 'g3': -16300, 's0': -2900, 'vP': -1000, 'gV': 11700, 'e1': -10000, 'v3': -19100, 'b0': -11000, 'pP': 700, 's2': 3000, 'sV': -300, 'p2': -300}, 'half': 13800, 'due': {'s0': -6000, 's1': -500, 's2': 4000, 's3': 6500, 'b0': 24500, 'b1': 28000, 'b2': 22000, 'b3': 2000, 'e0': 55000, 'e1': 85500, 'e2': 50000, 'e3': 28500}, 'wary': {'rem': 5000, 'G': 1.9}}
+CFG.update({'path': ['D2A2V2D2', 'A2D2D2A2'] + ['D4D2D2'] * 6, 'egat': ['S8S8', 'S2S4S5S5'] * 4, 'rep': 4, 'parts': [1, 1, 2, 3]})
+CFG = {'path': ['V2D2A2V2', 'A2V1V1V1D1A2', 'V2A2A2A1A1', 'D1D3D2D2', 'D4A1A1D2', 'D4D2D2', 'D4D4', 'D4A2D2'], 'egat': ['S3S5S8', 'S1S1S4S5S5', 'S8S7S1', 'S2S4S5S5', 'S8S1V2S5', 'V2S4S5S5', 'S8S8', 'S2S4S5S5'], 'pre': ['PQPPPQPQPPPPPPPP', 'PPPPPPPPQPPPPPPP', 'PPPPPPPPPPPPQQPP', 'PPPPPPPPPPPPPPPP'], 'parts': [1, 1, 2, 3], 'sub': 'DDVV', 'sum': 'DDDP', 'exp': ['S2S2S2S1S1S2S2S1S1S2', 'S1S3S2S1S1S4S2S1S1', 'S6S2S2S2S2S2', 'S4S4S1S3S2S1S1'], 'stretch': {'sV': 1.42, 'eP': 1.3, 'sS': 0.53, 'gS': 0.9, 'eV': 0.62, 'lS': 1.96, 'lY': 0.63, 'sP': 0.58, 'iS': 0.49, 'bS': 1.01, 'bP': 0.88, 'eY': 0.52, 'pV': 1.25, 'vV': 0.56, 'eS': 1.43, 'iV': 1.1, 'eG': 1.0, 'pP': 0.4, 'vP': 0.89, 'pG': 0.85, 'pS': 1.38, 'bV': 0.77, 'gV': 1.1, 'sG': 0.79}, 'rep': 4, 'ptv': 10, 'off': -1500, 'run': 8, 'tol': {'V': 300, 'S': 200, 'P': 200, 'G': 500, 'Y': 1000}, 'bonus': {'bV': 97400.0, 'bP': 100400.0, 'bS': 133700.0, 'sG': 118300.0, 'pG': 42400.0, 'late': -50700, 'sP': 114000.0, 'uV': 200000.0, 'uP': 200000.0, 'pS': 44900.0, 'sS': 35000.0, 'gS': -26900, 'iV': -400, 'e3': 13000, 'pV': 3600, 'g2': 20700, 'b2': -23400, 'e2': 1000, 's1': -600, 'b3': -4400, 'lY': 6000, 'p3': 1000, 'p0': -2300, 'v0': -20700, 'vV': 10700, 'eY': -5600, 'eV': 11400, 's3': -15300, 'g0': -400, 'v1': 4100, 'g1': -3000, 'e0': -13600, 'iS': -31500, 'eP': -6400, 'init': -8000, 'eG': 700, 'v2': -7700, 'eS': -2000, 'lS': -5600, 'b1': -6100, 'g3': -18400, 's0': 100, 'vP': -1000, 'gV': 21700, 'e1': -27000, 'v3': -19100, 'b0': -10000, 'pP': 100, 's2': 3000, 'sV': -3600, 'p2': -300, 'p1': 29700}, 'half': 14700, 'due': {'s0': 0, 's1': -2000, 's2': 4500, 's3': 20000, 'b0': 36000, 'b1': 23500, 'b2': 37000, 'b3': -500, 'e0': 53500, 'e1': 98500, 'e2': 51500, 'e3': 28000}, 'wary': {'rem': 5500, 'G': 1.56, 'gi': 1400, 'dma': 2000}}
+CFG = {'path': ['V2D2A2V2', 'A2V1V1V1A1A2', 'V1V1A2D2A1A1', 'D1D3D2D1D1', 'D4A1A1D2', 'D4A2D2', 'D4D4', 'D4A2D2'], 'egat': ['S3V5S8', 'S1S1S4S5S5', 'S8V5V2S1', 'S2S4S5S5', 'S8S1V2S5', 'V2S4S3S2S5', 'S5S3S8', 'S2S4S1S2S2S3S2'], 'pre': ['PQPPPQQQPPPPPPPP', 'PPPPPPPPQPPPPPPP', 'PPPPPPQPPPPPQPPP', 'PPPPPPPPPPPPPPPP'], 'parts': [1, 1, 2, 3], 'sub': 'DDVV', 'sum': 'DDDP', 'exp': ['S2S2S2S1S1S2S1S1S1S1S2', 'S4S2S1S1S4S3S1', 'S6S2S2S2S2S2', 'S4S4S4S2S1S1'], 'stretch': {'sV': 1.49, 'eP': 1.63, 'sS': 0.53, 'gS': 1.11, 'eV': 0.5, 'lS': 1.41, 'lY': 0.86, 'sP': 0.3, 'iS': 0.54, 'bS': 0.84, 'bP': 0.91, 'eY': 0.33, 'pV': 0.91, 'vV': 0.9, 'eS': 1.5, 'iV': 0.79, 'eG': 1.56, 'pP': 0.4, 'vP': 0.86, 'pG': 1.06, 'pS': 1.53, 'bV': 0.96, 'gV': 1.32, 'sG': 0.7}, 'rep': 4, 'ptv': 10, 'off': 500, 'run': 8, 'tol': {'V': 300, 'S': 200, 'P': 1200, 'G': 500, 'Y': 1000}, 'bonus': {'bV': 108700.0, 'bP': 93700.0, 'bS': 137000.0, 'sG': 121300.0, 'pG': 42400.0, 'late': -51400, 'sP': 123100.0, 'uV': 200000.0, 'uP': 200000.0, 'pS': 41600.0, 'sS': 37000.0, 'gS': -26600, 'iV': -8100, 'e3': 2700, 'pV': 3600, 'g2': 23700, 'b2': -33400, 'e2': 11000, 's1': 3700, 'b3': -1400, 'lY': 16000, 'p3': -2300, 'p0': -2300, 'v0': -36600, 'vV': 10700, 'eY': -3200, 'eV': 21100, 's3': -15300, 'g0': -10100, 'v1': 5100, 'g1': -14000, 'e0': -14600, 'iS': -21500, 'eP': 17600, 'init': -8000, 'eG': -9600, 'v2': -9400, 'eS': -4000, 'lS': -8900, 'b1': -19400, 'g3': -15400, 's0': 100, 'vP': 1300, 'gV': 12000, 'e1': -26400, 'v3': -19400, 'b0': -10000, 'pP': -6300, 's2': 3000, 'sV': -3600, 'p2': 0, 'p1': 29700}, 'half': 15300, 'due': {'s0': -7000, 's1': 9000, 's2': 5500, 's3': 43000, 'b0': 8500, 'b1': 30000, 'b2': 29500, 'b3': 10500, 'e0': 64500, 'e1': 100500, 'e2': 47500, 'e3': 28000}, 'wary': {'rem': 5500, 'G': 1.56, 'gi': 1400, 'dma': 2000}}
+CFG = {'path': ['V2D2D2D2', 'D2V2D2D2', 'D2A2D2D2', 'D2D2D1D1A1A1', 'A2D2D2A2', 'V2A2D2D2', 'D2D1D1D2D2', 'D2A2D3D1'], 'egat': ['S5S3S4S4', 'S2S5S4S5', 'S4S1S1V2S3V1S4', 'S1S1S1S3S5S5', 'V4S4S1S3S4', 'S2S4V5S2S3', 'V4S4S2S2S4', 'S2V4S5S5'], 'pre': ['QQOOOOOOOOOQQOOO', 'PPOOPPPPPPOOPPOO', 'POOOOOOOOOOQPPOO', 'PPOOQPPPPOOOOOOO'], 'parts': [1, 1, 2, 3], 'sub': 'DDVV', 'sum': 'DDDP', 'exp': ['S2S2S4S4S2S2', 'S2S2S2S1S1S2S2S2S2', 'S2S2S2S2S2S2S2S2', 'S4S2S2S2S2S4'], 'stretch': {'sV': 1.01, 'sP': 1.45, 'eG': 0.72, 'iV': 1.36, 'eS': 1.14, 'gS': 0.75, 'vV': 0.83, 'sG': 0.89, 'sS': 0.93, 'lY': 0.33, 'eV': 1.07, 'pP': 0.98, 'eY': 1.39, 'gV': 0.87, 'pV': 1.72, 'pG': 0.82, 'pS': 0.59, 'vP': 1.55, 'eP': 0.8, 'iS': 0.85, 'lS': 1.11, 'bS': 0.72, 'bP': 1.05, 'bV': 1.1}, 'rep': 4, 'ptv': 7, 'off': 0, 'run': 8, 'tol': {'V': 300, 'S': 500, 'P': 800, 'G': 2000, 'Y': 1000}, 'bonus': {'bV': 105000.0, 'bP': 78700.0, 'bS': 99000.0, 'sG': 109600.0, 'pG': 70000.0, 'late': 600, 'sP': 89700.0, 'uV': 200000.0, 'uP': 200000.0, 'pS': 43000.0, 'sS': 39000.0, 'gS': -14000, 'e0': 8700, 'v2': 6000, 'iS': 20400, 'g3': 5600, 'pP': -1300, 'g2': 29300, 'pV': 1000, 'g1': -3000, 'init': 35000, 'vP': 26300, 'eY': 16600, 'lY': -3000, 'b3': 5900, 'v1': -300, 's2': -300, 'p3': 11900, 'gV': -8000, 'v3': -17000, 'b2': -16000, 'e3': 7900, 'eP': 31600, 's3': -2700, 's0': 300, 'b1': 21000, 'v0': -6300, 'e2': -6400, 'iV': 26700, 'e1': -4000, 'lS': -23000, 'vV': -17300, 'p2': 6700, 'b0': -11300, 'g0': 9700, 'eV': -4400, 'eS': -300, 'sV': -1000, 'eG': -18000, 'p1': -1000, 's1': 3300}, 'half': 14800, 'due': {'s0': -7000, 's1': 7000, 's2': 2000, 's3': 29500, 'b0': 32500, 'b1': 12500, 'b2': 27000, 'b3': 32000, 'e0': 47500, 'e1': 47000, 'e2': 61500, 'e3': 28500}, 'wary': {'rem': 4500, 'pe': 0.55, 'gi': 1000, 'dma': 2000}}
 OPS = build(CFG)
+if "F" not in "".join(CFG["path"]): SCRATCH.pop("sf")
+if "A" not in CFG["sum"]: SCRATCH.pop("s2")
 link(OPS)
-ORDER, SPAN = plan(OPS, COST, CFG["slack"])
-SEMAPHORES = ["cV", "cS", "cP", "cG", "snt"] + ["arr%d" % t for t in range(4 * CFG["np"])] + ["d%d" % i for i, o in enumerate(OPS) if o["kind"] == "d"]
+ORDER, SPAN = plan(OPS, COST, CFG)
+SEMAPHORES = [x + str(j) for j in sorted({o["slot"] for o in OPS if o["kind"] == "f"}) for x in ("fa", "fb")] + ["cV", "cS", "cP", "cG", "snt"] + ["arr%d" % t for t in range(8)] + ["d%d" % i for i, o in enumerate(OPS) if o["kind"] == "d"]
 
 
 def rank_program(g, core, T, topo):
     rank = T.rank_of(core)
+    def helper(c): return [x for x in topo.cores_of(c) if x not in T.cores and topo.die(x) == topo.die(c)][0]
     if rank is None:
+        for c in T.cores:
+            if helper(c) == core:
+                seen = {}; sent = 0
+                for i in ORDER:
+                    o = OPS[i]
+                    if o["kind"] == "f":
+                        j = o["slot"]; seen[j] = seen.get(j, 0) + len(topo.engines(c, core)); dst = o["fn"](g, T)[0]
+                        g.wait_ge(T.sem["fa%d" % j], seen[j])
+                        g.remote_dma(dst, dst, T.sem["fb%d" % j], T.sem.snt, topo.addr(c)[1], topo.addr(c)[0], topo.mask(core, c))
+                        sent += len(topo.engines(core, c))
+                if sent: g.wait_ge(T.sem.snt, sent)
         return
+    mate = helper(core)
     nxt = T.cores[(rank + 1) % len(T.cores)]
     prv = T.cores[(rank - 1) % len(T.cores)]
     rid, pid, _ = topo.addr(nxt)
@@ -518,7 +550,9 @@ def rank_program(g, core, T, topo):
     count = {q: 0 for q in Q}; know = {q: {} for q in Q}; mark = {}; clock = {}; total = {}
     for i in ORDER:
         o = OPS[i]; q = o["q"]; kn = know[q]
-        for d in sorted(o["dep"], key=lambda d: -OPS[d]["start"]):
+        for d in sorted(o["all"], key=lambda d: -OPS[d]["start"]):
+            if d in o["free"]:
+                continue
             s, v = mark[d]
             if kn.get(s, 0) < v:
                 Q[q].wait_ge(T.sem[s], v)
@@ -526,7 +560,14 @@ def rank_program(g, core, T, topo):
                 for a, b in clock[d].items():
                     if kn.get(a, 0) < b: kn[a] = b
         clock[i] = dict(kn)
-        if o["kind"] == "r":
+        if o["kind"] == "f":
+            _, alu, folds = o["fn"](g, T); j = o["slot"]; eng = topo.engines(core, mate); n_h = len(eng); per = n_h // len(folds)
+            g.remote_dma_fused([RemoteDMATransfer(dst_ids=[DstId(rid=topo.addr(mate)[0], pnc=topo.addr(mate)[1])],
+                                                  dma_engine_mask=sum(1 << e for e in eng[x * per:(x + 1) * per]),
+                                                  remote_sem=T.sem["fa%d" % j], srcs=srcs, dsts=[dst], alu_op=alu)
+                                for x, (dst, srcs) in enumerate(folds)], local_sem=T.sem.snt)
+            mark[i] = ("fb%d" % j, total.get("fb%d" % j, 0) + len(topo.engines(mate, core))); total["snt"] = total.get("snt", 0) + n_h
+        elif o["kind"] == "r":
             t = o["n"]
             g.remote_dma(T.hl[:, t, 1], T.hl[:, t, 0], T.sem["arr%d" % t], T.sem.snt, pid, rid, mask)
             mark[i] = ("arr%d" % t, n_in); total["snt"] = total.get("snt", 0) + n_out

from concourse.bass import DstId, RemoteDMATransfer
from concourse.mybir import AluOpType as ALU, ActivationFunctionType as ACT

F32, BF, I32, U16 = "float32", "bfloat16", "int32", "uint16"

SCRATCH = {
    "nds": ("sbuf", [128, 16, 16], I32), "ia": ("sbuf", [128, 3, 16, 16], I32),
    "eas": ("sbuf", [128, 4096], BF), "ers": ("sbuf", [128, 1024], BF),
    "dls": ("sbuf", [128, 4], F32), "mm": ("sbuf", [128, 8], F32),
    "fr": ("sbuf", [128, 8, 2048], BF),
    "pt0": ("sbuf", [128, 5120], BF), "pt1": ("sbuf", [128, 5120], BF), "nt": ("sbuf", [128, 5120], F32),
    "jx": ("sbuf", [128, 2, 144], F32), "pi": ("sbuf", [128, 8], I32), "pf": ("sbuf", [128, 8], F32),
    "zz": ("sbuf", [128, 3, 2, 144], BF), "idb": ("sbuf", [128, 4, 128], BF), "idf": ("sbuf", [128, 2, 128], F32),
    "sc": ("sbuf", [128, 256], BF), "sf": ("sbuf", [128, 8, 64], F32),
    "hl": ("sbuf", [128, 10, 2, 2, 128], BF), "ul": ("sbuf", [128, 2560], U16), "o2": ("sbuf", [128, 2, 2, 192], F32),
    "eq": ("sbuf", [128, 2, 8, 256], BF),
    "dd": ("sbuf", [128, 8192], BF), "md": ("sbuf", [128, 8192], BF),
    "sv": ("sbuf", [128, 4, 72, 16], F32),
    "kk": ("sbuf", [128, 2, 16, 16], F32),
    "ne0": ("sbuf", [128, 2, 2048], F32), "ne1": ("sbuf", [128, 2, 2048], F32), "ne2": ("sbuf", [128, 2, 2048], F32),
    "tt": ("sbuf", [128, 256], F32), "cs": ("sbuf", [128, 256], F32),
    "bs": ("sbuf", [128, 2, 2, 1024], F32), "so": ("sbuf", [128, 256], F32), "s2": ("sbuf", [128, 256], F32),
    "key0": ("psum", [128, 4, 128], F32), "key1": ("psum", [128, 4, 128], F32), "aa": ("psum", [128, 512], F32),
    "bb": ("psum", [128, 512], F32), "xb": ("psum", [128, 512], F32),
    "sp": ("psum", [128, 4, 24, 16], F32),
}

NET = [(0, 0, 1, 0, 1, 4, 0, 8, 2), (1, 0, 1, 0, 1, 4, 1, 9, 2), (0, 4, 1, 4, 1, 4, 1, 8, 2), (1, 4, 1, 4, 1, 4, 0, 9, 2),
       (1, 8, 1, 8, 1, 4, 0, 27, 1), (0, 12, 1, 12, 1, 4, 0, 16, 1), (1, 12, 1, 12, 1, 4, 1, 18, 1), (0, 8, 1, 8, 1, 4, 1, 4, 1),
       (0, 27, 2, 5, 2, 2, 0, 20, 2), (1, 27, 2, 5, 2, 2, 1, 14, 2), (0, 17, 2, 18, 2, 2, 1, 9, 2), (1, 17, 2, 18, 2, 2, 0, 24, 2),
       (1, 16, 4, 4, 5, 4, 0, 31, 9), (0, 18, 4, 6, 5, 4, 0, 44, 9), (0, 16, 4, 4, 5, 4, 1, 22, -5), (1, 18, 4, 6, 5, 4, 1, 23, -5),
       (0, 31, 9, 12, -5, 2, 0, 45, 2), (0, 62, 9, 23, -5, 2, 1, 5, 4), (1, 31, 9, 12, -5, 2, 1, 19, 2), (1, 62, 9, 23, -5, 2, 0, 55, 2),
       (0, 45, 2, 17, 2, 3, 0, 46, 4), (1, 53, 2, 5, 4, 3, 0, 48, 4), (1, 45, 2, 17, 2, 3, 1, 18, -4), (0, 53, 2, 5, 4, 3, 1, 20, -4),
       (1, 44, 2, 22, -2, 4, 0, 1, 1), (1, 52, 2, 14, -2, 4, 0, 40, 1), (0, 52, 2, 14, -2, 4, 1, 9, 2), (0, 44, 2, 22, -2, 4, 1, 7, -1),
       (0, 1, 1, 9, 2, 4, 0, 36, 1), (1, 1, 1, 9, 2, 4, 1, 3, -1),
       (0, 36, 1, 5, -1, 6, 0, 0, 7), (1, 36, 1, 5, -1, 6, 1, 8, 2),
       (0, 0, 7, 6, 2, 7, 0, 50, -1), (1, 0, 7, 6, 2, 7, 1, 9, 2)]
MAGIC = 1.5 * 2.0 ** 30
BIG = 2.0 ** 24


def pieces(spec):
    out, a = [], 0
    for i in range(0, len(spec), 2):
        n = int(spec[i + 1]); out.append((spec[i], a, n)); a += n
    return out


def build(cfg):
    ops = []
    tag = ["init", 0]

    def add(q, kind, n, fn, r=(), w=(), banks=(), gat=False, grp=None):
        ops.append({"q": q, "kind": kind, "n": n, "fn": fn, "r": list(r), "w": list(w), "banks": list(banks), "gat": gat,
                    "tag": tag[0], "part": tag[1], "grp": grp, "last": [False]})

    def V(n, fn, r, w, banks=(), gat=False): add("V", "c", n, lambda g, T: [fn(g.vector, T)], r, w, banks, gat)
    def S(n, fn, r, w, banks=(), gat=False): add("S", "c", n, lambda g, T: [fn(g.scalar, T)], r, w, banks, gat)
    def GC(n, fn, r, w): add("G", "c", n, lambda g, T: [fn(g, T)], r, w)
    def Y(nb, fn, r, w, runs=1): add("Y", "d", (nb, runs), lambda g, T: [fn(g.sync, T)], r, w)
    def SD(nb, fn, r, w): add("S", "d", (nb, 1), lambda g, T: [fn(g.scalar, T)], r, w)
    def GD(nb, fn, r, w, runs=1): add("G", "d", (nb, runs), lambda g, T: [fn(g, T)], r, w)

    def PE(mms, r, w, banks, start=True, stop=True, grp=None):
        last = [False]
        def fn(g, T):
            out = []
            for i, m in enumerate(mms):
                o, a, b = m[1](T)
                out.append(g.tensor.matmul(o, a, b, start and i == 0, (last[0] if grp else stop) and i == len(mms) - 1))
            return out
        add("P", "c", [m[0] for m in mms], fn, r, w, banks, grp=grp)
        ops[-1]["last"] = last

    def sl(a, s, n): return slice(a, a + s * (n - 1) + 1, s) if s > 0 else slice(a, a + s * n if a + s * n >= 0 else None, s)
    def blk(q, n=1): return slice(q * 256, (q + n) * 256)
    def hb(q, n=1): return slice(q * 128, (q + n) * 128)

    Y(1 << 17, lambda e, T: e.dma_start(T.nds[:], T.nd[:]), [], ["nds"])
    PAS = [("md", j) for j in range(8)]
    SD(1 << 20, lambda e, T: e.dma_start(T.md[:, 0:4096], T.pa[:]), [], PAS)
    for j in range(4):
        Y(1 << 16, lambda e, T, j=j: e.dma_start(T.fr[:, 0:2, hb(j)], T.fc[:, blk(0)]), [], [("fr", 0, j)], 2)
    Y(1 << 18, lambda e, T: e.dma_start(T.fr[:, 0:2, 512:1024], T.fr[:, 0:2, 0:512]), [("fr", 0, j) for j in range(4)], [("fr", 0, 4)], 2)
    def FR(t, n): return [("fr", 0, j) for j in range(3 + n // 512)] if t == 0 else [("fr", min(t, 2), m) for m in (128, 256, 512, 1024, 2048) if m < 2 * n]
    Y(1 << 20, lambda e, T: e.dma_start(T.eas[:], T.ea[:]), PAS, ["eas"])
    tag[0] = "late"
    for j, a, z in ((1, 2, 4), (2, 4, 8)):
        wide = max(n for x in cfg["path"][a:z] for _, _, n in pieces(x)) * 512
        Y((z - a) << 15, lambda e, T, a=a, z=z: e.dma_start(T.fr[:, a:z, 0:128], T.fc[:, hb(a, z - a)]), ["eas"], [("fr", j, 128)], z - a)
        for n in (128, 256, 512, 1024):
            if n < wide:
                Y(n * (z - a) * 256, lambda e, T, n=n, a=a, z=z: e.dma_start(T.fr[:, a:z, n:2 * n], T.fr[:, a:z, 0:n]),
                  [("fr", j, m) for m in (128, 256, 512, 1024) if m <= n], [("fr", j, 2 * n)], z - a)
    Y(1 << 18, lambda e, T: e.dma_start(T.ers[:], T.er[:]), ["eas"], ["ers"])
    Y(1 << 10, lambda e, T: e.dma_start(T.dls[:, 0:1], T.dl[:]), ["eas"], ["dls"])
    MM = [("mm", s) for s in range(5)]
    for s, val in enumerate((1.0, -1.0, 1.5, 2.0, -2.0)):
        S(1, lambda a, T, s=s, val=val: a.activation(T.mm[:, s:s + 1], T.dls[:, 0:1], ACT.Identity, scale=val), ["dls"], [MM[s]])
    tag[0] = "init"
    GC(160, lambda g, T: g.iota(T.pi[:, 0:1], [[0, 1]], 0, 1), [], ["pi0"])
    GC(160 + 576, lambda g, T: g.iota(T.jx[:], [[-1, 2], [1, 144]], 0, 0, allow_small_or_imprecise_dtypes=True), [], ["jx"])
    GC(160, lambda g, T: g.iota(T.pf[:, 0:1], [[0, 1]], 0, 1, allow_small_or_imprecise_dtypes=True), [], ["pf0"])
    GC(160 + 512, lambda g, T: g.iota(T.sc[:], [[128, 32], [0, 8]], 0, 0, allow_small_or_imprecise_dtypes=True), [], ["sc"])
    V(1, lambda v, T: v.tensor_scalar(T.pi[:, 4:5], T.pi[:, 0:1], 112, None, ALU.bitwise_and), ["pi0"], ["pi4"])
    V(1, lambda v, T: v.tensor_scalar(T.pf[:, 4:5], T.pi[:, 4:5], 14.0, None, ALU.add), ["pi4"], ["pf4"])
    V(288, lambda v, T: v.tensor_scalar(T.zz[:, 0], T.jx[:], T.pf[:, 4:5], 4096.0, ALU.is_equal, ALU.mult), ["jx", "pf4"], [("zz", 0)])
    for s, val in ((1, 2.0), (2, -1.0)):
        S(288, lambda a, T, s=s, val=val: a.activation(T.zz[:, s], T.zz[:, 0], ACT.Identity, scale=val), [("zz", 0)], [("zz", s)])
    V(128, lambda v, T: v.tensor_scalar(T.idb[:, 0, :], T.jx[:, 0, 0:128], T.pf[:, 0:1], None, ALU.is_equal), ["jx", "pf0"], [("idb", 0)])
    for s, val in ((1, 64.0), (2, BIG)):
        S(128, lambda a, T, s=s, val=val: a.activation(T.idb[:, s, :], T.idb[:, 0, :], ACT.Identity, scale=val), [("idb", 0)], [("idb", s)])
    tag[0] = "late"
    S(128, lambda a, T: a.activation(T.idb[:, 3, :], T.idb[:, 0, :], ACT.Identity, scale=-1.0), [("idb", 0)], [("idb", 3)])
    for s, val in enumerate((0.5, 1.0)):
        S(128, lambda a, T, s=s, val=val: a.activation(T.idf[:, s, :], T.idb[:, 0, :], ACT.Identity, scale=val), [("idb", 0)], [("idf", s)])
    tag[0] = "init"

    def zw(T, s, r):
        i = r & 1
        return T.zz[:, s, i, 14 + i - r:142 + i - r]

    V(256, lambda v, T: v.tensor_scalar(T.ia[:, 0], T.nds[:], 15, None, ALU.bitwise_and), ["nds"], ["ia0"])
    V(256, lambda v, T: v.tensor_scalar(T.ia[:, 1], T.nds[:], 10, None, ALU.logical_shift_right), ["nds"], ["ia1"])
    V(256, lambda v, T: v.tensor_scalar(T.ia[:, 2], T.nds[:], 4, 63, ALU.logical_shift_right, ALU.bitwise_and), ["nds"], ["ia2"])
    for p in range(2):
        c = slice(8 * p, 8 * p + 8)
        V(128, lambda v, T, c=c, p=p: v.tensor_scalar(T.xb[:, hb(p)], T.ia[:, 0, :, c], 4.0, None, ALU.mult), ["ia0"], [("xb", p)], ["xb"])
        V(128, lambda v, T, c=c, p=p: v.tensor_tensor(T.hl[:, p, 0, 0, :], T.ia[:, 1, :, c], T.xb[:, hb(p)], ALU.add), ["ia1", ("xb", p)], [("hl", 0, p, 0, 0), "xb"], ["xb"])
        V(128, lambda v, T, c=c, p=p: v.tensor_scalar(T.hl[:, p, 0, 1, :], T.ia[:, 2, :, c], 0.0, None, ALU.add), ["ia2"], [("hl", 0, p, 0, 1)])

    for q in range(1, 17):
        if q <= cfg["ptv"]:
            V(128, lambda v, T, q=q: v.tensor_copy(T.pt0[:, blk(q)], T.md[:, q % 16:4096:16]), PAS, [("pt0", q)])
        else:
            S(256, lambda a, T, q=q: a.activation(T.pt0[:, blk(q)], T.md[:, q % 16:4096:16], ACT.Copy), PAS, [("pt0", q)])
    tag[0] = "late"
    def pcopy(dst, q, src, qs, n):
        Y(n << 16, lambda e, T: e.dma_start(T[dst][:, blk(q, n)], T[src][:, blk(qs, n)]), [(src, qs + i) for i in range(n)], [(dst, q + i) for i in range(n)])
    def pnew(dst, d):
        Y(1 << 16, lambda e, T: e.dma_start(T[dst][:, blk(16 + d)], T.fc[:, blk(d)]), ["eas"], [(dst, 16 + d)])
    pcopy("pt1", 2, "pt0", 2, 14); pcopy("pt1", 17, "pt0", 1, 1); pcopy("pt1", 19, "pt0", 3, 1); pcopy("pt0", 18, "pt0", 2, 1)
    pnew("pt1", 0); pnew("pt1", 2); pnew("pt0", 1)
    def NT(q): return [("nt", q, i) for i in range(2)]
    for q in range(1, 17):
        S(256, lambda a, T, q=q: a.activation(T.nt[:, blk(q)], T.eas[:, q % 16::16], ACT.Identity, scale=-1.0), ["eas"], NT(q))
    Y(3 << 17, lambda e, T: e.dma_start(T.nt[:, blk(17, 3)], T.nt[:, blk(1, 3)]), NT(1) + NT(2) + NT(3), NT(17) + NT(18) + NT(19))

    if "F" in "".join(cfg["path"]):
        PE([(384, lambda T, r=r: (T.bb[:, 0:384], zw(T, 2, r), T.fr[:, 2:8, r:1024:16])) for r in range(16)], [("zz", 2)] + FR(1, 1024) + FR(2, 1024), ["bb"], ["bb"])
        S(384, lambda a, T: a.activation(T.sf[:, 2:8, :], T.bb[:, 0:384], ACT.Copy), ["bb"], ["sf"], ["bb"])

    def ucol(t, p, h): return ((2 * t + p) * 2 + h) * 128

    def number(t, p, h, twice=True):
        def umm(j):
            PE([(128, lambda T, du=du: (T.aa[:, hb(2 * p + j)], T.idb[:, 1 - du, :], T.hl[:, 2 * t + p, h, du, :])) for du in range(2)],
               [("hl", t, p, h, 0), ("hl", t, p, h, 1), ("idb", 0), ("idb", 1)], [("aa", p, j)], ["aa"])
        old = tag[0]; tag[0] = "u%d" % t
        umm(0)
        if twice: umm(1)
        c = ucol(t, p, h)
        V(128, lambda v, T: v.tensor_copy(T.ul[:, c:c + 128], T.aa[:, hb(2 * p)]), [("aa", p, 0)], [("ul", t, p, h)], ["aa"])
        tag[0] = old

    def own_lists(t, p):
        if t < 4:
            add("G", "r", 2 * t + p, None, [("hl", t, p, 0, 0), ("hl", t, p, 0, 1)], [("hl", t, p, 1, 0), ("hl", t, p, 1, 1)])
        number(t, p, 0, t < 4)
        if t < 4:
            for j in range(2):
                a0 = 256 * p + 64 * j
                S(184, lambda a, T, j=j, a0=a0: a.activation(T.o2[:, p, j, 0:184], T.aa[:, a0:a0 + 184], ACT.Copy), [("aa", p, 0), ("aa", p, 1)], [("o2", p, j)], ["aa"])

    def select(t, p):
        w0 = (t + 1) * 256; tp_ = 2 * t + p; pt = "pt%d" % (t % 2); key = "key%d" % p
        PW = [(pt, q) for q in range(t + 1, t + 17)]
        grp = (key, t)
        KEY = [(key, j) for j in range(8)] + [(key, "v", r) for r in range(8)]
        PE([(256, lambda T: (T[key][:, 0:2, :], T.idb[:, 0, :], T.sc[:]))], ["sc", ("idb", 0)], KEY + [(key, "open")], [key], True, grp=grp)

        def chunk(who, u0, nu):
            e0, n = p * 4096 + u0 * 512, nu * 512; h = u0 // 4; o0 = ucol(t, p, 0) + u0 * 32; k0 = u0 % 4 * 32
            def win(T): return T[pt][:, w0:w0 + 4096].indirect(T.ul[:, o0:o0 + n // 16])
            def dd(T): return T.dd[:, e0:e0 + n]
            def md(T): return T.md[:, e0:e0 + n]
            rd = PW + [("ul", t, p, h)]
            dt_ = [("dd", 8 * p + u0 + j) for j in range(nu)]; mt = [("md", 8 * p + u0 + j) for j in range(nu)]
            if who == "F":
                S(n, lambda a, T: a.activation(dd(T), win(T), ACT.Copy), rd, dt_, gat=True)
                add("G", "f", (n * 512, 2), lambda g, T: (md(T), 2, [(md(T), [dd(T), T.fr[:, tp_, 0:n]])]), FR(t, n) + dt_, mt)
                ops[-1]["slot"] = 8 * p + u0
                PE([(n // 4, lambda T: (T[key][:, h, k0:k0 + n // 16], T.idf[:, 1, :], T.sf[:, tp_, 0:n // 16]))], ["sf", ("idf", 1), (key, "open")],
                   [(key, u0 + j) for j in range(nu)], [key], False, grp=grp)
            elif who in "DA":
                S(n, lambda a, T: a.activation(dd(T), win(T), ACT.Identity, scale=-1.0), rd, dt_, gat=True)
                GD(n * 512, lambda g, T: g.dma_start(dd(T), T.fr[:, tp_, 0:n], accum_op=ALU.add), FR(t, n) + dt_, dt_)
            else:
                V(n, lambda v, T: v.tensor_tensor(dd(T), win(T), T.fr[:, tp_, 0:n], ALU.subtract), rd + FR(t, n), dt_, gat=True)
            if who == "F":
                parts = [(2, "dd"), (1, "md")]
            elif who in "DR":
                V(n // 2, lambda v, T: v.tensor_scalar(md(T), dd(T), 0.0, None, ALU.max), dt_, mt)
                parts = [(2, "dd"), (1, "md")]
            else:
                S(n, lambda a, T: a.activation(md(T), dd(T), ACT.Abs), dt_, mt)
                parts = [(0, "md")]
            for s, name in parts:
                mms = [(n // 16, lambda T, s=s, r=r, name=name: (T[key][:, h, k0:k0 + n // 16], zw(T, s, r), T[name][:, e0 + r:e0 + n:16])) for r in range(16)]
                for x in range(0, 16, cfg["run"]):
                    PE(mms[x:x + cfg["run"]], [("zz", s), (key, "open")] + (mt if name == "md" else dt_), [(key, u0 + j) for j in range(nu)], [key], False, grp=grp)

        tag[0] = "p%d" % t
        todo = pieces(cfg["path"][tp_])
        for who, u0, nu in todo:
            if u0 < 4: chunk(who, u0, nu)
        number(t, p, 1)
        for who, u0, nu in todo:
            if u0 >= 4: chunk(who, u0, nu)
        if t < 2 and p == 1:
            pnew(pt, t)
        tag[0] = "v%d" % t
        for r in range(8):
            V(256, lambda v, T, r=r: v.tensor_tensor(T.eq[:, p, r, :], T.o2[:, p, :, 8 * r:8 * r + 128], T.aa[:, blk(p)], ALU.is_equal),
              [("o2", p, 0), ("o2", p, 1), ("aa", p, 0), ("aa", p, 1)], [("eq", p, r)], ["aa"])
            PE([(128, lambda T, r=r, j=j: (T[key][:, 1, :], T.idb[:, 2, :], T.eq[:, p, r, hb(j)])) for j in range(2)],
               [("eq", p, r), ("idb", 2), (key, "open")], [(key, "v", r)], [key], False, grp=grp)
        tag[0] = "s%d" % t
        H = slice(2 * p, 2 * p + 2); h0, h1 = 2 * p, 2 * p + 1
        def ts(h, x): return ("sv", p, h, x)
        def tp(h, x): return ("sp", p, h, x)
        for side in range(2):
            for du in range(2):
                kr = KEY + [("hl", t, p, h, du) for h in range(2)]
                c = slice(du * 8, du * 8 + 8); x = slice(side * 64, side * 64 + 64)
                wt = [(tp if side else ts)(h, x_) + (du,) for h in range(2) for x_ in range(8)]
                V(128, lambda v, T, c=c, x=x, side=side, du=du: v.tensor_tensor((T.sp if side else T.sv)[:, H, 0:8, c], T.hl[:, tp_, :, du, x],
                                                                                T[key][:, 0:2, x], ALU.add), kr, wt, [key])
        def both(xs): return [x + (du,) for x in xs for du in range(2)]
        def step(op, s0, ss, p0, ps, n, mem, o0, os_, hs=(0, 1), hp=(0, 1), ho=(0, 1)):
            def at(h): return H if len(h) == 2 else 2 * p + h[0]
            rt = both([ts(h, s0 + ss * j) for h in hs for j in range(n)] + [tp(h, p0 + ps * j) for h in hp for j in range(n)])
            wt = both([(tp if mem else ts)(h, o0 + os_ * j) for h in ho for j in range(n)])
            V(16 * n * len(hs), lambda v, T: v.tensor_tensor((T.sp if mem else T.sv)[:, at(ho), sl(o0, os_, n), :], T.sv[:, at(hs), sl(s0, ss, n), :],
                                                             T.sp[:, at(hp), sl(p0, ps, n), :], ALU.max if op else ALU.min), rt, wt)
        for x in NET:
            step(*x)
        step(0, 43, 1, 7, 2, 4, 1, 22, -4, [0], [1], [0]); step(0, 47, 1, 15, 2, 4, 0, 15, -2, [0], [1], [0])
        step(0, 43, 1, 7, 2, 4, 0, 8, 2, [1], [0], [0]); step(0, 47, 1, 15, 2, 4, 1, 8, 4, [1], [0], [0])
        SB, PB, PS = (8, 16, 24, 8), (8, 0, 8, 16), (2, 1, 1)
        for m in range(3):
            for side in range(2):
                for op in range(2):
                    step(1 - op, SB[m] + 4 * side, 1, PB[m] + 4 * side * PS[m], PS[m], 4, side, (PB if side else SB)[m + 1] + op, 2, [0], [0], [0])
        for op in range(2):
            V(128, lambda v, T, op=op: v.tensor_tensor(T.kk[:, p, op:16:2, :], T.sv[:, h0, 8:16, :], T.sp[:, h0, 16:24, :], ALU.min if op else ALU.max),
              both([ts(0, 8 + j) for j in range(8)] + [tp(0, 16 + j) for j in range(8)]), [("kk", p, op)])
        rw = both([tp(1, 8 + j) for j in range(8)]); kt = [("kk", p, 0), ("kk", p, 1)]
        V(128, lambda v, T: v.tensor_scalar(T.sp[:, h1, 8:16, :], T.kk[:, p, :, 0:8], MAGIC, -MAGIC, ALU.add, ALU.add), kt, rw)
        for du in range(2):
            V(128, lambda v, T, du=du: v.tensor_tensor(T.hl[:, tp_ + 2, 0, du, :], T.kk[:, p, :, du * 8:(du + 1) * 8], T.sp[:, h1, 8:16, :], ALU.subtract),
              kt + rw, [("hl", t + 1, p, 0, du)])

    def nk(t, ps, k0, n=1): return [("ne", t % 3, p, k) for p in ps for k in range(k0, k0 + n)]
    REG = {"bb": (lambda T, n: T.bb[:, 0:n], ["bb"]), "xb": (lambda T, n: T.xb[:, 0:n], ["xb"]),
           "key0": (lambda T, n: T.key0[:, 0, 0:n], [("key0", 0)]), "key1": (lambda T, n: T.key1[:, 0, 0:n], [("key1", 0)])}
    def lanes(t):
        return {1: [(["bb", "xb"], [0, 1])], 2: [(["bb"], [0]), (["xb"], [1])], 3: [(["bb", "key0"], [0]), (["xb", "key1"], [1])]}[cfg["parts"][t]]
    IDF = [("idf", s) for s in range(2)]
    last = []

    def errors(t, p):
        w0 = (t + 1) * 256; ne = "ne%d" % (t % 3)
        NW = [x for q in range(t + 1, t + 17) for x in NT(q)] + [("ul", t + 1, p, 0)]
        for who, k0, n in pieces(cfg["egat"][2 * t + p]):
            o0 = ucol(t + 1, p, 0) + k0 * 8
            def win(T, o0=o0, n=n): return T.nt[:, w0:w0 + 4096].indirect(T.ul[:, o0:o0 + n * 8])
            if who == "S":
                S(n * 128, lambda a, T, k0=k0, n=n, win=win: a.activation(T[ne][:, p, hb(k0, n)], win(T), ACT.Copy), NW, nk(t, [p], k0, n), gat=True)
            else:
                V(n * 128, lambda v, T, k0=k0, n=n, win=win: v.tensor_copy(T[ne][:, p, hb(k0, n)], win(T)), NW, nk(t, [p], k0, n), gat=True)

    def bias(t, banks, ps):
        ne = "ne%d" % (t % 3); a, wd = ps[0] * 128, len(ps) * 128; P_ = slice(ps[0], ps[-1] + 1)
        mode, off = [], [0]
        for k, c in enumerate(cfg["pre"][t]):
            if off[k] and c == "P": c = "Q"
            elif k == 15 and not off[k]: c = "P"
            mode.append(c); off.append(0 if c == "P" else 1 - off[k])
        def cs(T): return T.cs[:, a:a + wd]
        def tt(T): return T.tt[:, a:a + wd]
        def done(T): return T.bs[:, t % 2, P_, 0:128]
        tk = [("tt", p) for p in ps]; bk = [("bs", t % 2, 0, p) for p in ps]
        bank = banks[0]; old = None
        for k in range(16):
            if mode[k] != "O": bank = banks[k % len(banks)]
            bt = REG[bank][1]; o = off[k]; et = nk(t, ps, k)
            def e(T, k=k): return T[ne][:, P_, hb(k)]
            def x(T, bank=bank): return REG[bank][0](T, wd)
            new = (done, bk, []) if k == 15 else (x, bt, [bank]) if mode[k + 1] == "O" else (cs, [("cs", p) for p in ps], [])
            def relus(src, half, last):
                S(wd, lambda s, T, o=o: s.activation(tt(T), src[0](T), ACT.Relu, bias=T.mm[:, 2 * o:2 * o + 1], scale=(1.0 - 2 * o) * half), src[1] + MM, tk, src[2])
                S(wd, lambda s, T: s.activation(last[0](T), tt(T), ACT.Relu, bias=T.mm[:, 3:4], scale=-1.0), tk + MM, last[1], last[2])
            if k == 0 and mode[0] == "P":
                V(wd, lambda v, T, e=e: v.tensor_scalar(tt(T), e(T), T.mm[:, 3:4], T.mm[:, 4:5], ALU.min, ALU.max), et + MM, tk)
                V(wd, lambda v, T, new=new: v.tensor_scalar(new[0](T), tt(T), -0.5, None, ALU.mult), tk, new[1], new[2])
            elif k == 0:
                relus((e, et, []), 0.5, new)
            else:
                if mode[k] == "O":
                    V(wd, lambda v, T, e=e, x=x: v.tensor_tensor(tt(T), e(T), x(T), ALU.add), et + bt, tk, [bank])
                    relus((tt, tk, []), 0.5, (tt, tk, []))
                    step = (tt, tk)
                else:
                    grp = ("b", t, k, a); step = (x, bt)
                    PE([(4 * wd, lambda T, e=e, x=x: (x(T), T.idf[:, 0, :], e(T)))], et + IDF, bt, [bank], True, grp=grp)
                    PE([(4 * wd, lambda T, x=x: (x(T), T.idf[:, 0, :], cs(T)))], old[1] + IDF, bt, [bank], False, grp=grp)
                    if mode[k] == "P":
                        V(wd, lambda v, T, x=x: v.tensor_scalar(x(T), x(T), T.mm[:, 0:1], T.mm[:, 1:2], ALU.min, ALU.max), bt + MM, bt, [bank])
                    else:
                        relus((x, bt, [bank]), 1.0, (x, bt, [bank]))
                V(wd, lambda v, T, old=old, new=new, step=step, op=ALU.add if off[k + 1] else ALU.subtract: v.tensor_tensor(new[0](T), old[0](T), step[0](T), op),
                  old[1] + step[1], new[1], [bank])
            old = new
        if t < 3:
            e0 = (16 + t) * 256 + a; r0 = t * 256 + a
            PE([(wd, lambda T: (x(T), T.idb[:, 3, :], T.ers[:, r0:r0 + wd])), (4 * wd, lambda T: (x(T), T.idf[:, 1, :], done(T)))],
               bk + IDF + ["ers", ("idb", 3)], bt, [bank])
            S(wd, lambda s, T: s.activation(T.nt[:, e0:e0 + wd], x(T), ACT.Copy), bt, [NT(16 + t)[p] for p in ps], [bank])

    def spread(t):
        ne = "ne%d" % (t % 3); D = t % 2; B = [0, 1]
        BS = [("bs", t % 2, 0, p) for p in B]
        tag[1] = 1
        Y(1 << 17, lambda e, T: e.dma_start(T.yb[:, blk(t)], T.bs[:, D, :, 0:128]), BS, [("yb", t)], 2)
        def fold(ps, k0, n, first):
            def xs(T): return T[ne][:, ps[0]:ps[-1] + 1, hb(k0, n)]
            x = nk(t, ps, k0, n); m = n * 128 * len(ps)
            S(m, lambda s, T: s.activation(xs(T), xs(T), ACT.Abs), x, x)
            S(m + (1600 if first else 0), lambda s, T: s.activation(xs(T), xs(T), ACT.Exp, scale=-1.0), x, x)
        if cfg["sub"][t] == "D":
            nr = cfg["rep"]
            for i in (1, 2, 4)[:nr // 3 + 1]:
                BS = BS + [("bs", D, i)]
                Y(i << 17, lambda e, T, i=i: e.dma_start(T.bs[:, D, :, hb(i, i)], T.bs[:, D, :, hb(0, i)]), BS[:-1], BS[-1:], 2)
            for c in range(0, 16, nr):
                GD(nr << 18, lambda g, T, c=c: g.dma_start(T[ne][:, :, hb(c, nr)], T.bs[:, D, :, hb(0, nr)], accum_op=ALU.add), BS + nk(t, B, c, nr), nk(t, B, c, nr), 2)
            for _, k0, n in pieces(cfg["exp"][t]):
                fold(B, k0, n, t + k0 == 0)
        else:
            for p in B:
                tag[1] = p
                bank = ("bb", "xb")[p]
                for i in range(4):
                    PE([(512, lambda T, i=i, p=p, bank=bank: (T[bank][:, hb(i)], T.idf[:, 1, :], T.bs[:, D, p, 0:128]))], [BS[p]] + IDF, [bank], [bank])
                for c in range(0, 16, 4):
                    V(512, lambda v, T, c=c, p=p, bank=bank: v.tensor_tensor(T[ne][:, p, hb(c, 4)], T[ne][:, p, hb(c, 4)], T[bank][:], ALU.add),
                      nk(t, [p], c, 4) + [bank], nk(t, [p], c, 4), [bank])
                for _, k0, n in pieces(cfg["exp"][t]):
                    fold([p], k0, n, t + k0 + p == 0)
        if cfg["sum"][t] == "P":
            for p in B:
                tag[1] = p
                key = "key%d" % p
                for _, k0, n in pieces(cfg["exp"][t]):
                    PE([(512, lambda T, k=k, p=p, key=key: (T[key][:, 2, :], T.idf[:, 1, :], T[ne][:, p, hb(k)])) for k in range(k0, k0 + n)],
                       nk(t, [p], k0, n) + IDF, [(key, 0)], [key], k0 == 0, k0 + n == 16)
                V(128, lambda v, T, p=p, key=key: v.tensor_copy(T.so[:, hb(p)], T[key][:, 2, :]), [(key, 0)], [("so", p)], [key])
                Y(1 << 16, lambda e, T, p=p: e.dma_start(T.ys[:, hb(2 * t + p)], T.so[:, hb(p)]), [("so", p)], [("ys", t, p)])
        elif cfg["sum"][t] == "A":
            def later():
                tag[:] = ["e%d" % t, 1]; A = [("aa", 0, 0), ("aa", 0, 1)]
                for _, k0, n in pieces(cfg["exp"][t]):
                    PE([(1024, lambda T, k=k: (T.aa[:, 0:256], T.idf[:, 1, :], T[ne][:, :, hb(k)])) for k in range(k0, k0 + n)],
                       nk(t, B, k0, n) + IDF + [("ul", 4, 1, 0)], A, ["aa"], k0 == 0, k0 + n == 16)
                S(256, lambda s, T: s.activation(T.s2[:], T.aa[:, 0:256], ACT.Copy), A, ["s2"], ["aa"])
                Y(1 << 17, lambda e, T: e.dma_start(T.ys[:, blk(t)], T.s2[:]), ["s2"], [("ys", t)])
            last.append(later)
        elif cfg["sum"][t] == "F":
            add("G", "f", (1 << 21, 32), lambda g, T: (T.so[:], 1, [(T.so[:, hb(p)], [T[ne][:, p, hb(k)] for k in range(16)]) for p in B]),
                nk(t, B, 0, 16), [("so", 0), ("so", 1)])
            ops[-1]["slot"] = 16
            Y(1 << 17, lambda e, T: e.dma_start(T.ys[:, blk(t)], T.so[:]), [("so", 0), ("so", 1)], [("ys", t)])
        else:
            for m in (8, 4, 2, 1):
                GD(m << 18, lambda g, T, m=m: g.dma_start(T[ne][:, :, hb(0, m)], T[ne][:, :, hb(m, m)], accum_op=ALU.add), nk(t, B, 0, 2 * m), nk(t, B, 0, m), 2)
            Y(1 << 17, lambda e, T: e.dma_start(T.ys[:, blk(t)], T[ne][:, :, hb(0)]), nk(t, B, 0), [("ys", t)], 2)

    for p in range(2):
        tag[:] = ["init", p]
        own_lists(0, p)
    for t in range(4):
        for p in range(2):
            tag[:] = ["s%d" % t, p]
            select(t, p)
            own_lists(t + 1, p)
        for p in range(2):
            tag[:] = ["g%d" % t, p]
            errors(t, p)
        for banks, ps in lanes(t):
            tag[:] = ["b%d" % t, ps[-1]]
            bias(t, banks, ps)
        tag[0] = "e%d" % t
        spread(t)
    for fn in last:
        fn()
    return ops


def link(ops):
    lastw, readers = {}, {}
    for i, o in enumerate(ops):
        d = set()
        for x in o["r"]:
            if x in lastw: d.add(lastw[x])
        o["raw"] = set(d)
        for x in o["w"]:
            if x in lastw: d.add(lastw[x])
            d.update(readers.get(x, ()))
        d.discard(i)
        for x in o["r"]: readers.setdefault(x, []).append(i)
        for x in o["w"]:
            lastw[x] = i; readers[x] = []
        o["dep"] = d
        o["free"] = {j for j in d if o["grp"] and o["grp"] == ops[j]["grp"]}


def moved(o, C):
    return o["n"][0] / C["bw"] + 8 * o["n"][1] * C["row"]


def times(o, C):
    k, q, n = o["kind"], o["q"], o["n"]
    if k == "f": return C["gi"], C["fold"] + moved(o, C)
    if k == "r": return C["gi"], C["rem"]
    if k == "d":
        h = C["gi"] if q == "G" else C["yi"]
        return h, h + C["dma"] + moved(o, C)
    if q == "P":
        t = sum(max(64, x) * C["pe"] + C["pefix"] for x in n)
    elif q == "G":
        t = n * C["cy"]
    else:
        t = (n * C["G"] if o["gat"] else max(n, 64)) * C["cy"] + C["fix" + q]
    return t, t


def lat(a, b, C):
    return C["same"] if (a["q"] == b["q"] and a["kind"] == "c") else C["cross"]


def plan(ops, C, cfg):
    C = dict(C, **cfg["wary"])
    n = len(ops); succ = [[] for _ in ops]
    for i, o in enumerate(ops):
        for d in o["dep"]: succ[d].append(i)
    tm = [times(o, C) for o in ops]
    pr = [0.0] * n
    for i in range(n - 1, -1, -1):
        o = ops[i]; w = o["w"][0][0] if o["w"] else ""; due = []
        if o["tag"][0] in "sbe" and (w in ("hl", "nt", "ys", "yb") or not succ[i]):
            due = [-cfg["half"] * (2 * int(o["tag"][1]) + o["part"]) - cfg["due"][o["tag"]]]
        pr[i] = (tm[i][0] * cfg["stretch"].get(o["tag"][0] + o["q"], 1.0) + tm[i][1] - tm[i][0]
                 + max([pr[j] + lat(o, ops[j], C) for j in succ[i]] + due, default=-1e9))
    B = cfg["bonus"]
    pr = [pr[i] + B.get(o["tag"], 0.0) + B.get(o["tag"][0] + o["q"], 0.0) - cfg["off"] * o["part"] for i, o in enumerate(ops)]
    left = [len(o["dep"]) for o in ops]; ready = {q: [] for q in "VSPGY"}
    for i in range(n):
        if not left[i]: ready[ops[i]["q"]].append(i)
    free = dict.fromkeys(ready, 0.0); fin = [0.0] * n; rt = [0.0] * n; bank = {}; order = []; wire = 0.0; pick = dict.fromkeys(ready)
    stale = set(ready); cross = C["cross"]
    while len(order) < n:
        for q0 in stale:
            best = None; fence = 1e18; tol = cfg["tol"][q0]; f0 = free[q0]
            for i in sorted(ready[q0], key=lambda x: -pr[x]):
                s = rt[i] if rt[i] > f0 else f0
                for b in ops[i]["banks"]:
                    for q, j in bank.get(b, {}).items():
                        if q != q0 and fin[j] + cross > s: s = fin[j] + cross
                if (best is None or s < best[0]) and s + tm[i][0] - tol <= fence: best = (s, i)
                if s < fence: fence = s
            pick[q0] = best
        s, i = min(x for x in pick.values() if x)
        o = ops[i]; q0 = o["q"]; o["all"] = set(o["dep"]); o["start"] = s; stale = {q0}
        for b in o["banks"]:
            o["all"].update(j for q, j in bank.get(b, {}).items() if q != q0)
            bank.setdefault(b, {})[q0] = i; stale.update("VSP")
        free[q0] = s + tm[i][0]; fin[i] = s + tm[i][1]
        if o["kind"] in "df":
            wire = fin[i] = max(fin[i], wire + moved(o, C))
        order.append(i); ready[q0].remove(i)
        for j in succ[i]:
            rt[j] = max(rt[j], fin[i] + (0.0 if i in ops[j]["free"] else lat(o, ops[j], C))); left[j] -= 1
            if not left[j]: ready[ops[j]["q"]].append(j); stale.add(ops[j]["q"])
    last = {ops[i]["grp"]: i for i in order if ops[i]["grp"]}
    for i, o in enumerate(ops):
        o["last"][0] = last.get(o["grp"]) == i
    return order, max(fin)


COST = {"cy": 0.83, "G": 1.56, "fixV": 50.0, "fixS": 65.0, "pe": 0.42, "pefix": 5.0, "same": 140.0, "cross": 140.0,
        "dma": 2000.0, "bw": 550.0, "row": 25.0, "gi": 1000.0, "yi": 100.0, "rem": 3800.0, "fold": 7500.0}
CFG = {
    "path": ["R2D2R2D2", "D2D2D2D2"] + ["D2D2D2D2"] * 6,
    "egat": ["S8S8"] * 6 + ["S4S4S8", "S2V2S4V4S4"],
    "pre": ["PPQQPPQQPPQQPPQP"] * 3 + ["P" * 16],
    "parts": [1, 1, 1, 3], "sub": "DDDV", "sum": "DDDP", "exp": ["S8S8", "S8S8", "S8S8", "S4S4S4S4"],
    "rounds": 0, "stretch": {}, "rep": 8, "ptv": 10, "slack": 0.0, "off": 10000.0, "bonus": {"late": -20000.0, "bV": 50000.0, "bS": 50000.0},
}
CFG = {'path': ['R2D2R1R1A2', 'D2D1D1D2D2', 'D2D2D2D2', 'D2A2A2A2', 'D2D2D2D1D1', 'V2D2D2D2', 'D2D2D2D2', 'D2D2D2D2'], 'egat': ['S8S4S4', 'S2S3S1S5S5', 'S8S5S3', 'V2S4S5S5', 'S8S3S4S1', 'S2S4S5S5', 'S8S8', 'S2S4S4S6'], 'pre': ['PQPPQQPPPPPPPPPP', 'PPPPPPPPPPPPPPPP', 'PPPPPPPPPPPQQQPP', 'PPPPPPPPPPPPPQQQ'], 'parts': [1, 1, 1, 3], 'sub': 'DDDV', 'sum': 'FFFP', 'exp': ['S2S2S4S2S1S1S1S1S2', 'S2S2S2S2S4S2S2', 'S2S1S1S2S2S2S2S2S2', 'S4S4S4S4'], 'rounds': 0, 'mix': 1, 'stretch': {'sV': 1.42, 'eY': 1.12, 'sG': 0.88, 'vV': 1.09, 'bV': 1.31, 'gV': 0.71, 'sP': 0.81, 'iS': 0.88, 'lS': 1.0, 'sS': 1.25, 'iV': 1.14, 'pG': 0.99, 'vP': 0.92, 'eG': 1.12, 'eV': 0.64, 'eS': 0.88, 'pV': 1.1, 'bP': 1.04, 'pS': 1.05, 'lY': 0.9, 'pP': 0.8, 'gS': 1.19, 'eP': 1.25, 'bS': 1.05}, 'rep': 4, 'ptv': 6, 'slack': 0, 'off': 1000, 'bonus': {'bV': 110000.0, 'bP': 100000.0, 'bS': 97000.0, 'sG': 100000.0, 'pG': 49000.0, 'late': -11300, 'sP': 98300.0, 'uV': 200000.0, 'uP': 200000.0, 'pS': 50000.0, 'sS': 41000.0, 'gS': 3000, 'g0': 11300, 'v2': -4300, 'lY': 10700, 'g1': 20000, 's2': -3000, 'b2': -10000, 'pP': -1000, 's0': -300, 'vP': 10000, 'b0': 7000, 'eV': 10000, 'p3': 300, 'sV': -1000, 'eS': -3000, 'e1': 12000, 'p0': -19400, 'b1': -9700, 'e3': 3700, 's3': 10000, 'g3': 10000, 'eG': -10000, 'lS': -6000, 'p1': 4000, 'gV': -10000, 'iV': 600, 'b3': 1000, 'e0': -300, 'eY': -4000, 'g2': -1000, 'v3': -300, 'iS': -1300, 'vV': -20000, 'e2': 3000}, 'half': 13600, 'due': {'s0': -5500, 's1': -4500, 's2': -1500, 's3': -11500, 'b0': 9500, 'b1': 10000, 'b2': 10000, 'b3': 14500, 'e0': 71000, 'e1': 48500, 'e2': 65000, 'e3': 54500}}
CFG = {'path': ['R2A2V1V1D2', 'A2D2D2D2', 'D2A2D2D2', 'D2D2D2D2', 'D2D2D2D2', 'D2D2D2D2', 'D2D2D2D2', 'D2D2D2D2'], 'egat': ['S8S8', 'S2S4S5S5', 'S2S3S3S2S6', 'S2S4S5S3V2', 'S4S4S8', 'S2S2V2S5S5', 'S2S1S1S1S3S8', 'S2S3S1S5S2S3'], 'pre': ['PQPPPQQPPPPPPPPP', 'PPPPPPPPPPPPPPPP', 'PPPPPPPPPPPPPPPP', 'PPPPPPPPPPPPPPPP'], 'parts': [1, 1, 2, 3], 'sub': 'DDDV', 'sum': 'DDDP', 'exp': ['S2S2S2S2S2S2S1S1S2', 'S2S2S2S2S2S2S2S2', 'S2S1S1S2S2S2S2S2S2', 'S4S4S4S4'], 'stretch': {'sV': 1.66, 'eP': 1.25, 'sS': 0.8, 'gS': 1.28, 'eV': 1.36, 'lS': 0.85, 'lY': 1.43, 'sP': 1.14, 'iS': 0.84, 'bS': 1.31, 'bP': 1.09, 'eY': 0.69, 'pV': 0.9, 'vV': 0.9, 'eS': 1.35, 'iV': 1.3, 'eG': 0.94, 'pP': 0.72, 'vP': 1.12, 'pG': 1.28, 'pS': 1.19, 'bV': 0.85, 'gV': 1.21}, 'rep': 4, 'ptv': 13, 'off': -1000, 'run': 8, 'tol': {'V': 300, 'S': 600, 'P': 1200, 'G': 500, 'Y': 1000}, 'bonus': {'bV': 110000.0, 'bP': 91700.0, 'bS': 109700.0, 'sG': 117000.0, 'pG': 50700.0, 'late': -32400, 'sP': 102000.0, 'uV': 200000.0, 'uP': 200000.0, 'pS': 40000.0, 'sS': 37000.0, 'gS': -13000, 'iV': -3700, 'e3': 3000, 'pV': 3300, 'g2': -7000, 'b2': -6000, 'e2': -2000, 's1': -300, 'b3': 10300, 'lY': 19700, 'p3': -2000, 'p0': -1000, 'v0': -8700, 'vV': 1000, 'eY': -2000, 'eV': -10300, 's3': 5000, 'g0': -18700, 'v1': 2700, 'g1': -3000, 'e0': -5700, 'iS': -9300, 'eP': 3000, 'init': -3000, 'eG': -1000, 'v2': -3000, 'eS': -1000, 'lS': -9300, 'b1': 11300, 'g3': -11700, 's0': 700, 'vP': 3000, 'gV': -6000, 'e1': 1000, 'v3': -1000}, 'half': 14500, 'due': {'s0': -13500, 's1': -500, 's2': 4000, 's3': 4000, 'b0': 16000, 'b1': 31000, 'b2': 19500, 'b3': 500, 'e0': 65500, 'e1': 66500, 'e2': 45500, 'e3': 30000}}
CFG = {'path': ['R2A2V1V1D2', 'A2D2D2D2', 'D2A1A1D2D2', 'D2D2D2D2', 'D2D2D2D2', 'D2D2A2D2', 'D2D2D2D2', 'D2D2D2D2'], 'egat': ['S8S8', 'S2S4S5S5', 'S2S3S3S2S6', 'S2S4S5S2S1V2', 'S4S4S8', 'V2S2V2S5S4S1', 'S2S1S1V1S3S8', 'V2S3S1S5S1S4'], 'pre': ['PQQPPQPPPPPPPPPP', 'PPPPPPPPPPPPPPPP', 'PPPPPPPPPPPPPPPP', 'PPPPPPPPPPPPPPPP'], 'parts': [1, 1, 2, 3], 'sub': 'DDDV', 'sum': 'DDDP', 'exp': ['S2S2S2S2S2S2S1S1S2', 'S2S2S2S2S4S2S2', 'S2S1S1S2S2S2S2S2S2', 'S4S4S1S3S4'], 'stretch': {'sV': 1.66, 'eP': 1.8, 'sS': 0.64, 'gS': 1.02, 'eV': 1.34, 'lS': 1.03, 'lY': 1.02, 'sP': 0.9, 'iS': 0.6, 'bS': 1.31, 'bP': 1.09, 'eY': 0.59, 'pV': 1.05, 'vV': 0.71, 'eS': 1.28, 'iV': 1.5, 'eG': 0.85, 'pP': 0.65, 'vP': 1.04, 'pG': 0.84, 'pS': 1.22, 'bV': 0.85, 'gV': 1.65, 'sG': 1.04}, 'rep': 4, 'ptv': 13, 'off': -1500, 'run': 8, 'tol': {'V': 300, 'S': 800, 'P': 300, 'G': 100, 'Y': 1000}, 'bonus': {'bV': 97000.0, 'bP': 101400.0, 'bS': 112700.0, 'sG': 118000.0, 'pG': 50400.0, 'late': -33100, 'sP': 112300.0, 'uV': 200000.0, 'uP': 200000.0, 'pS': 43000.0, 'sS': 36000.0, 'gS': -13000, 'iV': 6300, 'e3': 12000, 'pV': 3300, 'g2': 11300, 'b2': -16000, 'e2': 0, 's1': 400, 'b3': 2300, 'lY': 20000, 'p3': -2300, 'p0': -1700, 'v0': 1300, 'vV': 400, 'eY': -11000, 'eV': 2400, 's3': 8000, 'g0': 1600, 'v1': 2700, 'g1': -3000, 'e0': -4000, 'iS': -300, 'eP': 5600, 'init': -9300, 'eG': -9000, 'v2': -4000, 'eS': -11300, 'lS': -10600, 'b1': 14300, 'g3': -12000, 's0': -1900, 'vP': 3000, 'gV': 8000, 'e1': -2300, 'v3': -700, 'b0': -4000, 'pP': -1000, 's2': -300}, 'half': 13500, 'due': {'s0': -20500, 's1': 0, 's2': 3500, 's3': 13000, 'b0': 34500, 'b1': 36500, 'b2': 21500, 'b3': -6000, 'e0': 63000, 'e1': 77000, 'e2': 44000, 'e3': 27500}}
CFG["wary"] = {"rem": 6500.0, "dma": 2400.0}
CFG = {'path': ['D2A2V2D2', 'D2A2D2D1D1', 'D2D1A1D2D2', 'D2D2D2D2', 'D2D2D2D2', 'D1D1D2A2D2', 'A2D2D2D2', 'D2D2D2D2'], 'egat': ['S3S5S8', 'S6S5S5', 'S2S3S3S2S1S5', 'S2S4S5S2S1V2', 'S8S8', 'V2S2V2S1S4S4S1', 'S2S1S1V1S3S8', 'V2S3S1S5S1S4'], 'pre': ['PQQPPQPPPPPPPPPP', 'PPPPPPPPPPPPPPPP', 'PPPPPPPPPPPPPPPP', 'PPPPPPPPPPPPPPPP'], 'parts': [1, 2, 2, 3], 'sub': 'DDDV', 'sum': 'DDDP', 'exp': ['S2S2S2S2S2S2S1S1S2', 'S2S2S2S1S1S4S2S1S1', 'S2S2S2S2S2S2S2S2', 'S4S4S1S3S2S2'], 'stretch': {'sV': 1.66, 'eP': 1.44, 'sS': 0.8, 'gS': 0.86, 'eV': 1.34, 'lS': 1.84, 'lY': 1.03, 'sP': 0.86, 'iS': 0.63, 'bS': 0.77, 'bP': 0.98, 'eY': 0.59, 'pV': 1.08, 'vV': 0.69, 'eS': 1.03, 'iV': 1.07, 'eG': 0.75, 'pP': 0.42, 'vP': 0.78, 'pG': 0.91, 'pS': 1.18, 'bV': 0.85, 'gV': 1.32, 'sG': 0.71}, 'rep': 2, 'ptv': 13, 'off': -2000, 'run': 8, 'tol': {'V': 300, 'S': 2000, 'P': 300, 'G': 100, 'Y': 1000}, 'bonus': {'bV': 97700.0, 'bP': 92400.0, 'bS': 112700.0, 'sG': 108000.0, 'pG': 46100.0, 'late': -26400, 'sP': 114300.0, 'uV': 200000.0, 'uP': 200000.0, 'pS': 41600.0, 'sS': 36000.0, 'gS': -6300, 'iV': -3400, 'e3': 2000, 'pV': 3600, 'g2': 19000, 'b2': -16000, 'e2': -10000, 's1': 100, 'b3': 3300, 'lY': 13000, 'p3': 6700, 'p0': -2000, 'v0': -28700, 'vV': 700, 'eY': -5300, 'eV': 15400, 's3': 9000, 'g0': -400, 'v1': 1400, 'g1': -3000, 'e0': -4600, 'iS': -42200, 'eP': -6400, 'init': -9300, 'eG': -5000, 'v2': -7000, 'eS': -2000, 'lS': -7600, 'b1': 4300, 'g3': -16300, 's0': -2900, 'vP': -1000, 'gV': 11700, 'e1': -10000, 'v3': -19100, 'b0': -11000, 'pP': 700, 's2': 3000, 'sV': -300, 'p2': -300}, 'half': 13800, 'due': {'s0': -6000, 's1': -500, 's2': 4000, 's3': 6500, 'b0': 24500, 'b1': 28000, 'b2': 22000, 'b3': 2000, 'e0': 55000, 'e1': 85500, 'e2': 50000, 'e3': 28500}, 'wary': {'rem': 5000, 'G': 1.9}}
CFG.update({'path': ['D2A2V2D2', 'A2D2D2A2'] + ['D4D2D2'] * 6, 'egat': ['S8S8', 'S2S4S5S5'] * 4, 'rep': 4, 'parts': [1, 1, 2, 3]})
CFG = {'path': ['V2D2A2V2', 'A2V1V1V1D1A2', 'V2A2A2A1A1', 'D1D3D2D2', 'D4A1A1D2', 'D4D2D2', 'D4D4', 'D4A2D2'], 'egat': ['S3S5S8', 'S1S1S4S5S5', 'S8S7S1', 'S2S4S5S5', 'S8S1V2S5', 'V2S4S5S5', 'S8S8', 'S2S4S5S5'], 'pre': ['PQPPPQPQPPPPPPPP', 'PPPPPPPPQPPPPPPP', 'PPPPPPPPPPPPQQPP', 'PPPPPPPPPPPPPPPP'], 'parts': [1, 1, 2, 3], 'sub': 'DDVV', 'sum': 'DDDP', 'exp': ['S2S2S2S1S1S2S2S1S1S2', 'S1S3S2S1S1S4S2S1S1', 'S6S2S2S2S2S2', 'S4S4S1S3S2S1S1'], 'stretch': {'sV': 1.42, 'eP': 1.3, 'sS': 0.53, 'gS': 0.9, 'eV': 0.62, 'lS': 1.96, 'lY': 0.63, 'sP': 0.58, 'iS': 0.49, 'bS': 1.01, 'bP': 0.88, 'eY': 0.52, 'pV': 1.25, 'vV': 0.56, 'eS': 1.43, 'iV': 1.1, 'eG': 1.0, 'pP': 0.4, 'vP': 0.89, 'pG': 0.85, 'pS': 1.38, 'bV': 0.77, 'gV': 1.1, 'sG': 0.79}, 'rep': 4, 'ptv': 10, 'off': -1500, 'run': 8, 'tol': {'V': 300, 'S': 200, 'P': 200, 'G': 500, 'Y': 1000}, 'bonus': {'bV': 97400.0, 'bP': 100400.0, 'bS': 133700.0, 'sG': 118300.0, 'pG': 42400.0, 'late': -50700, 'sP': 114000.0, 'uV': 200000.0, 'uP': 200000.0, 'pS': 44900.0, 'sS': 35000.0, 'gS': -26900, 'iV': -400, 'e3': 13000, 'pV': 3600, 'g2': 20700, 'b2': -23400, 'e2': 1000, 's1': -600, 'b3': -4400, 'lY': 6000, 'p3': 1000, 'p0': -2300, 'v0': -20700, 'vV': 10700, 'eY': -5600, 'eV': 11400, 's3': -15300, 'g0': -400, 'v1': 4100, 'g1': -3000, 'e0': -13600, 'iS': -31500, 'eP': -6400, 'init': -8000, 'eG': 700, 'v2': -7700, 'eS': -2000, 'lS': -5600, 'b1': -6100, 'g3': -18400, 's0': 100, 'vP': -1000, 'gV': 21700, 'e1': -27000, 'v3': -19100, 'b0': -10000, 'pP': 100, 's2': 3000, 'sV': -3600, 'p2': -300, 'p1': 29700}, 'half': 14700, 'due': {'s0': 0, 's1': -2000, 's2': 4500, 's3': 20000, 'b0': 36000, 'b1': 23500, 'b2': 37000, 'b3': -500, 'e0': 53500, 'e1': 98500, 'e2': 51500, 'e3': 28000}, 'wary': {'rem': 5500, 'G': 1.56, 'gi': 1400, 'dma': 2000}}
CFG = {'path': ['V2D2A2V2', 'A2V1V1V1A1A2', 'V1V1A2D2A1A1', 'D1D3D2D1D1', 'D4A1A1D2', 'D4A2D2', 'D4D4', 'D4A2D2'], 'egat': ['S3V5S8', 'S1S1S4S5S5', 'S8V5V2S1', 'S2S4S5S5', 'S8S1V2S5', 'V2S4S3S2S5', 'S5S3S8', 'S2S4S1S2S2S3S2'], 'pre': ['PQPPPQQQPPPPPPPP', 'PPPPPPPPQPPPPPPP', 'PPPPPPQPPPPPQPPP', 'PPPPPPPPPPPPPPPP'], 'parts': [1, 1, 2, 3], 'sub': 'DDVV', 'sum': 'DDDP', 'exp': ['S2S2S2S1S1S2S1S1S1S1S2', 'S4S2S1S1S4S3S1', 'S6S2S2S2S2S2', 'S4S4S4S2S1S1'], 'stretch': {'sV': 1.49, 'eP': 1.63, 'sS': 0.53, 'gS': 1.11, 'eV': 0.5, 'lS': 1.41, 'lY': 0.86, 'sP': 0.3, 'iS': 0.54, 'bS': 0.84, 'bP': 0.91, 'eY': 0.33, 'pV': 0.91, 'vV': 0.9, 'eS': 1.5, 'iV': 0.79, 'eG': 1.56, 'pP': 0.4, 'vP': 0.86, 'pG': 1.06, 'pS': 1.53, 'bV': 0.96, 'gV': 1.32, 'sG': 0.7}, 'rep': 4, 'ptv': 10, 'off': 500, 'run': 8, 'tol': {'V': 300, 'S': 200, 'P': 1200, 'G': 500, 'Y': 1000}, 'bonus': {'bV': 108700.0, 'bP': 93700.0, 'bS': 137000.0, 'sG': 121300.0, 'pG': 42400.0, 'late': -51400, 'sP': 123100.0, 'uV': 200000.0, 'uP': 200000.0, 'pS': 41600.0, 'sS': 37000.0, 'gS': -26600, 'iV': -8100, 'e3': 2700, 'pV': 3600, 'g2': 23700, 'b2': -33400, 'e2': 11000, 's1': 3700, 'b3': -1400, 'lY': 16000, 'p3': -2300, 'p0': -2300, 'v0': -36600, 'vV': 10700, 'eY': -3200, 'eV': 21100, 's3': -15300, 'g0': -10100, 'v1': 5100, 'g1': -14000, 'e0': -14600, 'iS': -21500, 'eP': 17600, 'init': -8000, 'eG': -9600, 'v2': -9400, 'eS': -4000, 'lS': -8900, 'b1': -19400, 'g3': -15400, 's0': 100, 'vP': 1300, 'gV': 12000, 'e1': -26400, 'v3': -19400, 'b0': -10000, 'pP': -6300, 's2': 3000, 'sV': -3600, 'p2': 0, 'p1': 29700}, 'half': 15300, 'due': {'s0': -7000, 's1': 9000, 's2': 5500, 's3': 43000, 'b0': 8500, 'b1': 30000, 'b2': 29500, 'b3': 10500, 'e0': 64500, 'e1': 100500, 'e2': 47500, 'e3': 28000}, 'wary': {'rem': 5500, 'G': 1.56, 'gi': 1400, 'dma': 2000}}
CFG = {'path': ['V2D2D2D2', 'D2V2D2D2', 'D2A2D2D2', 'D2D2D1D1A1A1', 'A2D2D2A2', 'V2A2D2D2', 'D2D1D1D2D2', 'D2A2D3D1'], 'egat': ['S5S3S4S4', 'S2S5S4S5', 'S4S1S1V2S3V1S4', 'S1S1S1S3S5S5', 'V4S4S1S3S4', 'S2S4V5S2S3', 'V4S4S2S2S4', 'S2V4S5S5'], 'pre': ['QQOOOOOOOOOQQOOO', 'PPOOPPPPPPOOPPOO', 'POOOOOOOOOOQPPOO', 'PPOOQPPPPOOOOOOO'], 'parts': [1, 1, 2, 3], 'sub': 'DDVV', 'sum': 'DDDP', 'exp': ['S2S2S4S4S2S2', 'S2S2S2S1S1S2S2S2S2', 'S2S2S2S2S2S2S2S2', 'S4S2S2S2S2S4'], 'stretch': {'sV': 1.01, 'sP': 1.45, 'eG': 0.72, 'iV': 1.36, 'eS': 1.14, 'gS': 0.75, 'vV': 0.83, 'sG': 0.89, 'sS': 0.93, 'lY': 0.33, 'eV': 1.07, 'pP': 0.98, 'eY': 1.39, 'gV': 0.87, 'pV': 1.72, 'pG': 0.82, 'pS': 0.59, 'vP': 1.55, 'eP': 0.8, 'iS': 0.85, 'lS': 1.11, 'bS': 0.72, 'bP': 1.05, 'bV': 1.1}, 'rep': 4, 'ptv': 7, 'off': 0, 'run': 8, 'tol': {'V': 300, 'S': 500, 'P': 800, 'G': 2000, 'Y': 1000}, 'bonus': {'bV': 105000.0, 'bP': 78700.0, 'bS': 99000.0, 'sG': 109600.0, 'pG': 70000.0, 'late': 600, 'sP': 89700.0, 'uV': 200000.0, 'uP': 200000.0, 'pS': 43000.0, 'sS': 39000.0, 'gS': -14000, 'e0': 8700, 'v2': 6000, 'iS': 20400, 'g3': 5600, 'pP': -1300, 'g2': 29300, 'pV': 1000, 'g1': -3000, 'init': 35000, 'vP': 26300, 'eY': 16600, 'lY': -3000, 'b3': 5900, 'v1': -300, 's2': -300, 'p3': 11900, 'gV': -8000, 'v3': -17000, 'b2': -16000, 'e3': 7900, 'eP': 31600, 's3': -2700, 's0': 300, 'b1': 21000, 'v0': -6300, 'e2': -6400, 'iV': 26700, 'e1': -4000, 'lS': -23000, 'vV': -17300, 'p2': 6700, 'b0': -11300, 'g0': 9700, 'eV': -4400, 'eS': -300, 'sV': -1000, 'eG': -18000, 'p1': -1000, 's1': 3300}, 'half': 14800, 'due': {'s0': -7000, 's1': 7000, 's2': 2000, 's3': 29500, 'b0': 32500, 'b1': 12500, 'b2': 27000, 'b3': 32000, 'e0': 47500, 'e1': 47000, 'e2': 61500, 'e3': 28500}, 'wary': {'rem': 4500, 'pe': 0.55, 'gi': 1000, 'dma': 2000}}
OPS = build(CFG)
if "F" not in "".join(CFG["path"]): SCRATCH.pop("sf")
if "A" not in CFG["sum"]: SCRATCH.pop("s2")
link(OPS)
ORDER, SPAN = plan(OPS, COST, CFG)
SEMAPHORES = [x + str(j) for j in sorted({o["slot"] for o in OPS if o["kind"] == "f"}) for x in ("fa", "fb")] + ["cV", "cS", "cP", "cG", "snt"] + ["arr%d" % t for t in range(8)] + ["d%d" % i for i, o in enumerate(OPS) if o["kind"] == "d"]


def rank_program(g, core, T, topo):
    rank = T.rank_of(core)
    def helper(c): return [x for x in topo.cores_of(c) if x not in T.cores and topo.die(x) == topo.die(c)][0]
    if rank is None:
        for c in T.cores:
            if helper(c) == core:
                seen = {}; sent = 0
                for i in ORDER:
                    o = OPS[i]
                    if o["kind"] == "f":
                        j = o["slot"]; seen[j] = seen.get(j, 0) + len(topo.engines(c, core)); dst = o["fn"](g, T)[0]
                        g.wait_ge(T.sem["fa%d" % j], seen[j])
                        g.remote_dma(dst, dst, T.sem["fb%d" % j], T.sem.snt, topo.addr(c)[1], topo.addr(c)[0], topo.mask(core, c))
                        sent += len(topo.engines(core, c))
                if sent: g.wait_ge(T.sem.snt, sent)
        return
    mate = helper(core)
    nxt = T.cores[(rank + 1) % len(T.cores)]
    prv = T.cores[(rank - 1) % len(T.cores)]
    rid, pid, _ = topo.addr(nxt)
    mask = topo.mask(core, nxt)
    n_out = len(topo.engines(core, nxt)); n_in = len(topo.engines(prv, core))
    Q = {"V": g.vector, "S": g.scalar, "P": g.tensor, "G": g, "Y": g.sync}
    count = {q: 0 for q in Q}; know = {q: {} for q in Q}; mark = {}; clock = {}; total = {}
    for i in ORDER:
        o = OPS[i]; q = o["q"]; kn = know[q]
        for d in sorted(o["all"], key=lambda d: -OPS[d]["start"]):
            if d in o["free"]:
                continue
            s, v = mark[d]
            if kn.get(s, 0) < v:
                Q[q].wait_ge(T.sem[s], v)
                kn[s] = v
                for a, b in clock[d].items():
                    if kn.get(a, 0) < b: kn[a] = b
        clock[i] = dict(kn)
        if o["kind"] == "f":
            _, alu, folds = o["fn"](g, T); j = o["slot"]; eng = topo.engines(core, mate); n_h = len(eng); per = n_h // len(folds)
            g.remote_dma_fused([RemoteDMATransfer(dst_ids=[DstId(rid=topo.addr(mate)[0], pnc=topo.addr(mate)[1])],
                                                  dma_engine_mask=sum(1 << e for e in eng[x * per:(x + 1) * per]),
                                                  remote_sem=T.sem["fa%d" % j], srcs=srcs, dsts=[dst], alu_op=alu)
                                for x, (dst, srcs) in enumerate(folds)], local_sem=T.sem.snt)
            mark[i] = ("fb%d" % j, total.get("fb%d" % j, 0) + len(topo.engines(mate, core))); total["snt"] = total.get("snt", 0) + n_h
        elif o["kind"] == "r":
            t = o["n"]
            g.remote_dma(T.hl[:, t, 1], T.hl[:, t, 0], T.sem["arr%d" % t], T.sem.snt, pid, rid, mask)
            mark[i] = ("arr%d" % t, n_in); total["snt"] = total.get("snt", 0) + n_out
            clock[i] = {}
        elif o["kind"] == "d":
            o["fn"](g, T)[0].then_inc(T.sem["d%d" % i], 16)
            mark[i] = ("d%d" % i, 16)
        else:
            for ins in o["fn"](g, T):
                ins.then_inc(T.sem["c" + q], 1); count[q] += 1
            mark[i] = ("c" + q, count[q])
        total[mark[i][0]] = mark[i][1]
    for s, v in total.items():
        if all(kn.get(s, 0) < v for kn in know.values()):
            g.wait_ge(T.sem[s], v)
